import numpy as np
import ml_dtypes


def mxq(x, axis, fmt="e4m3"):
    dtype, down = {"e4m3": (ml_dtypes.float8_e4m3fn, 7), "e5m2": (ml_dtypes.float8_e5m2, 14)}[fmt]
    v = np.moveaxis(np.asarray(x, np.float32).astype(ml_dtypes.bfloat16).astype(np.float64), axis, -1)
    blocks = v.reshape(v.shape[:-1] + (-1, 32))
    amax = np.abs(blocks).max(-1, keepdims=True)
    byte = np.maximum(np.where(amax > 0, np.frexp(amax)[1] - 1 + 127, 0) - down, 1)
    scale = np.exp2(byte - 127.0)
    codes = (blocks / scale).astype(np.float32).astype(dtype).astype(np.float64)
    return np.moveaxis((codes * scale).reshape(v.shape), -1, axis)


WIDE = False


def mx_kscale(k):
    if not WIDE:
        return np.ones(k)
    levels = np.array([10, -10, 5, -5, 0])
    if k % 512:
        return np.exp2(np.random.permutation(np.resize(levels, k // 32))).repeat(32)
    a = np.empty((k // 512, 16))
    for p in range(k // 512):
        a[p, :8] = np.random.permutation(np.resize(levels, 8))
        for g in range(8):
            far = levels[np.abs(levels - a[p, g]) >= 10]
            a[p, g + 8] = far[np.random.randint(len(far))]
    return np.exp2(a.ravel()).repeat(32)


def f64(x):
    return np.asarray(x).astype(np.float64)


def striped(idx):
    return np.tile(np.asarray(idx).reshape(-1, 16).T, (8, 1)).astype(np.uint16)


def unstriped(offs):
    return offs[:16].T.reshape(-1).astype(np.int64)


E2M1 = np.array([0.0, 0.5, 1.0, 1.5, 2.0, 3.0, 4.0, 6.0, -0.0, -0.5, -1.0, -1.5, -2.0, -3.0, -4.0, -6.0])


def pack_weight(w, fmt):
    k, n = w.shape
    w = f64(np.asarray(w, np.float32).astype(ml_dtypes.bfloat16)).reshape(k // 32, 32, n)
    amax = np.abs(w).max(1)
    if fmt == "e4m3":
        byte = np.frexp(amax)[1] - 1 + 127 - 7
    else:
        mant, ex = np.frexp(amax / 6.0)
        byte = np.where(mant > 0.5, ex, ex - 1) + 127
    byte = np.clip(np.where(amax > 0, byte, 1), 1, 254)
    scaled = (w * np.exp2(127.0 - byte)[:, None, :]).reshape(k, n).astype(np.float32)
    by_word = np.ascontiguousarray(scaled.reshape(k // 512, 128, 4, n).transpose(0, 1, 3, 2))
    if fmt == "e4m3":
        words = by_word.astype(ml_dtypes.float8_e4m3fn).view(np.uint8)
    else:
        c = by_word.astype(ml_dtypes.float4_e2m1fn).view(np.uint8) & 0xF
        words = (c[..., 0::2] | (c[..., 1::2] << 4)).reshape(k // 512, 128, 2 * n)
    return np.ascontiguousarray(words), np.ascontiguousarray(byte.astype(np.uint8).reshape(k // 512, 16, n))


def unpack_weight(words, scales, fmt):
    g, _, n = scales.shape
    words = np.ascontiguousarray(words).reshape(g, 128, n, -1)
    if fmt == "e4m3":
        vals = words.view(ml_dtypes.float8_e4m3fn).astype(np.float64)
    else:
        nib = np.empty((g, 128, n, 4), np.uint8)
        nib[..., 0::2] = words & 0xF
        nib[..., 1::2] = words >> 4
        vals = E2M1[nib]
    vals = vals * np.repeat(np.exp2(scales.astype(np.float64) - 127.0), 8, axis=1)[..., None]
    return vals.transpose(0, 1, 3, 2).reshape(g * 512, n)


B, N, T, D, DV, NQ = 2, 512, 2048, 512, 256, 128
PAGE = 32


def setup_inputs():
    n = np.random.standard_normal
    pages = np.random.permutation(T // PAGE)[:B * N // PAGE]
    idx = (pages[:, None] * PAGE + np.arange(PAGE)[None, :]).reshape(-1)
    s = mx_kscale(D)[:, None]
    u = np.ones(T)
    u[idx] = mx_kscale(B * N)
    r = np.random.uniform(0.5, 2.0, T)
    k = n((D, T)) / s
    v = n((DV, T)) / (u * r)
    kp = pack_weight(k, "e4m3")
    return {
        "qT": (n((B, D, NQ)) * s * (0.60 / np.sqrt(D))).astype(np.float32),
        "k_words": kp[0],
        "k_scales": kp[1],
        "vT": v.astype(np.float32),
        "vs": np.tile(u * r, (128, 1)).astype(np.float32),
        "offs": striped(idx),
    }


def reference(qT, k_words, k_scales, vT, vs, offs):
    idx = unstriped(offs)
    k = unpack_weight(k_words, k_scales, "e4m3")
    v = f64(vT)
    pick = lambda x: x[:, idx].reshape(x.shape[0], B, N).transpose(1, 0, 2)
    q = f64(qT)
    score = mxq(q, 1, "e4m3").transpose(0, 2, 1) @ pick(k)
    p = np.square(np.maximum(score, 0.0))
    total = p.sum(-1, keepdims=True) + 1.0
    w = p * pick(f64(vs))[:, :1, :]
    y = mxq(w, 2, "e4m3") @ mxq(pick(v).transpose(0, 2, 1), 1, "e4m3")
    y = y / total
    return y

@@ -1,0 +1,197 @@
+from contextlib import ExitStack
+
+import concourse.mybir as mybir
+from concourse.masks import make_identity
+
+B, N, T, D, DV, NQ = 2, 512, 2048, 512, 256, 128
+P = 128
+PACK = 4
+HALVES = DV // P
+VS_ROW = 8
+FLOPS = 2 * B * NQ * N * (D + DV)
+
+F32 = mybir.dt.float32
+BF16 = mybir.dt.bfloat16
+I32 = mybir.dt.int32
+U32 = mybir.dt.uint32
+U16 = mybir.dt.uint16
+U8 = mybir.dt.uint8
+FP8X4 = mybir.dt.float8_e4m3fn_x4
+ACT = mybir.ActivationFunctionType
+ALU = mybir.AluOpType
+
+
+def tile_attend_relu2_kernel(tc, qT, k_words, k_scales, vT, vs, offs, out):
+    nc = tc.nc
+    with ExitStack() as ctx:
+        sb = ctx.enter_context(tc.tile_pool(name="sb", bufs=1))
+        ps = ctx.enter_context(tc.psum_pool(name="ps", bufs=1))
+
+        def sbuf(name, shape, dtype):
+            return sb.tile(shape, dtype, name=name, align_bytes=64)
+
+        def bank(number, name, shape):
+            return ps.tile(shape, F32, name=name, tag="bank%d" % number)
+
+        offsets = sb.tile([P, B * N // 16], U16, name="offsets")
+        nc.sync.dma_start(offsets[:], offs)
+
+        def listed(b):
+            return offsets[:, b * N // 16 : (b + 1) * N // 16]
+
+        scale_pool = sbuf("scale_pool", [P, T], U8)
+        vs_pool = sbuf("vs_pool", [P, T], F32)
+        nc.vector.memset(scale_pool[:].bitcast(I32), 0)
+        nc.vector.memset(vs_pool[:], 0.0)
+        for quad in range(4):
+            nc.scalar.dma_start(
+                scale_pool[32 * quad : 32 * quad + 4, :].bitcast(I32),
+                k_scales[0, 4 * quad : 4 * quad + 4, :].bitcast(I32),
+            )
+        nc.gpsimd.dma_start(vs_pool[VS_ROW : VS_ROW + 1, :], vs[0:1, :])
+
+        q_raw = sb.tile([P, B, PACK, NQ], F32, name="q_raw", tag="q_then_v", align_bytes=64)
+        nc.sync.dma_start(q_raw[:], qT.rearrange("b (p j) n -> p b j n", j=PACK))
+        word_pool = sbuf("word_pool", [P, T], U32)
+        nc.sync.dma_start(word_pool[:].bitcast(I32), k_words[0].rearrange("p t r -> p (t r)").bitcast(I32))
+        v_pool = [sbuf("v_pool0", [P, T], F32)]
+        nc.sync.dma_start(v_pool[0][:], vT[0:P, :])
+
+        ident = sbuf("ident", [P, P], F32)
+        make_identity(nc, ident[:])
+
+        scale_listed = sbuf("scale_listed", [P, B * N], U8)
+        nc.vector.tensor_copy(scale_listed[:], scale_pool[:].indirect(offsets[:]))
+        vs_listed = sbuf("vs_listed", [P, B * N], F32)
+        nc.vector.tensor_copy(vs_listed[:], vs_pool[:].indirect(offsets[:]))
+        k_scale = sbuf("k_scale", [P, B * N], U8)
+        nc.vector.tensor_copy(
+            k_scale[:].bitcast(I32).rearrange("p (b t g w) -> p b t g w", b=B, t=PACK, w=2),
+            scale_listed[:].bitcast(I32).rearrange("p (b g t w) -> p b t g w", b=B, t=PACK, w=2),
+        )
+
+        q_bf = sbuf("q_bf", [P, B, NQ * PACK], BF16)
+        for b in range(B):
+            nc.scalar.activation(
+                q_bf[:, b, :].rearrange("p (c i j) -> p c j i", i=4, j=PACK),
+                q_raw[:, b, :, :].rearrange("p j (c i) -> p c j i", i=4),
+                ACT.Copy,
+            )
+        v_pool.append(sb.tile([P, T], F32, name="v_pool1", tag="q_then_v", align_bytes=64))
+        nc.sync.dma_start(v_pool[1][:], vT[P:DV, :])
+        q_codes = sbuf("q_codes", [P, B * NQ], U32)
+        q_scale = sbuf("q_scale", [P, B * NQ], U8)
+        nc.vector.quantize_mx(
+            out=q_codes[:].bitcast(FP8X4), scales=q_scale[:], in_=q_bf[:].rearrange("p b n -> p (b n)")
+        )
+
+        vs_slot = sbuf("vs_slot", [P, B, PACK], F32)
+        for b in range(B):
+            vs_turned = bank(b, "vs_turned%d" % b, [P, PACK, P])
+            vs_placed = sbuf("vs_placed%d" % b, [P, PACK, P], F32)
+            nc.scalar.copy(
+                vs_placed[:].rearrange("p t (g r) -> p t g r", r=8),
+                vs_listed[:, b * N : (b + 1) * N].rearrange("p (g t r) -> p t g r", t=PACK, r=8),
+            )
+            for t in range(PACK):
+                nc.tensor.transpose(vs_turned[:, t, :], vs_placed[:, t, :], ident[:])
+            nc.scalar.copy(vs_slot[:, b, :], vs_turned[:, :, VS_ROW])
+
+        keys = []
+        for b in range(B):
+            k_listed = sbuf("k_listed%d" % b, [P, N], U32)
+            nc.vector.tensor_copy(
+                k_listed[:].rearrange("p (t g r) -> p g t r", t=PACK, r=8),
+                word_pool[:].indirect(listed(b)),
+            )
+            keys.append(k_listed)
+
+        weights = []
+        for b in range(B):
+            scores = bank(2 + b, "scores%d" % b, [P, PACK, NQ])
+            for t in range(PACK):
+                c0 = b * N + t * P
+                nc.tensor.matmul_mx(
+                    out=scores[:, t, :],
+                    lhsT=keys[b][:, t * P : (t + 1) * P].bitcast(FP8X4),
+                    lhsT_scale=k_scale[:, c0 : c0 + P],
+                    rhs=q_codes[:, b * NQ : (b + 1) * NQ].bitcast(FP8X4),
+                    rhs_scale=q_scale[:, b * NQ : (b + 1) * NQ],
+                    start=True,
+                    stop=True,
+                )
+            positive = sbuf("positive%d" % b, [P, NQ, PACK], F32)
+            nc.scalar.activation(positive[:], scores[:].rearrange("p t q -> p q t"), ACT.Relu)
+            weight = sbuf("weight%d" % b, [P, NQ, PACK], F32)
+            nc.scalar.activation(weight[:], positive[:], ACT.Square)
+            weights.append(weight)
+
+        def gather_values(b, h):
+            v_listed = sbuf("v_listed%d%d" % (b, h), [P, N], BF16)
+            nc.vector.tensor_copy(
+                v_listed[:].rearrange("p (u g r s) -> p g u s r", u=2, r=8, s=2),
+                v_pool[h][:].indirect(listed(b)),
+            )
+            return v_listed
+
+        def turn_values(b, h, v_listed, number):
+            v_turned = bank(number, "v_turned%d%d" % (b, h), [P, 2, P])
+            pairs = v_listed[:].bitcast(F32)
+            for u in range(2):
+                nc.tensor.transpose(v_turned[:, u, :], pairs[:, u * P : (u + 1) * P], ident[:])
+            v_bf = sbuf("v_bf%d%d" % (b, h), [P, P * PACK], BF16)
+            nc.scalar.copy(
+                v_bf[:].bitcast(F32).rearrange("p (e u) -> p e u", u=2), v_turned[:].rearrange("p u e -> p e u")
+            )
+            return v_bf
+
+        def quantize(name, values, width):
+            codes = sbuf(name + "_codes", [P, width], U32)
+            scale = sbuf(name + "_scale", [P, width], U8)
+            nc.vector.quantize_mx(out=codes[:].bitcast(FP8X4), scales=scale[:], in_=values)
+            return codes, scale
+
+        def product(b, h, v_mx, number, target):
+            sums = bank(number, "sums%d%d" % (b, h), [P, P])
+            nc.tensor.matmul_mx(
+                out=sums[:],
+                lhsT=w_codes[:, b * P : (b + 1) * P].bitcast(FP8X4),
+                lhsT_scale=w_scale[:, b * P : (b + 1) * P],
+                rhs=v_mx[0][:].bitcast(FP8X4),
+                rhs_scale=v_mx[1][:],
+                start=True,
+                stop=True,
+            )
+            nc.scalar.activation(target, sums[:], ACT.Copy, scale=inverse[:, b : b + 1])
+
+        v_first = [turn_values(b, 0, gather_values(b, 0), b) for b in range(B)]
+
+        w_bf = sbuf("w_bf", [P, B, NQ, PACK], BF16)
+        total = sbuf("total", [P, B], F32)
+        for b in range(B):
+            nc.vector.tensor_tensor(
+                w_bf[:, b, :, :], weights[b][:], vs_slot[:, b : b + 1, :].to_broadcast([P, NQ, PACK]), ALU.mult
+            )
+            partial = bank(4 + b, "partial%d" % b, [P, P])
+            for t in range(PACK):
+                nc.tensor.matmul(
+                    partial[:], weights[b][:, :, t], ident[:], start=(t == 0), stop=(t == PACK - 1), is_transpose=True
+                )
+            shifted = sbuf("shifted%d" % b, [P, P], F32)
+            nc.scalar.activation(shifted[:], partial[:], ACT.Identity, bias=1.0 / P, accum_out=total[:, b : b + 1])
+
+        v_mx = [quantize("v%d0" % b, v_first[b][:], P) for b in range(B)]
+        v_second = [turn_values(b, 1, gather_values(b, 1), 6 + b) for b in range(B)]
+
+        w_codes, w_scale = quantize("w", w_bf[:].rearrange("p b q t -> p (b q t)"), B * NQ)
+        inverse = sbuf("inverse", [P, B], F32)
+        nc.vector.reciprocal(inverse[:], total[:])
+        first = sbuf("first", [P, B, P], F32)
+        for b in range(B):
+            product(b, 0, v_mx[b], 2 + b, first[:, b, :])
+        nc.sync.dma_start(out[:, :, 0:P].rearrange("b q e -> q b e"), first[:])
+
+        for b in range(B):
+            second = sbuf("second%d" % b, [P, P], F32)
+            product(b, 1, quantize("v%d1" % b, v_second[b][:], P), b, second[:])
+            nc.sync.dma_start(out[b, :, P:DV], second[:])

@@ -48,14 +48,15 @@ def tile_attend_relu2_kernel(tc, qT, k_words, k_scales, vT, vs, offs, out):
                 scale_pool[32 * quad : 32 * quad + 4, :].bitcast(I32),
                 k_scales[0, 4 * quad : 4 * quad + 4, :].bitcast(I32),
             )
-        nc.gpsimd.dma_start(vs_pool[VS_ROW : VS_ROW + 1, :], vs[0:1, :])
+        nc.scalar.dma_start(vs_pool[VS_ROW : VS_ROW + 1, :], vs[0:1, :])
 
-        q_raw = sb.tile([P, B, PACK, NQ], F32, name="q_raw", tag="q_then_v", align_bytes=64)
+        q_raw = sbuf("q_raw", [P, B, PACK, NQ], F32)
         nc.sync.dma_start(q_raw[:], qT.rearrange("b (p j) n -> p b j n", j=PACK))
         word_pool = sbuf("word_pool", [P, T], U32)
         nc.sync.dma_start(word_pool[:].bitcast(I32), k_words[0].rearrange("p t r -> p (t r)").bitcast(I32))
-        v_pool = [sbuf("v_pool0", [P, T], F32)]
-        nc.sync.dma_start(v_pool[0][:], vT[0:P, :])
+        v_pool = [sbuf("v_pool%d" % h, [P, T], F32) for h in range(HALVES)]
+        for h in range(HALVES):
+            nc.sync.dma_start(v_pool[h][:], vT[h * P : (h + 1) * P, :])
 
         ident = sbuf("ident", [P, P], F32)
         make_identity(nc, ident[:])
@@ -63,7 +64,10 @@ def tile_attend_relu2_kernel(tc, qT, k_words, k_scales, vT, vs, offs, out):
         scale_listed = sbuf("scale_listed", [P, B * N], U8)
         nc.vector.tensor_copy(scale_listed[:], scale_pool[:].indirect(offsets[:]))
         vs_listed = sbuf("vs_listed", [P, B * N], F32)
-        nc.vector.tensor_copy(vs_listed[:], vs_pool[:].indirect(offsets[:]))
+        nc.vector.tensor_copy(
+            vs_listed[:].bitcast(U32).rearrange("p (b t g r) -> p b g t r", b=B, t=PACK, r=8),
+            vs_pool[:].bitcast(U32).indirect(offsets[:]),
+        )
         k_scale = sbuf("k_scale", [P, B * N], U8)
         nc.vector.tensor_copy(
             k_scale[:].bitcast(I32).rearrange("p (b t g w) -> p b t g w", b=B, t=PACK, w=2),
@@ -77,8 +81,6 @@ def tile_attend_relu2_kernel(tc, qT, k_words, k_scales, vT, vs, offs, out):
                 q_raw[:, b, :, :].rearrange("p j (c i) -> p c j i", i=4),
                 ACT.Copy,
             )
-        v_pool.append(sb.tile([P, T], F32, name="v_pool1", tag="q_then_v", align_bytes=64))
-        nc.sync.dma_start(v_pool[1][:], vT[P:DV, :])
         q_codes = sbuf("q_codes", [P, B * NQ], U32)
         q_scale = sbuf("q_scale", [P, B * NQ], U8)
         nc.vector.quantize_mx(
@@ -88,13 +90,9 @@ def tile_attend_relu2_kernel(tc, qT, k_words, k_scales, vT, vs, offs, out):
         vs_slot = sbuf("vs_slot", [P, B, PACK], F32)
         for b in range(B):
             vs_turned = bank(b, "vs_turned%d" % b, [P, PACK, P])
-            vs_placed = sbuf("vs_placed%d" % b, [P, PACK, P], F32)
-            nc.scalar.copy(
-                vs_placed[:].rearrange("p t (g r) -> p t g r", r=8),
-                vs_listed[:, b * N : (b + 1) * N].rearrange("p (g t r) -> p t g r", t=PACK, r=8),
-            )
             for t in range(PACK):
-                nc.tensor.transpose(vs_turned[:, t, :], vs_placed[:, t, :], ident[:])
+                c0 = b * N + t * P
+                nc.tensor.transpose(vs_turned[:, t, :], vs_listed[:, c0 : c0 + P], ident[:])
             nc.scalar.copy(vs_slot[:, b, :], vs_turned[:, :, VS_ROW])
 
         keys = []

@@ -25,7 +25,11 @@ def tile_attend_relu2_kernel(tc, qT, k_words, k_scales, vT, vs, offs, out):
     nc = tc.nc
     with ExitStack() as ctx:
         sb = ctx.enter_context(tc.tile_pool(name="sb", bufs=1))
+        reused = ctx.enter_context(tc.tile_pool(name="reused", bufs=1))
         ps = ctx.enter_context(tc.psum_pool(name="ps", bufs=1))
+
+        def placed(name, shape, dtype, kib):
+            return reused.tile(shape, dtype, name=name, align_bytes=64, offset=kib * 1024)
 
         def sbuf(name, shape, dtype):
             return sb.tile(shape, dtype, name=name, align_bytes=64)
@@ -39,8 +43,8 @@ def tile_attend_relu2_kernel(tc, qT, k_words, k_scales, vT, vs, offs, out):
         def listed(b):
             return offsets[:, b * N // 16 : (b + 1) * N // 16]
 
-        scale_pool = sbuf("scale_pool", [P, T], U8)
-        vs_pool = sbuf("vs_pool", [P, T], F32)
+        scale_pool = placed("scale_pool", [P, T], U8, 0)
+        vs_pool = placed("vs_pool", [P, T], F32, 4)
         nc.vector.memset(scale_pool[:].bitcast(I32), 0)
         nc.vector.memset(vs_pool[:], 0.0)
         for quad in range(4):
@@ -48,22 +52,21 @@ def tile_attend_relu2_kernel(tc, qT, k_words, k_scales, vT, vs, offs, out):
                 scale_pool[32 * quad : 32 * quad + 4, :].bitcast(I32),
                 k_scales[0, 4 * quad : 4 * quad + 4, :].bitcast(I32),
             )
-        nc.scalar.dma_start(vs_pool[VS_ROW : VS_ROW + 1, :], vs[0:1, :])
+        nc.scalar.dma_start(vs_pool[VS_ROW:P:64, :], vs[0:2, :])
 
-        q_raw = sbuf("q_raw", [P, B, PACK, NQ], F32)
+        q_raw = placed("q_raw", [P, B, PACK, NQ], F32, 20)
         nc.sync.dma_start(q_raw[:], qT.rearrange("b (p j) n -> p b j n", j=PACK))
-        word_pool = sbuf("word_pool", [P, T], U32)
+        word_pool = placed("word_pool", [P, T], U32, 12)
         nc.sync.dma_start(word_pool[:].bitcast(I32), k_words[0].rearrange("p t r -> p (t r)").bitcast(I32))
-        v_pool = [sbuf("v_pool%d" % h, [P, T], F32) for h in range(HALVES)]
-        for h in range(HALVES):
-            nc.sync.dma_start(v_pool[h][:], vT[h * P : (h + 1) * P, :])
+        v_pool = [sbuf("v_pool0", [P, T], F32)]
+        nc.sync.dma_start(v_pool[0][:], vT[0:P, :])
 
         ident = sbuf("ident", [P, P], F32)
         make_identity(nc, ident[:])
 
         scale_listed = sbuf("scale_listed", [P, B * N], U8)
         nc.vector.tensor_copy(scale_listed[:], scale_pool[:].indirect(offsets[:]))
-        vs_listed = sbuf("vs_listed", [P, B * N], F32)
+        vs_listed = placed("vs_listed", [P, B * N], F32, 0)
         nc.vector.tensor_copy(
             vs_listed[:].bitcast(U32).rearrange("p (b t g r) -> p b g t r", b=B, t=PACK, r=8),
             vs_pool[:].bitcast(U32).indirect(offsets[:]),
@@ -81,7 +84,9 @@ def tile_attend_relu2_kernel(tc, qT, k_words, k_scales, vT, vs, offs, out):
                 q_raw[:, b, :, :].rearrange("p j (c i) -> p c j i", i=4),
                 ACT.Copy,
             )
-        q_codes = sbuf("q_codes", [P, B * NQ], U32)
+        v_pool.append(placed("v_pool1", [P, T], F32, 20))
+        nc.sync.dma_start(v_pool[1][:], vT[P:DV, :])
+        q_codes = placed("q_codes", [P, B * NQ], U32, 10)
         q_scale = sbuf("q_scale", [P, B * NQ], U8)
         nc.vector.quantize_mx(
             out=q_codes[:].bitcast(FP8X4), scales=q_scale[:], in_=q_bf[:].rearrange("p b n -> p (b n)")
@@ -97,7 +102,7 @@ def tile_attend_relu2_kernel(tc, qT, k_words, k_scales, vT, vs, offs, out):
 
         keys = []
         for b in range(B):
-            k_listed = sbuf("k_listed%d" % b, [P, N], U32)
+            k_listed = placed("k_listed%d" % b, [P, N], U32, 4 + 2 * b)
             nc.vector.tensor_copy(
                 k_listed[:].rearrange("p (t g r) -> p g t r", t=PACK, r=8),
                 word_pool[:].indirect(listed(b)),
@@ -125,7 +130,7 @@ def tile_attend_relu2_kernel(tc, qT, k_words, k_scales, vT, vs, offs, out):
             weights.append(weight)
 
         def gather_values(b, h):
-            v_listed = sbuf("v_listed%d%d" % (b, h), [P, N], BF16)
+            v_listed = placed("v_listed%d%d" % (b, h), [P, N], BF16, 8 + 4 * h + b)
             nc.vector.tensor_copy(
                 v_listed[:].rearrange("p (u g r s) -> p g u s r", u=2, r=8, s=2),
                 v_pool[h][:].indirect(listed(b)),

@@ -4,11 +4,13 @@ import concourse.mybir as mybir
 from concourse.masks import make_identity
 
 B, N, T, D, DV, NQ = 2, 512, 2048, 512, 256, 128
+FLOPS = 2 * B * NQ * N * (D + DV)
+
 P = 128
 PACK = 4
-HALVES = DV // P
+RUN = 8
 VS_ROW = 8
-FLOPS = 2 * B * NQ * N * (D + DV)
+LOW_CUTS = (0, 512, 1280, T)
 
 F32 = mybir.dt.float32
 BF16 = mybir.dt.bfloat16
@@ -24,20 +26,26 @@ ALU = mybir.AluOpType
 def tile_attend_relu2_kernel(tc, qT, k_words, k_scales, vT, vs, offs, out):
     nc = tc.nc
     with ExitStack() as ctx:
-        sb = ctx.enter_context(tc.tile_pool(name="sb", bufs=1))
+        held = ctx.enter_context(tc.tile_pool(name="held", bufs=1))
         reused = ctx.enter_context(tc.tile_pool(name="reused", bufs=1))
-        ps = ctx.enter_context(tc.psum_pool(name="ps", bufs=1))
+        psum = ctx.enter_context(tc.psum_pool(name="psum", bufs=1))
+
+        def sbuf(name, shape, dtype):
+            return held.tile(shape, dtype, name=name, align_bytes=64)
 
         def placed(name, shape, dtype, kib):
             return reused.tile(shape, dtype, name=name, align_bytes=64, offset=kib * 1024)
 
-        def sbuf(name, shape, dtype):
-            return sb.tile(shape, dtype, name=name, align_bytes=64)
+        def bank(number, name, shape, dtype=F32):
+            return psum.tile(shape, dtype, name=name, tag="bank%d" % number)
 
-        def bank(number, name, shape):
-            return ps.tile(shape, F32, name=name, tag="bank%d" % number)
+        def quantize(name, values, words):
+            codes = sbuf(name + "_codes", [P, words], U32)
+            scale = sbuf(name + "_scale", [P, words], U8)
+            nc.vector.quantize_mx(out=codes[:].bitcast(FP8X4), scales=scale[:], in_=values)
+            return codes, scale
 
-        offsets = sb.tile([P, B * N // 16], U16, name="offsets")
+        offsets = held.tile([P, B * N // 16], U16, name="offsets")
         nc.sync.dma_start(offsets[:], offs)
 
         def listed(b):
@@ -47,35 +55,43 @@ def tile_attend_relu2_kernel(tc, qT, k_words, k_scales, vT, vs, offs, out):
         vs_pool = placed("vs_pool", [P, T], F32, 4)
         nc.vector.memset(scale_pool[:].bitcast(I32), 0)
         nc.vector.memset(vs_pool[:], 0.0)
+        pieces = [slice(LOW_CUTS[c], LOW_CUTS[c + 1]) for c in range(len(LOW_CUTS) - 1)]
+        widths = [cols.stop - cols.start for cols in pieces]
+        v_low = [sbuf("v_low%d" % c, [P, width], F32) for c, width in enumerate(widths[:-1])]
+        v_low.append(placed("v_low_last", [P, widths[-1]], F32, 20))
+        nc.sync.dma_start(v_low[0][:], vT[0:P, pieces[0]])
         for quad in range(4):
-            nc.scalar.dma_start(
+            (nc.sync, nc.scalar)[quad % 2].dma_start(
                 scale_pool[32 * quad : 32 * quad + 4, :].bitcast(I32),
                 k_scales[0, 4 * quad : 4 * quad + 4, :].bitcast(I32),
             )
-        nc.scalar.dma_start(vs_pool[VS_ROW:P:64, :], vs[0:2, :])
-
-        q_raw = placed("q_raw", [P, B, PACK, NQ], F32, 20)
+        for c in range(1, len(pieces)):
+            nc.sync.dma_start(v_low[c][:], vT[0:P, pieces[c]])
+        q_raw = sbuf("q_raw", [P, B, PACK, NQ], F32)
         nc.sync.dma_start(q_raw[:], qT.rearrange("b (p j) n -> p b j n", j=PACK))
+        nc.sync.dma_start(vs_pool[VS_ROW : P : P // 2, :], vs[0:2, :])
         word_pool = placed("word_pool", [P, T], U32, 12)
         nc.sync.dma_start(word_pool[:].bitcast(I32), k_words[0].rearrange("p t r -> p (t r)").bitcast(I32))
-        v_pool = [sbuf("v_pool0", [P, T], F32)]
-        nc.sync.dma_start(v_pool[0][:], vT[0:P, :])
 
         ident = sbuf("ident", [P, P], F32)
         make_identity(nc, ident[:])
+        ident_bf = sbuf("ident_bf", [P, P], BF16)
+        make_identity(nc, ident_bf[:])
 
         scale_listed = sbuf("scale_listed", [P, B * N], U8)
         nc.vector.tensor_copy(scale_listed[:], scale_pool[:].indirect(offsets[:]))
-        vs_listed = placed("vs_listed", [P, B * N], F32, 0)
-        nc.vector.tensor_copy(
-            vs_listed[:].bitcast(U32).rearrange("p (b t g r) -> p b g t r", b=B, t=PACK, r=8),
-            vs_pool[:].bitcast(U32).indirect(offsets[:]),
-        )
-        k_scale = sbuf("k_scale", [P, B * N], U8)
-        nc.vector.tensor_copy(
-            k_scale[:].bitcast(I32).rearrange("p (b t g w) -> p b t g w", b=B, t=PACK, w=2),
-            scale_listed[:].bitcast(I32).rearrange("p (b g t w) -> p b t g w", b=B, t=PACK, w=2),
-        )
+        vs_lanes = placed("vs_lanes", [P, B * N], F32, 0)
+        for b in range(B):
+            nc.vector.tensor_copy(
+                vs_lanes[:, b * N : (b + 1) * N].bitcast(U32).rearrange("p (t g r) -> p g t r", t=PACK, r=RUN),
+                vs_pool[:].bitcast(U32).indirect(listed(b)),
+            )
+
+        v_low_bf = placed("v_low_bf", [P, T], BF16, 28)
+        for c, cols in enumerate(pieces):
+            nc.scalar.activation(v_low_bf[:, cols], v_low[c][:], ACT.Copy)
+        v_high = placed("v_high", [P, T], F32, 20)
+        nc.scalar.dma_start(v_high[:], vT[P:DV, :])
 
         q_bf = sbuf("q_bf", [P, B, NQ * PACK], BF16)
         for b in range(B):
@@ -84,40 +100,47 @@ def tile_attend_relu2_kernel(tc, qT, k_words, k_scales, vT, vs, offs, out):
                 q_raw[:, b, :, :].rearrange("p j (c i) -> p c j i", i=4),
                 ACT.Copy,
             )
-        v_pool.append(placed("v_pool1", [P, T], F32, 20))
-        nc.sync.dma_start(v_pool[1][:], vT[P:DV, :])
-        q_codes = placed("q_codes", [P, B * NQ], U32, 10)
-        q_scale = sbuf("q_scale", [P, B * NQ], U8)
-        nc.vector.quantize_mx(
-            out=q_codes[:].bitcast(FP8X4), scales=q_scale[:], in_=q_bf[:].rearrange("p b n -> p (b n)")
+        q_codes, q_scale = quantize("q", q_bf[:].rearrange("p b n -> p (b n)"), B * NQ)
+
+        k_scale = sbuf("k_scale", [P, B * N], U8)
+        nc.vector.tensor_copy(
+            k_scale[:].bitcast(I32).rearrange("p (b t g w) -> p b t g w", b=B, t=PACK, w=RUN // 4),
+            scale_listed[:].bitcast(I32).rearrange("p (b g t w) -> p b t g w", b=B, t=PACK, w=RUN // 4),
         )
 
-        vs_slot = sbuf("vs_slot", [P, B, PACK], F32)
+        low_lanes = []
+        for b in range(B):
+            lanes = sbuf("low_lanes%d" % b, [P, PACK, P], BF16)
+            nc.scalar.activation(
+                lanes[:].rearrange("p t (g r) -> p g t r", r=RUN), v_low_bf[:].indirect(listed(b)), ACT.Copy
+            )
+            low_lanes.append(lanes)
+
+        vs_slot = placed("vs_slot", [P, B, PACK], F32, 28)
         for b in range(B):
             vs_turned = bank(b, "vs_turned%d" % b, [P, PACK, P])
             for t in range(PACK):
-                c0 = b * N + t * P
-                nc.tensor.transpose(vs_turned[:, t, :], vs_listed[:, c0 : c0 + P], ident[:])
+                lane = slice(b * N + t * P, b * N + (t + 1) * P)
+                nc.tensor.transpose(vs_turned[:, t, :], vs_lanes[:, lane], ident[:])
             nc.scalar.copy(vs_slot[:, b, :], vs_turned[:, :, VS_ROW])
 
-        keys = []
+        k_lanes = []
         for b in range(B):
-            k_listed = placed("k_listed%d" % b, [P, N], U32, 4 + 2 * b)
+            lanes = placed("k_lanes%d" % b, [P, N], U32, 4 + 2 * b)
             nc.vector.tensor_copy(
-                k_listed[:].rearrange("p (t g r) -> p g t r", t=PACK, r=8),
-                word_pool[:].indirect(listed(b)),
+                lanes[:].rearrange("p (t g r) -> p g t r", t=PACK, r=RUN), word_pool[:].indirect(listed(b))
             )
-            keys.append(k_listed)
+            k_lanes.append(lanes)
 
-        weights = []
+        squares = []
         for b in range(B):
             scores = bank(2 + b, "scores%d" % b, [P, PACK, NQ])
             for t in range(PACK):
-                c0 = b * N + t * P
+                lane = slice(b * N + t * P, b * N + (t + 1) * P)
                 nc.tensor.matmul_mx(
                     out=scores[:, t, :],
-                    lhsT=keys[b][:, t * P : (t + 1) * P].bitcast(FP8X4),
-                    lhsT_scale=k_scale[:, c0 : c0 + P],
+                    lhsT=k_lanes[b][:, t * P : (t + 1) * P].bitcast(FP8X4),
+                    lhsT_scale=k_scale[:, lane],
                     rhs=q_codes[:, b * NQ : (b + 1) * NQ].bitcast(FP8X4),
                     rhs_scale=q_scale[:, b * NQ : (b + 1) * NQ],
                     start=True,
@@ -125,76 +148,70 @@ def tile_attend_relu2_kernel(tc, qT, k_words, k_scales, vT, vs, offs, out):
                 )
             positive = sbuf("positive%d" % b, [P, NQ, PACK], F32)
             nc.scalar.activation(positive[:], scores[:].rearrange("p t q -> p q t"), ACT.Relu)
-            weight = sbuf("weight%d" % b, [P, NQ, PACK], F32)
-            nc.scalar.activation(weight[:], positive[:], ACT.Square)
-            weights.append(weight)
+            square = sbuf("square%d" % b, [P, NQ, PACK], F32)
+            nc.scalar.activation(square[:], positive[:], ACT.Square)
+            squares.append(square)
 
-        def gather_values(b, h):
-            v_listed = placed("v_listed%d%d" % (b, h), [P, N], BF16, 8 + 4 * h + b)
+        high_lanes = []
+        for b in range(B):
+            lanes = placed("high_lanes%d" % b, [P, N], BF16, 12 + b)
             nc.vector.tensor_copy(
-                v_listed[:].rearrange("p (u g r s) -> p g u s r", u=2, r=8, s=2),
-                v_pool[h][:].indirect(listed(b)),
+                lanes[:].rearrange("p (u g r s) -> p g u s r", u=2, r=RUN, s=2), v_high[:].indirect(listed(b))
             )
-            return v_listed
+            high_lanes.append(lanes)
 
-        def turn_values(b, h, v_listed, number):
-            v_turned = bank(number, "v_turned%d%d" % (b, h), [P, 2, P])
-            pairs = v_listed[:].bitcast(F32)
-            for u in range(2):
-                nc.tensor.transpose(v_turned[:, u, :], pairs[:, u * P : (u + 1) * P], ident[:])
-            v_bf = sbuf("v_bf%d%d" % (b, h), [P, P * PACK], BF16)
+        v_bf = []
+        for b in range(B):
+            values = sbuf("v_bf%d" % b, [P, DV // P, P * PACK], BF16)
+            low_turned = bank(6 + b, "low_turned%d" % b, [P, PACK, P], BF16)
+            for t in range(PACK):
+                nc.tensor.transpose(low_turned[:, t, :], low_lanes[b][:, t, :], ident_bf[:])
             nc.scalar.copy(
-                v_bf[:].bitcast(F32).rearrange("p (e u) -> p e u", u=2), v_turned[:].rearrange("p u e -> p e u")
+                values[:, 0, :].rearrange("p (e t) -> p e t", t=PACK), low_turned[:].rearrange("p t e -> p e t")
             )
-            return v_bf
-
-        def quantize(name, values, width):
-            codes = sbuf(name + "_codes", [P, width], U32)
-            scale = sbuf(name + "_scale", [P, width], U8)
-            nc.vector.quantize_mx(out=codes[:].bitcast(FP8X4), scales=scale[:], in_=values)
-            return codes, scale
-
-        def product(b, h, v_mx, number, target):
-            sums = bank(number, "sums%d%d" % (b, h), [P, P])
-            nc.tensor.matmul_mx(
-                out=sums[:],
-                lhsT=w_codes[:, b * P : (b + 1) * P].bitcast(FP8X4),
-                lhsT_scale=w_scale[:, b * P : (b + 1) * P],
-                rhs=v_mx[0][:].bitcast(FP8X4),
-                rhs_scale=v_mx[1][:],
-                start=True,
-                stop=True,
+            high_turned = bank(4 + b, "high_turned%d" % b, [P, 2, P])
+            for u in range(2):
+                nc.tensor.transpose(
+                    high_turned[:, u, :], high_lanes[b][:].bitcast(F32)[:, u * P : (u + 1) * P], ident[:]
+                )
+            nc.scalar.copy(
+                values[:, 1, :].bitcast(F32).rearrange("p (e u) -> p e u", u=2),
+                high_turned[:].rearrange("p u e -> p e u"),
             )
-            nc.scalar.activation(target, sums[:], ACT.Copy, scale=inverse[:, b : b + 1])
-
-        v_first = [turn_values(b, 0, gather_values(b, 0), b) for b in range(B)]
+            v_bf.append(values)
 
         w_bf = sbuf("w_bf", [P, B, NQ, PACK], BF16)
         total = sbuf("total", [P, B], F32)
         for b in range(B):
             nc.vector.tensor_tensor(
-                w_bf[:, b, :, :], weights[b][:], vs_slot[:, b : b + 1, :].to_broadcast([P, NQ, PACK]), ALU.mult
+                w_bf[:, b, :, :], squares[b][:], vs_slot[:, b : b + 1, :].to_broadcast([P, NQ, PACK]), ALU.mult
             )
-            partial = bank(4 + b, "partial%d" % b, [P, P])
+            partial = bank(2 + b, "partial%d" % b, [P, P])
             for t in range(PACK):
                 nc.tensor.matmul(
-                    partial[:], weights[b][:, :, t], ident[:], start=(t == 0), stop=(t == PACK - 1), is_transpose=True
+                    partial[:], squares[b][:, :, t], ident[:], start=(t == 0), stop=(t == PACK - 1), is_transpose=True
                 )
-            shifted = sbuf("shifted%d" % b, [P, P], F32)
-            nc.scalar.activation(shifted[:], partial[:], ACT.Identity, bias=1.0 / P, accum_out=total[:, b : b + 1])
+            summands = sbuf("summands%d" % b, [P, P], F32)
+            nc.scalar.activation(summands[:], partial[:], ACT.Identity, bias=1.0 / P, accum_out=total[:, b : b + 1])
 
-        v_mx = [quantize("v%d0" % b, v_first[b][:], P) for b in range(B)]
-        v_second = [turn_values(b, 1, gather_values(b, 1), 6 + b) for b in range(B)]
-
+        v_mx = [quantize("v0", v_bf[0][:].rearrange("p h n -> p (h n)"), DV)]
         w_codes, w_scale = quantize("w", w_bf[:].rearrange("p b q t -> p (b q t)"), B * NQ)
-        inverse = sbuf("inverse", [P, B], F32)
-        nc.vector.reciprocal(inverse[:], total[:])
-        first = sbuf("first", [P, B, P], F32)
-        for b in range(B):
-            product(b, 0, v_mx[b], 2 + b, first[:, b, :])
-        nc.sync.dma_start(out[:, :, 0:P].rearrange("b q e -> q b e"), first[:])
+        inverse = [sbuf("inverse%d" % b, [P, 1], F32) for b in range(B)]
+        nc.vector.reciprocal(inverse[0][:], total[:, 0:1])
+        v_mx.append(quantize("v1", v_bf[1][:].rearrange("p h n -> p (h n)"), DV))
+        nc.vector.reciprocal(inverse[1][:], total[:, 1:2])
 
         for b in range(B):
-            second = sbuf("second%d" % b, [P, P], F32)
-            product(b, 1, quantize("v%d1" % b, v_second[b][:], P), b, second[:])
-            nc.sync.dma_start(out[b, :, P:DV], second[:])
+            sums = bank(b, "sums%d" % b, [P, DV])
+            nc.tensor.matmul_mx(
+                out=sums[:],
+                lhsT=w_codes[:, b * NQ : (b + 1) * NQ].bitcast(FP8X4),
+                lhsT_scale=w_scale[:, b * NQ : (b + 1) * NQ],
+                rhs=v_mx[b][0][:].bitcast(FP8X4),
+                rhs_scale=v_mx[b][1][:],
+                start=True,
+                stop=True,
+            )
+            result = sbuf("result%d" % b, [P, DV], F32)
+            nc.scalar.activation(result[:], sums[:], ACT.Copy, scale=inverse[b][:])
+            nc.sync.dma_start(out[b], result[:])

@@ -8,8 +8,7 @@ FLOPS = 2 * B * NQ * N * (D + DV)
 
 P = 128
 PACK = 4
-RUN = 8
-VS_ROW = 8
+VS_ROW = P - 1
 LOW_CUTS = (0, 512, 1280, T)
 
 F32 = mybir.dt.float32
@@ -51,167 +50,143 @@ def tile_attend_relu2_kernel(tc, qT, k_words, k_scales, vT, vs, offs, out):
         def listed(b):
             return offsets[:, b * N // 16 : (b + 1) * N // 16]
 
-        scale_pool = placed("scale_pool", [P, T], U8, 0)
-        vs_pool = placed("vs_pool", [P, T], F32, 4)
-        nc.vector.memset(scale_pool[:].bitcast(I32), 0)
-        nc.vector.memset(vs_pool[:], 0.0)
+        scale_pool = sbuf("scale_pool", [P, T], U8)
+        vs_pool = sbuf("vs_pool", [P, T], F32)
+        nc.gpsimd.memset(scale_pool[:].bitcast(I32), 0)
+        nc.vector.memset(vs_pool[0:VS_ROW, :], 0.0)
+        nc.sync.dma_start(vs_pool[VS_ROW:P, :], vs[0:1, :])
         pieces = [slice(LOW_CUTS[c], LOW_CUTS[c + 1]) for c in range(len(LOW_CUTS) - 1)]
-        widths = [cols.stop - cols.start for cols in pieces]
-        v_low = [sbuf("v_low%d" % c, [P, width], F32) for c, width in enumerate(widths[:-1])]
-        v_low.append(placed("v_low_last", [P, widths[-1]], F32, 20))
+        v_low = [sbuf("v_low%d" % c, [P, cols.stop - cols.start], F32) for c, cols in enumerate(pieces)]
         nc.sync.dma_start(v_low[0][:], vT[0:P, pieces[0]])
         for quad in range(4):
-            (nc.sync, nc.scalar)[quad % 2].dma_start(
+            nc.sync.dma_start(
                 scale_pool[32 * quad : 32 * quad + 4, :].bitcast(I32),
                 k_scales[0, 4 * quad : 4 * quad + 4, :].bitcast(I32),
             )
         for c in range(1, len(pieces)):
             nc.sync.dma_start(v_low[c][:], vT[0:P, pieces[c]])
-        q_raw = sbuf("q_raw", [P, B, PACK, NQ], F32)
-        nc.sync.dma_start(q_raw[:], qT.rearrange("b (p j) n -> p b j n", j=PACK))
-        nc.sync.dma_start(vs_pool[VS_ROW : P : P // 2, :], vs[0:2, :])
-        word_pool = placed("word_pool", [P, T], U32, 12)
+        q_raw = []
+        for b in range(B):
+            raw = placed("q_raw%d" % b, [P, PACK, NQ], F32, 2 * b)
+            nc.sync.dma_start(raw[:], qT[b].rearrange("(p j) n -> p j n", j=PACK))
+            q_raw.append(raw)
+        word_pool = sbuf("word_pool", [P, T], U32)
         nc.sync.dma_start(word_pool[:].bitcast(I32), k_words[0].rearrange("p t r -> p (t r)").bitcast(I32))
+        v_high = sbuf("v_high", [P, T], F32)
+        nc.sync.dma_start(v_high[:], vT[P:DV, :])
 
         ident = sbuf("ident", [P, P], F32)
         make_identity(nc, ident[:])
-        ident_bf = sbuf("ident_bf", [P, P], BF16)
-        make_identity(nc, ident_bf[:])
-
-        scale_listed = sbuf("scale_listed", [P, B * N], U8)
-        nc.vector.tensor_copy(scale_listed[:], scale_pool[:].indirect(offsets[:]))
-        vs_lanes = placed("vs_lanes", [P, B * N], F32, 0)
+        positive = [sbuf("positive%d" % b, [P, N + 1], F32) for b in range(B)]
         for b in range(B):
-            nc.vector.tensor_copy(
-                vs_lanes[:, b * N : (b + 1) * N].bitcast(U32).rearrange("p (t g r) -> p g t r", t=PACK, r=RUN),
-                vs_pool[:].bitcast(U32).indirect(listed(b)),
-            )
+            nc.gpsimd.memset(positive[b][:, N : N + 1], 1.0)
 
-        v_low_bf = placed("v_low_bf", [P, T], BF16, 28)
+        vs_listed = sbuf("vs_listed", [P, B * N], F32)
+        nc.vector.tensor_copy(vs_listed[:], vs_pool[:].indirect(offsets[:]))
+        k_scale = sbuf("k_scale", [P, B * N], U8)
+        nc.vector.tensor_copy(k_scale[:], scale_pool[:].indirect(offsets[:]))
+
+        v_low_bf = placed("v_low_bf", [P, T], BF16, 4)
         for c, cols in enumerate(pieces):
             nc.scalar.activation(v_low_bf[:, cols], v_low[c][:], ACT.Copy)
-        v_high = placed("v_high", [P, T], F32, 20)
-        nc.scalar.dma_start(v_high[:], vT[P:DV, :])
 
         q_bf = sbuf("q_bf", [P, B, NQ * PACK], BF16)
         for b in range(B):
             nc.scalar.activation(
                 q_bf[:, b, :].rearrange("p (c i j) -> p c j i", i=4, j=PACK),
-                q_raw[:, b, :, :].rearrange("p j (c i) -> p c j i", i=4),
+                q_raw[b][:].rearrange("p j (c i) -> p c j i", i=4),
                 ACT.Copy,
             )
         q_codes, q_scale = quantize("q", q_bf[:].rearrange("p b n -> p (b n)"), B * NQ)
 
-        k_scale = sbuf("k_scale", [P, B * N], U8)
-        nc.vector.tensor_copy(
-            k_scale[:].bitcast(I32).rearrange("p (b t g w) -> p b t g w", b=B, t=PACK, w=RUN // 4),
-            scale_listed[:].bitcast(I32).rearrange("p (b g t w) -> p b t g w", b=B, t=PACK, w=RUN // 4),
-        )
-
-        low_lanes = []
+        low_listed = []
         for b in range(B):
-            lanes = sbuf("low_lanes%d" % b, [P, PACK, P], BF16)
-            nc.scalar.activation(
-                lanes[:].rearrange("p t (g r) -> p g t r", r=RUN), v_low_bf[:].indirect(listed(b)), ACT.Copy
-            )
-            low_lanes.append(lanes)
+            picked = placed("low_listed%d" % b, [P, N], BF16, 2 + b)
+            nc.scalar.activation(picked[:], v_low_bf[:].indirect(listed(b)), ACT.Copy)
+            low_listed.append(picked)
 
-        vs_slot = placed("vs_slot", [P, B, PACK], F32, 28)
+        vs_turned = bank(0, "vs_turned", [P, P + B * PACK])
+        for lane in reversed(range(B * PACK)):
+            b, t = divmod(lane, PACK)
+            nc.tensor.transpose(vs_turned[:, lane : lane + P], vs_listed[:, b * N + t : (b + 1) * N : PACK], ident[:])
+        vs_slot = placed("vs_slot", [P, B, PACK], F32, 4)
+        nc.scalar.copy(vs_slot[:].rearrange("p b t -> p (b t)"), vs_turned[:, VS_ROW : VS_ROW + B * PACK])
+
+        k_listed = []
         for b in range(B):
-            vs_turned = bank(b, "vs_turned%d" % b, [P, PACK, P])
-            for t in range(PACK):
-                lane = slice(b * N + t * P, b * N + (t + 1) * P)
-                nc.tensor.transpose(vs_turned[:, t, :], vs_lanes[:, lane], ident[:])
-            nc.scalar.copy(vs_slot[:, b, :], vs_turned[:, :, VS_ROW])
+            picked = sbuf("k_listed%d" % b, [P, N], U32)
+            nc.vector.tensor_copy(picked[:], word_pool[:].indirect(listed(b)))
+            k_listed.append(picked)
 
-        k_lanes = []
-        for b in range(B):
-            lanes = placed("k_lanes%d" % b, [P, N], U32, 4 + 2 * b)
-            nc.vector.tensor_copy(
-                lanes[:].rearrange("p (t g r) -> p g t r", t=PACK, r=RUN), word_pool[:].indirect(listed(b))
-            )
-            k_lanes.append(lanes)
-
-        squares = []
-        for b in range(B):
-            scores = bank(2 + b, "scores%d" % b, [P, PACK, NQ])
-            for t in range(PACK):
-                lane = slice(b * N + t * P, b * N + (t + 1) * P)
-                nc.tensor.matmul_mx(
-                    out=scores[:, t, :],
-                    lhsT=k_lanes[b][:, t * P : (t + 1) * P].bitcast(FP8X4),
-                    lhsT_scale=k_scale[:, lane],
-                    rhs=q_codes[:, b * NQ : (b + 1) * NQ].bitcast(FP8X4),
-                    rhs_scale=q_scale[:, b * NQ : (b + 1) * NQ],
-                    start=True,
-                    stop=True,
-                )
-            positive = sbuf("positive%d" % b, [P, NQ, PACK], F32)
-            nc.scalar.activation(positive[:], scores[:].rearrange("p t q -> p q t"), ACT.Relu)
-            square = sbuf("square%d" % b, [P, NQ, PACK], F32)
-            nc.scalar.activation(square[:], positive[:], ACT.Square)
-            squares.append(square)
-
-        high_lanes = []
-        for b in range(B):
-            lanes = placed("high_lanes%d" % b, [P, N], BF16, 12 + b)
-            nc.vector.tensor_copy(
-                lanes[:].rearrange("p (u g r s) -> p g u s r", u=2, r=RUN, s=2), v_high[:].indirect(listed(b))
-            )
-            high_lanes.append(lanes)
-
-        v_bf = []
-        for b in range(B):
-            values = sbuf("v_bf%d" % b, [P, DV // P, P * PACK], BF16)
-            low_turned = bank(6 + b, "low_turned%d" % b, [P, PACK, P], BF16)
-            for t in range(PACK):
-                nc.tensor.transpose(low_turned[:, t, :], low_lanes[b][:, t, :], ident_bf[:])
-            nc.scalar.copy(
-                values[:, 0, :].rearrange("p (e t) -> p e t", t=PACK), low_turned[:].rearrange("p t e -> p e t")
-            )
-            high_turned = bank(4 + b, "high_turned%d" % b, [P, 2, P])
-            for u in range(2):
-                nc.tensor.transpose(
-                    high_turned[:, u, :], high_lanes[b][:].bitcast(F32)[:, u * P : (u + 1) * P], ident[:]
-                )
-            nc.scalar.copy(
-                values[:, 1, :].bitcast(F32).rearrange("p (e u) -> p e u", u=2),
-                high_turned[:].rearrange("p u e -> p e u"),
-            )
-            v_bf.append(values)
-
-        w_bf = sbuf("w_bf", [P, B, NQ, PACK], BF16)
         total = sbuf("total", [P, B], F32)
+        p_turned = []
+        for b in range(B):
+            scores = bank(2 + b, "scores%d" % b, [P, N])
+            nc.tensor.matmul_mx(
+                out=scores[:],
+                lhsT=q_codes[:, b * NQ : (b + 1) * NQ].bitcast(FP8X4),
+                lhsT_scale=q_scale[:, b * NQ : (b + 1) * NQ],
+                rhs=k_listed[b][:].bitcast(FP8X4),
+                rhs_scale=k_scale[:, b * N : (b + 1) * N],
+                start=True,
+                stop=True,
+            )
+            nc.scalar.activation(
+                positive[b][:, 0:N].rearrange("p (t s) -> p t s", t=PACK),
+                scores[:].rearrange("p (s t) -> p t s", t=PACK),
+                ACT.Relu,
+            )
+            square = sbuf("square%d" % b, [P, N + 1], F32)
+            nc.scalar.activation(square[:], positive[b][:], ACT.Square, accum_out=total[:, b : b + 1])
+            turned = bank(4 + b, "p_turned%d" % b, [P, PACK, NQ])
+            for t in range(PACK):
+                nc.tensor.transpose(turned[:, t, :], square[:, t * P : (t + 1) * P], ident[:])
+            p_turned.append(turned)
+
+        high_listed = []
+        for b in range(B):
+            picked = sbuf("high_listed%d" % b, [P, N], BF16)
+            nc.vector.tensor_copy(picked[:], v_high[:].indirect(listed(b)))
+            high_listed.append(picked)
+
+        v_bf = [sbuf("v_bf%d" % b, [P, DV // P, P * PACK], BF16) for b in range(B)]
+
+        def turn_values(number, name, picked, target):
+            turned = bank(number, name, [P, 2, P])
+            for u in range(2):
+                nc.tensor.transpose(turned[:, u, :], picked[:].bitcast(F32)[:, u : N // 2 : 2], ident[:])
+            nc.scalar.copy(
+                target.bitcast(F32).rearrange("p (e u) -> p e u", u=2), turned[:].rearrange("p u e -> p e u")
+            )
+
+        for b in range(B):
+            turn_values(2 + b, "low_turned%d" % b, low_listed[b], v_bf[b][:, 0, :])
+            turn_values(6 + b, "high_turned%d" % b, high_listed[b], v_bf[b][:, 1, :])
+
+        w_bf = [sbuf("w_bf%d" % b, [P, NQ, PACK], BF16) for b in range(B)]
+        inverse = sbuf("inverse", [P, B], F32)
         for b in range(B):
             nc.vector.tensor_tensor(
-                w_bf[:, b, :, :], squares[b][:], vs_slot[:, b : b + 1, :].to_broadcast([P, NQ, PACK]), ALU.mult
+                w_bf[b][:],
+                p_turned[b][:].rearrange("p t q -> p q t"),
+                vs_slot[:, b : b + 1, :].to_broadcast([P, NQ, PACK]),
+                ALU.mult,
             )
-            partial = bank(2 + b, "partial%d" % b, [P, P])
-            for t in range(PACK):
-                nc.tensor.matmul(
-                    partial[:], squares[b][:, :, t], ident[:], start=(t == 0), stop=(t == PACK - 1), is_transpose=True
-                )
-            summands = sbuf("summands%d" % b, [P, P], F32)
-            nc.scalar.activation(summands[:], partial[:], ACT.Identity, bias=1.0 / P, accum_out=total[:, b : b + 1])
-
-        v_mx = [quantize("v0", v_bf[0][:].rearrange("p h n -> p (h n)"), DV)]
-        w_codes, w_scale = quantize("w", w_bf[:].rearrange("p b q t -> p (b q t)"), B * NQ)
-        inverse = [sbuf("inverse%d" % b, [P, 1], F32) for b in range(B)]
-        nc.vector.reciprocal(inverse[0][:], total[:, 0:1])
-        v_mx.append(quantize("v1", v_bf[1][:].rearrange("p h n -> p (h n)"), DV))
-        nc.vector.reciprocal(inverse[1][:], total[:, 1:2])
+        nc.vector.reciprocal(inverse[:], total[:])
 
         for b in range(B):
+            w_codes, w_scale = quantize("w%d" % b, w_bf[b][:].rearrange("p q t -> p (q t)"), NQ)
+            v_codes, v_scale = quantize("v%d" % b, v_bf[b][:].rearrange("p h n -> p (h n)"), DV)
             sums = bank(b, "sums%d" % b, [P, DV])
             nc.tensor.matmul_mx(
                 out=sums[:],
-                lhsT=w_codes[:, b * NQ : (b + 1) * NQ].bitcast(FP8X4),
-                lhsT_scale=w_scale[:, b * NQ : (b + 1) * NQ],
-                rhs=v_mx[b][0][:].bitcast(FP8X4),
-                rhs_scale=v_mx[b][1][:],
+                lhsT=w_codes[:].bitcast(FP8X4),
+                lhsT_scale=w_scale[:],
+                rhs=v_codes[:].bitcast(FP8X4),
+                rhs_scale=v_scale[:],
                 start=True,
                 stop=True,
             )
             result = sbuf("result%d" % b, [P, DV], F32)
-            nc.scalar.activation(result[:], sums[:], ACT.Copy, scale=inverse[b][:])
+            nc.scalar.activation(result[:], sums[:], ACT.Copy, scale=inverse[:, b : b + 1])
             nc.sync.dma_start(out[b], result[:])

@@ -9,7 +9,7 @@ FLOPS = 2 * B * NQ * N * (D + DV)
 P = 128
 PACK = 4
 VS_ROW = P - 1
-LOW_CUTS = (0, 512, 1280, T)
+LOW_CUTS = (0, 512, 1408, T)
 
 F32 = mybir.dt.float32
 BF16 = mybir.dt.bfloat16
@@ -57,27 +57,26 @@ def tile_attend_relu2_kernel(tc, qT, k_words, k_scales, vT, vs, offs, out):
         nc.sync.dma_start(vs_pool[VS_ROW:P, :], vs[0:1, :])
         pieces = [slice(LOW_CUTS[c], LOW_CUTS[c + 1]) for c in range(len(LOW_CUTS) - 1)]
         v_low = [sbuf("v_low%d" % c, [P, cols.stop - cols.start], F32) for c, cols in enumerate(pieces)]
-        nc.sync.dma_start(v_low[0][:], vT[0:P, pieces[0]])
+        for c in range(2):
+            nc.sync.dma_start(v_low[c][:], vT[0:P, pieces[c]])
         for quad in range(4):
             nc.sync.dma_start(
                 scale_pool[32 * quad : 32 * quad + 4, :].bitcast(I32),
                 k_scales[0, 4 * quad : 4 * quad + 4, :].bitcast(I32),
             )
-        for c in range(1, len(pieces)):
+        for c in range(2, len(pieces)):
             nc.sync.dma_start(v_low[c][:], vT[0:P, pieces[c]])
-        q_raw = []
-        for b in range(B):
-            raw = placed("q_raw%d" % b, [P, PACK, NQ], F32, 2 * b)
-            nc.sync.dma_start(raw[:], qT[b].rearrange("(p j) n -> p j n", j=PACK))
-            q_raw.append(raw)
+        q_raw = [placed("q_raw%d" % b, [P, PACK, NQ], F32, 2 * b) for b in range(B)]
+        nc.sync.dma_start(q_raw[0][:], qT[0].rearrange("(p j) n -> p j n", j=PACK))
         word_pool = sbuf("word_pool", [P, T], U32)
         nc.sync.dma_start(word_pool[:].bitcast(I32), k_words[0].rearrange("p t r -> p (t r)").bitcast(I32))
-        v_high = sbuf("v_high", [P, T], F32)
+        nc.sync.dma_start(q_raw[1][:], qT[1].rearrange("(p j) n -> p j n", j=PACK))
+        v_high = placed("v_high", [P, T], F32, 8)
         nc.sync.dma_start(v_high[:], vT[P:DV, :])
 
         ident = sbuf("ident", [P, P], F32)
         make_identity(nc, ident[:])
-        positive = [sbuf("positive%d" % b, [P, N + 1], F32) for b in range(B)]
+        positive = [sbuf("positive0", [P, N + 1], F32), placed("positive1", [P, N + 1], F32, 17)]
         for b in range(B):
             nc.gpsimd.memset(positive[b][:, N : N + 1], 1.0)
 
@@ -90,20 +89,18 @@ def tile_attend_relu2_kernel(tc, qT, k_words, k_scales, vT, vs, offs, out):
         for c, cols in enumerate(pieces):
             nc.scalar.activation(v_low_bf[:, cols], v_low[c][:], ACT.Copy)
 
-        q_bf = sbuf("q_bf", [P, B, NQ * PACK], BF16)
+        q_mx = []
         for b in range(B):
+            q_bf = sbuf("q_bf%d" % b, [P, NQ * PACK], BF16)
             nc.scalar.activation(
-                q_bf[:, b, :].rearrange("p (c i j) -> p c j i", i=4, j=PACK),
+                q_bf[:].rearrange("p (c i j) -> p c j i", i=4, j=PACK),
                 q_raw[b][:].rearrange("p j (c i) -> p c j i", i=4),
                 ACT.Copy,
             )
-        q_codes, q_scale = quantize("q", q_bf[:].rearrange("p b n -> p (b n)"), B * NQ)
+            q_mx.append(quantize("q%d" % b, q_bf[:], NQ))
 
-        low_listed = []
-        for b in range(B):
-            picked = placed("low_listed%d" % b, [P, N], BF16, 2 + b)
-            nc.scalar.activation(picked[:], v_low_bf[:].indirect(listed(b)), ACT.Copy)
-            low_listed.append(picked)
+        low_listed = placed("low_listed", [P, B * N], BF16, 0)
+        nc.scalar.activation(low_listed[:], v_low_bf[:].indirect(offsets[:]), ACT.Copy)
 
         vs_turned = bank(0, "vs_turned", [P, P + B * PACK])
         for lane in reversed(range(B * PACK)):
@@ -124,16 +121,16 @@ def tile_attend_relu2_kernel(tc, qT, k_words, k_scales, vT, vs, offs, out):
             scores = bank(2 + b, "scores%d" % b, [P, N])
             nc.tensor.matmul_mx(
                 out=scores[:],
-                lhsT=q_codes[:, b * NQ : (b + 1) * NQ].bitcast(FP8X4),
-                lhsT_scale=q_scale[:, b * NQ : (b + 1) * NQ],
+                lhsT=q_mx[b][0][:].bitcast(FP8X4),
+                lhsT_scale=q_mx[b][1][:],
                 rhs=k_listed[b][:].bitcast(FP8X4),
                 rhs_scale=k_scale[:, b * N : (b + 1) * N],
                 start=True,
                 stop=True,
             )
             nc.scalar.activation(
-                positive[b][:, 0:N].rearrange("p (t s) -> p t s", t=PACK),
-                scores[:].rearrange("p (s t) -> p t s", t=PACK),
+                positive[b][:, 0:N].rearrange("p (t s) -> p s t", t=PACK),
+                scores[:].rearrange("p (s t) -> p s t", t=PACK),
                 ACT.Relu,
             )
             square = sbuf("square%d" % b, [P, N + 1], F32)
@@ -149,21 +146,38 @@ def tile_attend_relu2_kernel(tc, qT, k_words, k_scales, vT, vs, offs, out):
             nc.vector.tensor_copy(picked[:], v_high[:].indirect(listed(b)))
             high_listed.append(picked)
 
-        v_bf = [sbuf("v_bf%d" % b, [P, DV // P, P * PACK], BF16) for b in range(B)]
+        v_codes = [sbuf("v_codes%d" % b, [P, DV], U32) for b in range(B)]
+        v_scale = [sbuf("v_scale%d" % b, [P, DV], U8) for b in range(B)]
 
-        def turn_values(number, name, picked, target):
-            turned = bank(number, name, [P, 2, P])
+        def turn_words(turned, picked):
             for u in range(2):
-                nc.tensor.transpose(turned[:, u, :], picked[:].bitcast(F32)[:, u : N // 2 : 2], ident[:])
-            nc.scalar.copy(
-                target.bitcast(F32).rearrange("p (e u) -> p e u", u=2), turned[:].rearrange("p u e -> p e u")
-            )
+                nc.tensor.transpose(turned[:, u, :], picked.bitcast(F32)[:, u : N // 2 : 2], ident[:])
 
+        def quantize_values(b, half, values):
+            cols = slice(half * P, (half + 1) * P)
+            nc.vector.quantize_mx(out=v_codes[b][:, cols].bitcast(FP8X4), scales=v_scale[b][:, cols], in_=values)
+
+        low_turned = bank(2, "low_turned", [P, B, 2, P])
         for b in range(B):
-            turn_values(2 + b, "low_turned%d" % b, low_listed[b], v_bf[b][:, 0, :])
-            turn_values(6 + b, "high_turned%d" % b, high_listed[b], v_bf[b][:, 1, :])
+            turn_words(low_turned[:, b, :, :], low_listed[:, b * N : (b + 1) * N])
+        low_bf = placed("low_bf", [P, B * N], BF16, 16)
+        nc.scalar.copy(
+            low_bf[:].bitcast(F32).rearrange("p (b e u) -> p b e u", b=B, u=2),
+            low_turned[:].rearrange("p b u e -> p b e u"),
+        )
 
-        w_bf = [sbuf("w_bf%d" % b, [P, NQ, PACK], BF16) for b in range(B)]
+        def high_values(b, number):
+            turned = bank(number, "high_turned%d" % b, [P, 2, P])
+            turn_words(turned[:], high_listed[b][:])
+            values = placed("high_bf%d" % b, [P, N], BF16, 18 + b)
+            nc.scalar.copy(
+                values[:].bitcast(F32).rearrange("p (e u) -> p e u", u=2), turned[:].rearrange("p u e -> p e u")
+            )
+            return values
+
+        high_bf = [high_values(0, 7)]
+
+        w_bf = [placed("w_bf%d" % b, [P, NQ, PACK], BF16, 8 + b) for b in range(B)]
         inverse = sbuf("inverse", [P, B], F32)
         for b in range(B):
             nc.vector.tensor_tensor(
@@ -173,17 +187,19 @@ def tile_attend_relu2_kernel(tc, qT, k_words, k_scales, vT, vs, offs, out):
                 ALU.mult,
             )
         nc.vector.reciprocal(inverse[:], total[:])
+        high_bf.append(high_values(1, 4))
 
         for b in range(B):
             w_codes, w_scale = quantize("w%d" % b, w_bf[b][:].rearrange("p q t -> p (q t)"), NQ)
-            v_codes, v_scale = quantize("v%d" % b, v_bf[b][:].rearrange("p h n -> p (h n)"), DV)
+            quantize_values(b, 0, low_bf[:, b * N : (b + 1) * N])
+            quantize_values(b, 1, high_bf[b][:])
             sums = bank(b, "sums%d" % b, [P, DV])
             nc.tensor.matmul_mx(
                 out=sums[:],
                 lhsT=w_codes[:].bitcast(FP8X4),
                 lhsT_scale=w_scale[:],
-                rhs=v_codes[:].bitcast(FP8X4),
-                rhs_scale=v_scale[:],
+                rhs=v_codes[b][:].bitcast(FP8X4),
+                rhs_scale=v_scale[b][:],
                 start=True,
                 stop=True,
             )

@@ -33,7 +33,7 @@ def tile_attend_relu2_kernel(tc, qT, k_words, k_scales, vT, vs, offs, out):
             return held.tile(shape, dtype, name=name, align_bytes=64)
 
         def placed(name, shape, dtype, kib):
-            return reused.tile(shape, dtype, name=name, align_bytes=64, offset=kib * 1024)
+            return reused.tile(shape, dtype, name=name, align_bytes=64, offset=int(kib * 1024))
 
         def bank(number, name, shape, dtype=F32):
             return psum.tile(shape, dtype, name=name, tag="bank%d" % number)
@@ -45,7 +45,6 @@ def tile_attend_relu2_kernel(tc, qT, k_words, k_scales, vT, vs, offs, out):
             return codes, scale
 
         offsets = held.tile([P, B * N // 16], U16, name="offsets")
-        nc.sync.dma_start(offsets[:], offs)
 
         def listed(b):
             return offsets[:, b * N // 16 : (b + 1) * N // 16]
@@ -54,11 +53,12 @@ def tile_attend_relu2_kernel(tc, qT, k_words, k_scales, vT, vs, offs, out):
         vs_pool = sbuf("vs_pool", [P, T], F32)
         nc.gpsimd.memset(scale_pool[:].bitcast(I32), 0)
         nc.vector.memset(vs_pool[0:VS_ROW, :], 0.0)
-        nc.sync.dma_start(vs_pool[VS_ROW:P, :], vs[0:1, :])
         pieces = [slice(LOW_CUTS[c], LOW_CUTS[c + 1]) for c in range(len(LOW_CUTS) - 1)]
         v_low = [sbuf("v_low%d" % c, [P, cols.stop - cols.start], F32) for c, cols in enumerate(pieces)]
-        for c in range(2):
-            nc.sync.dma_start(v_low[c][:], vT[0:P, pieces[c]])
+        nc.sync.dma_start(v_low[0][:], vT[0:P, pieces[0]])
+        nc.sync.dma_start(offsets[:], offs)
+        nc.sync.dma_start(vs_pool[VS_ROW:P, :], vs[0:1, :])
+        nc.sync.dma_start(v_low[1][:], vT[0:P, pieces[1]])
         for quad in range(4):
             nc.sync.dma_start(
                 scale_pool[32 * quad : 32 * quad + 4, :].bitcast(I32),
@@ -91,15 +91,18 @@ def tile_attend_relu2_kernel(tc, qT, k_words, k_scales, vT, vs, offs, out):
 
         q_mx = []
         for b in range(B):
-            q_bf = sbuf("q_bf%d" % b, [P, NQ * PACK], BF16)
-            nc.scalar.activation(
-                q_bf[:].rearrange("p (c i j) -> p c j i", i=4, j=PACK),
-                q_raw[b][:].rearrange("p j (c i) -> p c j i", i=4),
-                ACT.Copy,
+            q_bf = placed("q_bf%d" % b, [P, NQ * PACK], BF16, 24 + 4 * b)
+            nc.gpsimd.tensor_scalar(
+                q_bf[:].rearrange("p (n j) -> p n j", j=PACK),
+                q_raw[b][:].rearrange("p j n -> p n j"),
+                1.0,
+                0.0,
+                ALU.mult,
+                ALU.add,
             )
             q_mx.append(quantize("q%d" % b, q_bf[:], NQ))
 
-        low_listed = placed("low_listed", [P, B * N], BF16, 0)
+        low_listed = sbuf("low_listed", [P, B * N], BF16)
         nc.scalar.activation(low_listed[:], v_low_bf[:].indirect(offsets[:]), ACT.Copy)
 
         vs_turned = bank(0, "vs_turned", [P, P + B * PACK])
@@ -146,7 +149,7 @@ def tile_attend_relu2_kernel(tc, qT, k_words, k_scales, vT, vs, offs, out):
             nc.vector.tensor_copy(picked[:], v_high[:].indirect(listed(b)))
             high_listed.append(picked)
 
-        v_codes = [sbuf("v_codes%d" % b, [P, DV], U32) for b in range(B)]
+        v_codes = [placed("v_codes%d" % b, [P, DV], U32, 27.5 + b) for b in range(B)]
         v_scale = [sbuf("v_scale%d" % b, [P, DV], U8) for b in range(B)]
 
         def turn_words(turned, picked):
@@ -157,10 +160,10 @@ def tile_attend_relu2_kernel(tc, qT, k_words, k_scales, vT, vs, offs, out):
             cols = slice(half * P, (half + 1) * P)
             nc.vector.quantize_mx(out=v_codes[b][:, cols].bitcast(FP8X4), scales=v_scale[b][:, cols], in_=values)
 
-        low_turned = bank(2, "low_turned", [P, B, 2, P])
+        low_turned = bank(6, "low_turned", [P, B, 2, P])
         for b in range(B):
             turn_words(low_turned[:, b, :, :], low_listed[:, b * N : (b + 1) * N])
-        low_bf = placed("low_bf", [P, B * N], BF16, 16)
+        low_bf = sbuf("low_bf", [P, B * N], BF16)
         nc.scalar.copy(
             low_bf[:].bitcast(F32).rearrange("p (b e u) -> p b e u", b=B, u=2),
             low_turned[:].rearrange("p b u e -> p b e u"),
@@ -187,22 +190,28 @@ def tile_attend_relu2_kernel(tc, qT, k_words, k_scales, vT, vs, offs, out):
                 ALU.mult,
             )
         nc.vector.reciprocal(inverse[:], total[:])
-        high_bf.append(high_values(1, 4))
+        high_bf.append(high_values(1, 3))
 
         for b in range(B):
             w_codes, w_scale = quantize("w%d" % b, w_bf[b][:].rearrange("p q t -> p (q t)"), NQ)
             quantize_values(b, 0, low_bf[:, b * N : (b + 1) * N])
             quantize_values(b, 1, high_bf[b][:])
-            sums = bank(b, "sums%d" % b, [P, DV])
-            nc.tensor.matmul_mx(
-                out=sums[:],
-                lhsT=w_codes[:].bitcast(FP8X4),
-                lhsT_scale=w_scale[:],
-                rhs=v_codes[b][:].bitcast(FP8X4),
-                rhs_scale=v_scale[b][:],
-                start=True,
-                stop=True,
-            )
-            result = sbuf("result%d" % b, [P, DV], F32)
-            nc.scalar.activation(result[:], sums[:], ACT.Copy, scale=inverse[:, b : b + 1])
-            nc.sync.dma_start(out[b], result[:])
+            parts = [(slice(0, DV), 0)] if b == 0 else [(slice(0, P), 1), (slice(P, DV), 6)]
+            for cols, number in parts:
+                width = cols.stop - cols.start
+                sums = bank(number, "sums%d" % number, [P, width])
+                nc.tensor.matmul_mx(
+                    out=sums[:],
+                    lhsT=w_codes[:].bitcast(FP8X4),
+                    lhsT_scale=w_scale[:],
+                    rhs=v_codes[b][:, cols].bitcast(FP8X4),
+                    rhs_scale=v_scale[b][:, cols],
+                    start=True,
+                    stop=True,
+                )
+                result = sbuf("result%d" % number, [P, width], F32)
+                if b == 0:
+                    nc.scalar.activation(result[:], sums[:], ACT.Copy, scale=inverse[:, b : b + 1])
+                else:
+                    nc.vector.tensor_scalar_mul(result[:], sums[:], inverse[:, b : b + 1])
+                nc.sync.dma_start(out[b, :, cols], result[:])

@@ -55,10 +55,10 @@ def tile_attend_relu2_kernel(tc, qT, k_words, k_scales, vT, vs, offs, out):
         nc.vector.memset(vs_pool[0:VS_ROW, :], 0.0)
         pieces = [slice(LOW_CUTS[c], LOW_CUTS[c + 1]) for c in range(len(LOW_CUTS) - 1)]
         v_low = [sbuf("v_low%d" % c, [P, cols.stop - cols.start], F32) for c, cols in enumerate(pieces)]
-        nc.sync.dma_start(v_low[0][:], vT[0:P, pieces[0]])
         nc.sync.dma_start(offsets[:], offs)
-        nc.sync.dma_start(vs_pool[VS_ROW:P, :], vs[0:1, :])
-        nc.sync.dma_start(v_low[1][:], vT[0:P, pieces[1]])
+        nc.scalar.dma_start(vs_pool[VS_ROW:P, :], vs[0:1, :])
+        for c in range(2):
+            nc.sync.dma_start(v_low[c][:], vT[0:P, pieces[c]])
         for quad in range(4):
             nc.sync.dma_start(
                 scale_pool[32 * quad : 32 * quad + 4, :].bitcast(I32),
@@ -76,9 +76,9 @@ def tile_attend_relu2_kernel(tc, qT, k_words, k_scales, vT, vs, offs, out):
 
         ident = sbuf("ident", [P, P], F32)
         make_identity(nc, ident[:])
-        positive = [sbuf("positive0", [P, N + 1], F32), placed("positive1", [P, N + 1], F32, 17)]
+        positive = [sbuf("positive0", [P, 2, P + 1, 2], F32), placed("positive1", [P, 2, P + 1, 2], F32, 17)]
         for b in range(B):
-            nc.gpsimd.memset(positive[b][:, N : N + 1], 1.0)
+            nc.gpsimd.memset(positive[b][:, :, P, :], 0.5)
 
         vs_listed = sbuf("vs_listed", [P, B * N], F32)
         nc.vector.tensor_copy(vs_listed[:], vs_pool[:].indirect(offsets[:]))
@@ -132,15 +132,20 @@ def tile_attend_relu2_kernel(tc, qT, k_words, k_scales, vT, vs, offs, out):
                 stop=True,
             )
             nc.scalar.activation(
-                positive[b][:, 0:N].rearrange("p (t s) -> p s t", t=PACK),
-                scores[:].rearrange("p (s t) -> p s t", t=PACK),
+                positive[b][:, :, 0:P, :].rearrange("p u s e -> p s u e"),
+                scores[:].rearrange("p (s u e) -> p s u e", u=2, e=2),
                 ACT.Relu,
             )
-            square = sbuf("square%d" % b, [P, N + 1], F32)
-            nc.scalar.activation(square[:], positive[b][:], ACT.Square, accum_out=total[:, b : b + 1])
+            square = sbuf("square%d" % b, [P, 2, 2, P + 4], F32)
+            nc.scalar.activation(
+                square[:, :, :, 0 : P + 1],
+                positive[b][:].rearrange("p u s e -> p u e s"),
+                ACT.Square,
+                accum_out=total[:, b : b + 1],
+            )
             turned = bank(4 + b, "p_turned%d" % b, [P, PACK, NQ])
             for t in range(PACK):
-                nc.tensor.transpose(turned[:, t, :], square[:, t * P : (t + 1) * P], ident[:])
+                nc.tensor.transpose(turned[:, t, :], square[:, t // 2, t % 2, 0:P], ident[:])
             p_turned.append(turned)
 
         high_listed = []
@@ -165,8 +170,8 @@ def tile_attend_relu2_kernel(tc, qT, k_words, k_scales, vT, vs, offs, out):
             turn_words(low_turned[:, b, :, :], low_listed[:, b * N : (b + 1) * N])
         low_bf = sbuf("low_bf", [P, B * N], BF16)
         nc.scalar.copy(
-            low_bf[:].bitcast(F32).rearrange("p (b e u) -> p b e u", b=B, u=2),
-            low_turned[:].rearrange("p b u e -> p b e u"),
+            low_bf[:].bitcast(F32).rearrange("p (b c i u) -> p b c u i", b=B, i=2, u=2),
+            low_turned[:].rearrange("p b u (c i) -> p b c u i", i=2),
         )
 
         def high_values(b, number):
@@ -174,7 +179,8 @@ def tile_attend_relu2_kernel(tc, qT, k_words, k_scales, vT, vs, offs, out):
             turn_words(turned[:], high_listed[b][:])
             values = placed("high_bf%d" % b, [P, N], BF16, 18 + b)
             nc.scalar.copy(
-                values[:].bitcast(F32).rearrange("p (e u) -> p e u", u=2), turned[:].rearrange("p u e -> p e u")
+                values[:].bitcast(F32).rearrange("p (c i u) -> p c u i", i=2, u=2),
+                turned[:].rearrange("p u (c i) -> p c u i", i=2),
             )
             return values
 
@@ -184,9 +190,9 @@ def tile_attend_relu2_kernel(tc, qT, k_words, k_scales, vT, vs, offs, out):
         inverse = sbuf("inverse", [P, B], F32)
         for b in range(B):
             nc.vector.tensor_tensor(
-                w_bf[b][:],
-                p_turned[b][:].rearrange("p t q -> p q t"),
-                vs_slot[:, b : b + 1, :].to_broadcast([P, NQ, PACK]),
+                w_bf[b][:].rearrange("p (c i) t -> p c t i", i=2),
+                p_turned[b][:].rearrange("p t (c i) -> p c t i", i=2),
+                vs_slot[:, b : b + 1, :].unsqueeze(3).to_broadcast([P, NQ // 2, PACK, 2]),
                 ALU.mult,
             )
         nc.vector.reciprocal(inverse[:], total[:])

@@ -92,13 +92,9 @@ def tile_attend_relu2_kernel(tc, qT, k_words, k_scales, vT, vs, offs, out):
         q_mx = []
         for b in range(B):
             q_bf = placed("q_bf%d" % b, [P, NQ * PACK], BF16, 24 + 4 * b)
-            nc.gpsimd.tensor_scalar(
-                q_bf[:].rearrange("p (n j) -> p n j", j=PACK),
-                q_raw[b][:].rearrange("p j n -> p n j"),
-                1.0,
-                0.0,
-                ALU.mult,
-                ALU.add,
+            nc.vector.tensor_copy(
+                q_bf[:].rearrange("p (c i j) -> p c j i", i=4, j=PACK),
+                q_raw[b][:].rearrange("p j (c i) -> p c j i", i=4),
             )
             q_mx.append(quantize("q%d" % b, q_bf[:], NQ))
 

@@ -9,7 +9,8 @@ FLOPS = 2 * B * NQ * N * (D + DV)
 P = 128
 PACK = 4
 VS_ROW = P - 1
-LOW_CUTS = (0, 512, 1408, T)
+LOW_CUTS = (0, 512, 768, 1536, T)
+OVER = {"positive0":["q_raw1",-1024],"vs_listed1":["q_raw1",1024],"vs_slot1":["v_low2",0],"plus_one":["v_low2",64],"high_bf0":["v_low2",128],"w_bf0":["v_low2",1152],"w0_codes":["v_low3",0],"w_bf1":["v_low3",512],"high_bf1":["v_low3",1536],"vs_slot0":["positive0",0]}
 
 F32 = mybir.dt.float32
 BF16 = mybir.dt.bfloat16
@@ -20,20 +21,27 @@ U8 = mybir.dt.uint8
 FP8X4 = mybir.dt.float8_e4m3fn_x4
 ACT = mybir.ActivationFunctionType
 ALU = mybir.AluOpType
+WIDTH = {F32: 4, BF16: 2, U32: 4, U8: 1}
 
 
 def tile_attend_relu2_kernel(tc, qT, k_words, k_scales, vT, vs, offs, out):
     nc = tc.nc
     with ExitStack() as ctx:
         held = ctx.enter_context(tc.tile_pool(name="held", bufs=1))
-        reused = ctx.enter_context(tc.tile_pool(name="reused", bufs=1))
+        work = ctx.enter_context(tc.tile_pool(name="work", bufs=1))
         psum = ctx.enter_context(tc.psum_pool(name="psum", bufs=1))
+        places = {"end": 0}
 
         def sbuf(name, shape, dtype):
-            return held.tile(shape, dtype, name=name, align_bytes=64)
-
-        def placed(name, shape, dtype, kib):
-            return reused.tile(shape, dtype, name=name, align_bytes=64, offset=int(kib * 1024))
+            size = WIDTH[dtype]
+            for extent in shape[1:]:
+                size = size * extent
+            if name in OVER:
+                places[name] = places[OVER[name][0]] + OVER[name][1]
+            else:
+                places[name] = places["end"]
+                places["end"] = places["end"] + (size + 63) // 64 * 64
+            return work.tile(shape, dtype, name=name, align_bytes=64, offset=places[name])
 
         def bank(number, name, shape, dtype=F32):
             return psum.tile(shape, dtype, name=name, tag="bank%d" % number)
@@ -52,168 +60,246 @@ def tile_attend_relu2_kernel(tc, qT, k_words, k_scales, vT, vs, offs, out):
         scale_pool = sbuf("scale_pool", [P, T], U8)
         vs_pool = sbuf("vs_pool", [P, T], F32)
         nc.gpsimd.memset(scale_pool[:].bitcast(I32), 0)
-        nc.vector.memset(vs_pool[0:VS_ROW, :], 0.0)
+        nc.vector.memset(vs_pool[0:VS_ROW, 0 : T // 2], 0.0)
+        nc.gpsimd.memset(vs_pool[0:VS_ROW, T // 2 : T], 0.0)
         pieces = [slice(LOW_CUTS[c], LOW_CUTS[c + 1]) for c in range(len(LOW_CUTS) - 1)]
         v_low = [sbuf("v_low%d" % c, [P, cols.stop - cols.start], F32) for c, cols in enumerate(pieces)]
-        nc.sync.dma_start(offsets[:], offs)
-        nc.scalar.dma_start(vs_pool[VS_ROW:P, :], vs[0:1, :])
-        for c in range(2):
-            nc.sync.dma_start(v_low[c][:], vT[0:P, pieces[c]])
-        for quad in range(4):
-            nc.sync.dma_start(
+        q_raw = [sbuf("q_raw%d" % b, [P, PACK, NQ], F32) for b in range(B)]
+        word_pool = sbuf("word_pool", [P, T], U32)
+        v_high = sbuf("v_high", [P, T], F32)
+
+        def load_scales(queue, quad):
+            queue.dma_start(
                 scale_pool[32 * quad : 32 * quad + 4, :].bitcast(I32),
                 k_scales[0, 4 * quad : 4 * quad + 4, :].bitcast(I32),
             )
-        for c in range(2, len(pieces)):
+
+        def load_queries(b):
+            nc.sync.dma_start(q_raw[b][:], qT[b].rearrange("(p j) n -> p j n", j=PACK))
+
+        def load_words():
+            nc.sync.dma_start(word_pool[:].bitcast(I32), k_words[0].rearrange("p t r -> p (t r)").bitcast(I32))
+
+        def load_low(c):
             nc.sync.dma_start(v_low[c][:], vT[0:P, pieces[c]])
-        q_raw = [placed("q_raw%d" % b, [P, PACK, NQ], F32, 2 * b) for b in range(B)]
-        nc.sync.dma_start(q_raw[0][:], qT[0].rearrange("(p j) n -> p j n", j=PACK))
-        word_pool = sbuf("word_pool", [P, T], U32)
-        nc.sync.dma_start(word_pool[:].bitcast(I32), k_words[0].rearrange("p t r -> p (t r)").bitcast(I32))
-        nc.sync.dma_start(q_raw[1][:], qT[1].rearrange("(p j) n -> p j n", j=PACK))
-        v_high = placed("v_high", [P, T], F32, 8)
-        nc.sync.dma_start(v_high[:], vT[P:DV, :])
+
+        def load_high():
+            nc.sync.dma_start(v_high[:], vT[P:DV, :])
+
+        nc.sync.dma_start(offsets[:], offs)
+        nc.scalar.dma_start(vs_pool[VS_ROW:P, :], vs[0:1, :])
+        load_queries(0)
+        for quad in range(4):
+            load_scales(nc.sync, quad)
+        load_words()
+        load_low(0)
+        load_queries(1)
+        load_low(1)
+        load_high()
+        load_low(2)
+        load_low(3)
 
         ident = sbuf("ident", [P, P], F32)
         make_identity(nc, ident[:])
-        positive = [sbuf("positive0", [P, 2, P + 1, 2], F32), placed("positive1", [P, 2, P + 1, 2], F32, 17)]
+        total = sbuf("total", [P, B], F32)
+        inverse = sbuf("inverse", [P, B], F32)
+        got = {}
+
+        def gather_vs(b):
+            got["vs_listed", b] = sbuf("vs_listed%d" % b, [P, N], F32)
+            nc.vector.tensor_copy(got["vs_listed", b][:], vs_pool[:].indirect(listed(b)))
+
+        def gather_scales():
+            got["k_scale"] = sbuf("k_scale", [P, B * N], U8)
+            nc.vector.tensor_copy(got["k_scale"][:], scale_pool[:].indirect(offsets[:]))
+
+        v_low_bf = sbuf("v_low_bf", [P, T], BF16)
+
+        def cast_low(c, first, last):
+            start = pieces[c].start
+            nc.scalar.activation(v_low_bf[:, start + first : start + last], v_low[c][:, first:last], ACT.Copy)
+
+        low_listed = [sbuf("low_listed%d" % b, [P, N], BF16) for b in range(B)]
         for b in range(B):
-            nc.gpsimd.memset(positive[b][:, :, P, :], 0.5)
+            got["low_listed", b] = low_listed[b]
 
-        vs_listed = sbuf("vs_listed", [P, B * N], F32)
-        nc.vector.tensor_copy(vs_listed[:], vs_pool[:].indirect(offsets[:]))
-        k_scale = sbuf("k_scale", [P, B * N], U8)
-        nc.vector.tensor_copy(k_scale[:], scale_pool[:].indirect(offsets[:]))
+        def gather_low(b, first, last, on_scalar):
+            window = v_low_bf[:].indirect(offsets[:, (b * N + first) // 16 : (b * N + last) // 16])
+            if on_scalar:
+                nc.scalar.activation(low_listed[b][:, first:last], window, ACT.Copy)
+            else:
+                nc.vector.tensor_copy(low_listed[b][:, first:last], window)
 
-        v_low_bf = placed("v_low_bf", [P, T], BF16, 4)
-        for c, cols in enumerate(pieces):
-            nc.scalar.activation(v_low_bf[:, cols], v_low[c][:], ACT.Copy)
+        def turn_vs(b, number, copy):
+            turned = bank(number, "vs_turned%d" % b, [P, P + PACK])
+            for t in reversed(range(PACK)):
+                nc.tensor.transpose(turned[:, t : t + P], got["vs_listed", b][:, t:N:PACK], ident[:])
+            got["vs_slot", b] = sbuf("vs_slot%d" % b, [P, 1, PACK], F32)
+            copy(got["vs_slot", b][:, 0, :], turned[:, VS_ROW : VS_ROW + PACK])
 
-        q_mx = []
-        for b in range(B):
-            q_bf = placed("q_bf%d" % b, [P, NQ * PACK], BF16, 24 + 4 * b)
-            nc.vector.tensor_copy(
-                q_bf[:].rearrange("p (c i j) -> p c j i", i=4, j=PACK),
+        def gather_keys(b):
+            got["k", b] = sbuf("k_listed%d" % b, [P, N], U32)
+            nc.vector.tensor_copy(got["k", b][:], word_pool[:].indirect(listed(b)))
+
+        def act_copy(to, source):
+            nc.scalar.activation(to, source, ACT.Copy)
+
+        def weave_queries(b, copy):
+            got["q_bf", b] = sbuf("q_bf%d" % b, [P, NQ * PACK], BF16)
+            copy(
+                got["q_bf", b][:].rearrange("p (c i j) -> p c j i", i=4, j=PACK),
                 q_raw[b][:].rearrange("p j (c i) -> p c j i", i=4),
             )
-            q_mx.append(quantize("q%d" % b, q_bf[:], NQ))
 
-        low_listed = sbuf("low_listed", [P, B * N], BF16)
-        nc.scalar.activation(low_listed[:], v_low_bf[:].indirect(offsets[:]), ACT.Copy)
+        def quantize_queries(b):
+            got["q", b] = quantize("q%d" % b, got["q_bf", b][:], NQ)
 
-        vs_turned = bank(0, "vs_turned", [P, P + B * PACK])
-        for lane in reversed(range(B * PACK)):
-            b, t = divmod(lane, PACK)
-            nc.tensor.transpose(vs_turned[:, lane : lane + P], vs_listed[:, b * N + t : (b + 1) * N : PACK], ident[:])
-        vs_slot = placed("vs_slot", [P, B, PACK], F32, 4)
-        nc.scalar.copy(vs_slot[:].rearrange("p b t -> p (b t)"), vs_turned[:, VS_ROW : VS_ROW + B * PACK])
-
-        k_listed = []
-        for b in range(B):
-            picked = sbuf("k_listed%d" % b, [P, N], U32)
-            nc.vector.tensor_copy(picked[:], word_pool[:].indirect(listed(b)))
-            k_listed.append(picked)
-
-        total = sbuf("total", [P, B], F32)
-        p_turned = []
-        for b in range(B):
-            scores = bank(2 + b, "scores%d" % b, [P, N])
+        def score(b, number):
+            got["scores", b] = bank(number, "scores%d" % b, [P, N])
             nc.tensor.matmul_mx(
-                out=scores[:],
-                lhsT=q_mx[b][0][:].bitcast(FP8X4),
-                lhsT_scale=q_mx[b][1][:],
-                rhs=k_listed[b][:].bitcast(FP8X4),
-                rhs_scale=k_scale[:, b * N : (b + 1) * N],
+                out=got["scores", b][:],
+                lhsT=got["q", b][0][:].bitcast(FP8X4),
+                lhsT_scale=got["q", b][1][:],
+                rhs=got["k", b][:].bitcast(FP8X4),
+                rhs_scale=got["k_scale"][:, b * N : (b + 1) * N],
                 start=True,
                 stop=True,
             )
+
+        def relu(b):
+            got["positive", b] = sbuf("positive%d" % b, [P, 2, P, 2], F32)
             nc.scalar.activation(
-                positive[b][:, :, 0:P, :].rearrange("p u s e -> p s u e"),
-                scores[:].rearrange("p (s u e) -> p s u e", u=2, e=2),
+                got["positive", b][:].rearrange("p u s e -> p s u e"),
+                got["scores", b][:].rearrange("p (s u e) -> p s u e", u=2, e=2),
                 ACT.Relu,
             )
-            square = sbuf("square%d" % b, [P, 2, 2, P + 4], F32)
+
+        def square(b):
+            got["p", b] = sbuf("square%d" % b, [P, 2, 2, P], F32)
             nc.scalar.activation(
-                square[:, :, :, 0 : P + 1],
-                positive[b][:].rearrange("p u s e -> p u e s"),
+                got["p", b][:],
+                got["positive", b][:].rearrange("p u s e -> p u e s"),
                 ACT.Square,
                 accum_out=total[:, b : b + 1],
             )
-            turned = bank(4 + b, "p_turned%d" % b, [P, PACK, NQ])
+
+        def turn_squares(b, number):
+            got["p_turned", b] = bank(number, "p_turned%d" % b, [P, PACK, NQ])
             for t in range(PACK):
-                nc.tensor.transpose(turned[:, t, :], square[:, t // 2, t % 2, 0:P], ident[:])
-            p_turned.append(turned)
+                nc.tensor.transpose(got["p_turned", b][:, t, :], got["p", b][:, t // 2, t % 2, 0:P], ident[:])
 
-        high_listed = []
-        for b in range(B):
-            picked = sbuf("high_listed%d" % b, [P, N], BF16)
-            nc.vector.tensor_copy(picked[:], v_high[:].indirect(listed(b)))
-            high_listed.append(picked)
+        def gather_high(b):
+            got["high_listed", b] = sbuf("high_listed%d" % b, [P, N], BF16)
+            nc.vector.tensor_copy(got["high_listed", b][:], v_high[:].indirect(listed(b)))
 
-        v_codes = [placed("v_codes%d" % b, [P, DV], U32, 27.5 + b) for b in range(B)]
-        v_scale = [sbuf("v_scale%d" % b, [P, DV], U8) for b in range(B)]
-
-        def turn_words(turned, picked):
+        def turn_values(half, b, number):
+            got[half + "_turned", b] = bank(number, "%s_turned%d" % (half, b), [P, 2, P])
             for u in range(2):
-                nc.tensor.transpose(turned[:, u, :], picked.bitcast(F32)[:, u : N // 2 : 2], ident[:])
+                nc.tensor.transpose(
+                    got[half + "_turned", b][:, u, :], got[half + "_listed", b][:].bitcast(F32)[:, u : N // 2 : 2], ident[:]
+                )
 
-        def quantize_values(b, half, values):
-            cols = slice(half * P, (half + 1) * P)
-            nc.vector.quantize_mx(out=v_codes[b][:, cols].bitcast(FP8X4), scales=v_scale[b][:, cols], in_=values)
-
-        low_turned = bank(6, "low_turned", [P, B, 2, P])
-        for b in range(B):
-            turn_words(low_turned[:, b, :, :], low_listed[:, b * N : (b + 1) * N])
-        low_bf = sbuf("low_bf", [P, B * N], BF16)
-        nc.scalar.copy(
-            low_bf[:].bitcast(F32).rearrange("p (b c i u) -> p b c u i", b=B, i=2, u=2),
-            low_turned[:].rearrange("p b u (c i) -> p b c u i", i=2),
-        )
-
-        def high_values(b, number):
-            turned = bank(number, "high_turned%d" % b, [P, 2, P])
-            turn_words(turned[:], high_listed[b][:])
-            values = placed("high_bf%d" % b, [P, N], BF16, 18 + b)
-            nc.scalar.copy(
-                values[:].bitcast(F32).rearrange("p (c i u) -> p c u i", i=2, u=2),
-                turned[:].rearrange("p u (c i) -> p c u i", i=2),
+        def copy_values(half, b, copy):
+            got[half + "_bf", b] = sbuf("%s_bf%d" % (half, b), [P, N], BF16)
+            copy(
+                got[half + "_bf", b][:].bitcast(F32).rearrange("p (c i u) -> p c u i", i=2, u=2),
+                got[half + "_turned", b][:].rearrange("p u (c i) -> p c u i", i=2),
             )
-            return values
 
-        high_bf = [high_values(0, 7)]
+        def quantize_values(half, b):
+            got[half, b] = quantize("%s%d" % (half, b), got[half + "_bf", b][:], P)
 
-        w_bf = [placed("w_bf%d" % b, [P, NQ, PACK], BF16, 8 + b) for b in range(B)]
-        inverse = sbuf("inverse", [P, B], F32)
-        for b in range(B):
+        def weigh(b):
+            got["w_bf", b] = sbuf("w_bf%d" % b, [P, NQ, PACK], BF16)
             nc.vector.tensor_tensor(
-                w_bf[b][:].rearrange("p (c i) t -> p c t i", i=2),
-                p_turned[b][:].rearrange("p t (c i) -> p c t i", i=2),
-                vs_slot[:, b : b + 1, :].unsqueeze(3).to_broadcast([P, NQ // 2, PACK, 2]),
+                got["w_bf", b][:].rearrange("p (c i) t -> p c t i", i=2),
+                got["p_turned", b][:].rearrange("p t (c i) -> p c t i", i=2),
+                got["vs_slot", b][:].unsqueeze(3).to_broadcast([P, NQ // 2, PACK, 2]),
                 ALU.mult,
             )
-        nc.vector.reciprocal(inverse[:], total[:])
-        high_bf.append(high_values(1, 3))
 
-        for b in range(B):
-            w_codes, w_scale = quantize("w%d" % b, w_bf[b][:].rearrange("p q t -> p (q t)"), NQ)
-            quantize_values(b, 0, low_bf[:, b * N : (b + 1) * N])
-            quantize_values(b, 1, high_bf[b][:])
-            parts = [(slice(0, DV), 0)] if b == 0 else [(slice(0, P), 1), (slice(P, DV), 6)]
-            for cols, number in parts:
-                width = cols.stop - cols.start
-                sums = bank(number, "sums%d" % number, [P, width])
-                nc.tensor.matmul_mx(
-                    out=sums[:],
-                    lhsT=w_codes[:].bitcast(FP8X4),
-                    lhsT_scale=w_scale[:],
-                    rhs=v_codes[b][:, cols].bitcast(FP8X4),
-                    rhs_scale=v_scale[b][:, cols],
-                    start=True,
-                    stop=True,
-                )
-                result = sbuf("result%d" % number, [P, width], F32)
-                if b == 0:
-                    nc.scalar.activation(result[:], sums[:], ACT.Copy, scale=inverse[:, b : b + 1])
-                else:
-                    nc.vector.tensor_scalar_mul(result[:], sums[:], inverse[:, b : b + 1])
-                nc.sync.dma_start(out[b, :, cols], result[:])
+        def quantize_weights(b):
+            got["w", b] = quantize("w%d" % b, got["w_bf", b][:].rearrange("p q t -> p (q t)"), NQ)
+
+        def add_one():
+            got["plus_one"] = sbuf("plus_one", [P, B], F32)
+            nc.scalar.activation(got["plus_one"][:], total[:], ACT.Identity, bias=1.0)
+
+        def invert():
+            nc.vector.reciprocal(inverse[:], got["plus_one"][:])
+
+        def multiply(b, half, sums):
+            codes, scale = got[half, b]
+            nc.tensor.matmul_mx(
+                out=sums,
+                lhsT=got["w", b][0][:].bitcast(FP8X4),
+                lhsT_scale=got["w", b][1][:],
+                rhs=codes[:].bitcast(FP8X4),
+                rhs_scale=scale[:],
+                start=True,
+                stop=True,
+            )
+
+        def finish(b, cols, sums, on_scalar, queue):
+            result = sbuf("result%d_%d" % (b, cols.start), [P, cols.stop - cols.start], F32)
+            if on_scalar:
+                nc.scalar.activation(result[:], sums, ACT.Copy, scale=inverse[:, b : b + 1])
+            else:
+                nc.vector.tensor_scalar_mul(result[:], sums, inverse[:, b : b + 1])
+            queue.dma_start(out[b, :, cols], result[:])
+
+        gather_vs(0)
+        weave_queries(0, act_copy)
+        quantize_queries(0)
+        gather_scales()
+        gather_keys(0)
+        gather_keys(1)
+        cast_low(0, 0, LOW_CUTS[1])
+        weave_queries(1, nc.scalar.copy)
+        quantize_queries(1)
+        score(0, 0)
+        score(1, 1)
+        gather_vs(1)
+        relu(0)
+        square(0)
+        turn_vs(0, 5, nc.scalar.copy)
+        turn_squares(0, 2)
+        relu(1)
+        square(1)
+        cast_low(1, 0, LOW_CUTS[2] - LOW_CUTS[1])
+        gather_high(0)
+        gather_high(1)
+        cast_low(2, 0, LOW_CUTS[3] - LOW_CUTS[2])
+        cast_low(3, 0, LOW_CUTS[4] - LOW_CUTS[3])
+        turn_vs(1, 1, nc.scalar.copy)
+        turn_squares(1, 3)
+        gather_low(0, 0, N, True)
+        weigh(0)
+        gather_low(1, 0, N, False)
+        weigh(1)
+        add_one()
+        turn_values("high", 0, 7)
+        copy_values("high", 0, nc.scalar.copy)
+        turn_values("high", 1, 6)
+        copy_values("high", 1, nc.scalar.copy)
+        turn_values("low", 0, 4)
+        copy_values("low", 0, nc.scalar.copy)
+        turn_values("low", 1, 6)
+        copy_values("low", 1, nc.scalar.copy)
+        quantize_weights(0)
+        quantize_values("high", 0)
+        invert()
+        quantize_weights(1)
+        quantize_values("high", 1)
+        quantize_values("low", 0)
+        quantize_values("low", 1)
+        sums0 = bank(4, "sums0", [P, DV])
+        multiply(0, "high", sums0[:, P:DV])
+        sums1 = bank(1, "sums1", [P, P])
+        multiply(1, "high", sums1[:])
+        multiply(0, "low", sums0[:, 0:P])
+        sums2 = bank(2, "sums2", [P, P])
+        multiply(1, "low", sums2[:])
+        finish(1, slice(P, DV), sums1[:], True, nc.sync)
+        finish(0, slice(0, DV), sums0[:], True, nc.sync)
+        finish(1, slice(0, P), sums2[:], False, nc.sync)

@@ -9,8 +9,9 @@ FLOPS = 2 * B * NQ * N * (D + DV)
 P = 128
 PACK = 4
 VS_ROW = P - 1
-LOW_CUTS = (0, 512, 768, 1536, T)
-OVER = {"positive0":["q_raw1",-1024],"vs_listed1":["q_raw1",1024],"vs_slot1":["v_low2",0],"plus_one":["v_low2",64],"high_bf0":["v_low2",128],"w_bf0":["v_low2",1152],"w0_codes":["v_low3",0],"w_bf1":["v_low3",512],"high_bf1":["v_low3",1536],"vs_slot0":["positive0",0]}
+LOW_CUTS = (0, T)
+PAD = {"q_raw1":1024,"high_listed0":1024}
+OVER = {"positive0":["q_raw1",-1024],"vs_listed1":["q_raw1",1024],"vs_slot0":["positive0",0],"w_bf1":["high_listed0",-960],"w0_scale":["high_listed0",64],"low0_scale":["high_listed0",192],"low1_scale":["high_listed0",320],"inverse":["high_listed0",448]}
 
 F32 = mybir.dt.float32
 BF16 = mybir.dt.bfloat16
@@ -39,8 +40,8 @@ def tile_attend_relu2_kernel(tc, qT, k_words, k_scales, vT, vs, offs, out):
             if name in OVER:
                 places[name] = places[OVER[name][0]] + OVER[name][1]
             else:
-                places[name] = places["end"]
-                places["end"] = places["end"] + (size + 63) // 64 * 64
+                places[name] = places["end"] + PAD.get(name, 0)
+                places["end"] = places[name] + (size + 63) // 64 * 64
             return work.tile(shape, dtype, name=name, align_bytes=64, offset=places[name])
 
         def bank(number, name, shape, dtype=F32):
@@ -60,8 +61,7 @@ def tile_attend_relu2_kernel(tc, qT, k_words, k_scales, vT, vs, offs, out):
         scale_pool = sbuf("scale_pool", [P, T], U8)
         vs_pool = sbuf("vs_pool", [P, T], F32)
         nc.gpsimd.memset(scale_pool[:].bitcast(I32), 0)
-        nc.vector.memset(vs_pool[0:VS_ROW, 0 : T // 2], 0.0)
-        nc.gpsimd.memset(vs_pool[0:VS_ROW, T // 2 : T], 0.0)
+        nc.vector.memset(vs_pool[0:VS_ROW, :], 0.0)
         pieces = [slice(LOW_CUTS[c], LOW_CUTS[c + 1]) for c in range(len(LOW_CUTS) - 1)]
         v_low = [sbuf("v_low%d" % c, [P, cols.stop - cols.start], F32) for c, cols in enumerate(pieces)]
         q_raw = [sbuf("q_raw%d" % b, [P, PACK, NQ], F32) for b in range(B)]
@@ -77,8 +77,9 @@ def tile_attend_relu2_kernel(tc, qT, k_words, k_scales, vT, vs, offs, out):
         def load_queries(b):
             nc.sync.dma_start(q_raw[b][:], qT[b].rearrange("(p j) n -> p j n", j=PACK))
 
-        def load_words():
-            nc.sync.dma_start(word_pool[:].bitcast(I32), k_words[0].rearrange("p t r -> p (t r)").bitcast(I32))
+        def load_words(queue, first, last):
+            words = k_words[0].rearrange("p t r -> p (t r)").bitcast(I32)
+            queue.dma_start(word_pool[:, first:last].bitcast(I32), words[:, first:last])
 
         def load_low(c):
             nc.sync.dma_start(v_low[c][:], vT[0:P, pieces[c]])
@@ -91,29 +92,27 @@ def tile_attend_relu2_kernel(tc, qT, k_words, k_scales, vT, vs, offs, out):
         load_queries(0)
         for quad in range(4):
             load_scales(nc.sync, quad)
-        load_words()
-        load_low(0)
+        load_words(nc.sync, 0, T)
         load_queries(1)
-        load_low(1)
+        load_low(0)
         load_high()
-        load_low(2)
-        load_low(3)
 
         ident = sbuf("ident", [P, P], F32)
         make_identity(nc, ident[:])
         total = sbuf("total", [P, B], F32)
-        inverse = sbuf("inverse", [P, B], F32)
         got = {}
 
-        def gather_vs(b):
-            got["vs_listed", b] = sbuf("vs_listed%d" % b, [P, N], F32)
-            nc.vector.tensor_copy(got["vs_listed", b][:], vs_pool[:].indirect(listed(b)))
+        def gather_vs(b, first, last):
+            if first == 0:
+                got["vs_listed", b] = sbuf("vs_listed%d" % b, [P, N], F32)
+            window = vs_pool[:].indirect(offsets[:, (b * N + first) // 16 : (b * N + last) // 16])
+            nc.vector.tensor_copy(got["vs_listed", b][:, first:last], window)
 
         def gather_scales():
             got["k_scale"] = sbuf("k_scale", [P, B * N], U8)
             nc.vector.tensor_copy(got["k_scale"][:], scale_pool[:].indirect(offsets[:]))
 
-        v_low_bf = sbuf("v_low_bf", [P, T], BF16)
+        v_low_bf = None
 
         def cast_low(c, first, last):
             start = pieces[c].start
@@ -136,6 +135,10 @@ def tile_attend_relu2_kernel(tc, qT, k_words, k_scales, vT, vs, offs, out):
                 nc.tensor.transpose(turned[:, t : t + P], got["vs_listed", b][:, t:N:PACK], ident[:])
             got["vs_slot", b] = sbuf("vs_slot%d" % b, [P, 1, PACK], F32)
             copy(got["vs_slot", b][:, 0, :], turned[:, VS_ROW : VS_ROW + PACK])
+
+        def spread_vs(b):
+            got["vs_slot", b] = sbuf("vs_slot%d" % b, [P, 1, PACK], F32)
+            nc.sync.dma_start(got["vs_slot", b][:, 0, :], got["vs_listed", b][VS_ROW:P, :])
 
         def gather_keys(b):
             got["k", b] = sbuf("k_listed%d" % b, [P, N], U32)
@@ -192,6 +195,9 @@ def tile_attend_relu2_kernel(tc, qT, k_words, k_scales, vT, vs, offs, out):
             got["high_listed", b] = sbuf("high_listed%d" % b, [P, N], BF16)
             nc.vector.tensor_copy(got["high_listed", b][:], v_high[:].indirect(listed(b)))
 
+        def gather_low_whole(b):
+            nc.vector.tensor_copy(low_listed[b][:], v_low[0][:].indirect(listed(b)))
+
         def turn_values(half, b, number):
             got[half + "_turned", b] = bank(number, "%s_turned%d" % (half, b), [P, 2, P])
             for u in range(2):
@@ -226,7 +232,8 @@ def tile_attend_relu2_kernel(tc, qT, k_words, k_scales, vT, vs, offs, out):
             nc.scalar.activation(got["plus_one"][:], total[:], ACT.Identity, bias=1.0)
 
         def invert():
-            nc.vector.reciprocal(inverse[:], got["plus_one"][:])
+            got["inverse"] = sbuf("inverse", [P, B], F32)
+            nc.vector.reciprocal(got["inverse"][:], got["plus_one"][:])
 
         def multiply(b, half, sums):
             codes, scale = got[half, b]
@@ -243,63 +250,59 @@ def tile_attend_relu2_kernel(tc, qT, k_words, k_scales, vT, vs, offs, out):
         def finish(b, cols, sums, on_scalar, queue):
             result = sbuf("result%d_%d" % (b, cols.start), [P, cols.stop - cols.start], F32)
             if on_scalar:
-                nc.scalar.activation(result[:], sums, ACT.Copy, scale=inverse[:, b : b + 1])
+                nc.scalar.activation(result[:], sums, ACT.Copy, scale=got["inverse"][:, b : b + 1])
             else:
-                nc.vector.tensor_scalar_mul(result[:], sums, inverse[:, b : b + 1])
+                nc.vector.tensor_scalar_mul(result[:], sums, got["inverse"][:, b : b + 1])
             queue.dma_start(out[b, :, cols], result[:])
 
-        gather_vs(0)
+        gather_vs(0, 0, N)
         weave_queries(0, act_copy)
-        quantize_queries(0)
         gather_scales()
+        quantize_queries(0)
         gather_keys(0)
         gather_keys(1)
-        cast_low(0, 0, LOW_CUTS[1])
         weave_queries(1, nc.scalar.copy)
         quantize_queries(1)
+        gather_vs(1, 0, N)
         score(0, 0)
         score(1, 1)
-        gather_vs(1)
         relu(0)
         square(0)
-        turn_vs(0, 5, nc.scalar.copy)
+        turn_vs(0, 6, nc.scalar.copy)
         turn_squares(0, 2)
         relu(1)
         square(1)
-        cast_low(1, 0, LOW_CUTS[2] - LOW_CUTS[1])
+        turn_vs(1, 1, nc.scalar.copy)
+        gather_low_whole(0)
+        gather_low_whole(1)
+        turn_values("low", 0, 4)
+        turn_squares(1, 3)
+        copy_values("low", 0, nc.scalar.copy)
+        add_one()
+        turn_values("low", 1, 5)
+        copy_values("low", 1, nc.scalar.copy)
+        weigh(0)
         gather_high(0)
         gather_high(1)
-        cast_low(2, 0, LOW_CUTS[3] - LOW_CUTS[2])
-        cast_low(3, 0, LOW_CUTS[4] - LOW_CUTS[3])
-        turn_vs(1, 1, nc.scalar.copy)
-        turn_squares(1, 3)
-        gather_low(0, 0, N, True)
-        weigh(0)
-        gather_low(1, 0, N, False)
         weigh(1)
-        add_one()
+        quantize_weights(0)
+        quantize_values("low", 0)
+        quantize_values("low", 1)
+        invert()
+        quantize_weights(1)
         turn_values("high", 0, 7)
         copy_values("high", 0, nc.scalar.copy)
         turn_values("high", 1, 6)
         copy_values("high", 1, nc.scalar.copy)
-        turn_values("low", 0, 4)
-        copy_values("low", 0, nc.scalar.copy)
-        turn_values("low", 1, 6)
-        copy_values("low", 1, nc.scalar.copy)
-        quantize_weights(0)
-        quantize_values("high", 0)
-        invert()
-        quantize_weights(1)
-        quantize_values("high", 1)
-        quantize_values("low", 0)
-        quantize_values("low", 1)
-        sums0 = bank(4, "sums0", [P, DV])
-        multiply(0, "high", sums0[:, P:DV])
-        sums1 = bank(1, "sums1", [P, P])
-        multiply(1, "high", sums1[:])
+        sums0 = bank(0, "sums0", [P, DV])
         multiply(0, "low", sums0[:, 0:P])
+        sums1 = bank(1, "sums1", [P, P])
+        multiply(1, "low", sums1[:])
+        quantize_values("high", 0)
+        multiply(0, "high", sums0[:, P:DV])
+        quantize_values("high", 1)
         sums2 = bank(2, "sums2", [P, P])
-        multiply(1, "low", sums2[:])
-        finish(1, slice(P, DV), sums1[:], True, nc.sync)
+        multiply(1, "high", sums2[:])
+        finish(1, slice(0, P), sums1[:], True, nc.sync)
         finish(0, slice(0, DV), sums0[:], True, nc.sync)
-        finish(1, slice(0, P), sums2[:], False, nc.sync)
+        finish(1, slice(P, DV), sums2[:], False, nc.sync)

@@ -9,9 +9,9 @@ FLOPS = 2 * B * NQ * N * (D + DV)
 P = 128
 PACK = 4
 VS_ROW = P - 1
-LOW_CUTS = (0, T)
-PAD = {"q_raw1":1024,"high_listed0":1024}
-OVER = {"positive0":["q_raw1",-1024],"vs_listed1":["q_raw1",1024],"vs_slot0":["positive0",0],"w_bf1":["high_listed0",-960],"w0_scale":["high_listed0",64],"low0_scale":["high_listed0",192],"low1_scale":["high_listed0",320],"inverse":["high_listed0",448]}
+LOW_CUTS = (0, 768, T)
+PAD = {"q_raw1":1024,"square0":1024}
+OVER = {"positive0":["q_raw1",-1024],"vs_listed1":["q_raw1",1024],"low_listed1":["q_bf1",0],"vs_slot0":["positive0",0],"vs_slot1":["v_low",0],"low_bf1":["positive1",0],"high_listed0":["square0",0],"high_listed1":["square0",1024],"w_bf1":["high_listed0",-960],"w0_scale":["high_listed0",64],"inverse":["high_listed0",448]}
 
 F32 = mybir.dt.float32
 BF16 = mybir.dt.bfloat16
@@ -61,9 +61,10 @@ def tile_attend_relu2_kernel(tc, qT, k_words, k_scales, vT, vs, offs, out):
         scale_pool = sbuf("scale_pool", [P, T], U8)
         vs_pool = sbuf("vs_pool", [P, T], F32)
         nc.gpsimd.memset(scale_pool[:].bitcast(I32), 0)
-        nc.vector.memset(vs_pool[0:VS_ROW, :], 0.0)
+        nc.vector.memset(vs_pool[0:VS_ROW, 0 : 3 * T // 4], 0.0)
+        nc.gpsimd.memset(vs_pool[0:VS_ROW, 3 * T // 4 : T], 0.0)
         pieces = [slice(LOW_CUTS[c], LOW_CUTS[c + 1]) for c in range(len(LOW_CUTS) - 1)]
-        v_low = [sbuf("v_low%d" % c, [P, cols.stop - cols.start], F32) for c, cols in enumerate(pieces)]
+        v_low = sbuf("v_low", [P, T], F32)
         q_raw = [sbuf("q_raw%d" % b, [P, PACK, NQ], F32) for b in range(B)]
         word_pool = sbuf("word_pool", [P, T], U32)
         v_high = sbuf("v_high", [P, T], F32)
@@ -82,7 +83,7 @@ def tile_attend_relu2_kernel(tc, qT, k_words, k_scales, vT, vs, offs, out):
             queue.dma_start(word_pool[:, first:last].bitcast(I32), words[:, first:last])
 
         def load_low(c):
-            nc.sync.dma_start(v_low[c][:], vT[0:P, pieces[c]])
+            nc.sync.dma_start(v_low[:, pieces[c]], vT[0:P, pieces[c]])
 
         def load_high():
             nc.sync.dma_start(v_high[:], vT[P:DV, :])
@@ -93,8 +94,9 @@ def tile_attend_relu2_kernel(tc, qT, k_words, k_scales, vT, vs, offs, out):
         for quad in range(4):
             load_scales(nc.sync, quad)
         load_words(nc.sync, 0, T)
-        load_queries(1)
         load_low(0)
+        load_queries(1)
+        load_low(1)
         load_high()
 
         ident = sbuf("ident", [P, P], F32)
@@ -112,22 +114,23 @@ def tile_attend_relu2_kernel(tc, qT, k_words, k_scales, vT, vs, offs, out):
             got["k_scale"] = sbuf("k_scale", [P, B * N], U8)
             nc.vector.tensor_copy(got["k_scale"][:], scale_pool[:].indirect(offsets[:]))
 
-        v_low_bf = None
+        v_low_bf = sbuf("v_low_bf", [P, T], BF16)
 
         def cast_low(c, first, last):
             start = pieces[c].start
-            nc.scalar.activation(v_low_bf[:, start + first : start + last], v_low[c][:, first:last], ACT.Copy)
+            nc.scalar.activation(v_low_bf[:, start + first : start + last], v_low[:, start + first : start + last], ACT.Copy)
 
-        low_listed = [sbuf("low_listed%d" % b, [P, N], BF16) for b in range(B)]
-        for b in range(B):
-            got["low_listed", b] = low_listed[b]
+        low_listed = {}
 
         def gather_low(b, first, last, on_scalar):
-            window = v_low_bf[:].indirect(offsets[:, (b * N + first) // 16 : (b * N + last) // 16])
+            if b not in low_listed:
+                low_listed[b] = sbuf("low_listed%d" % b, [P, N], BF16)
+                got["low_listed", b] = low_listed[b]
+            picks = offsets[:, (b * N + first) // 16 : (b * N + last) // 16]
             if on_scalar:
-                nc.scalar.activation(low_listed[b][:, first:last], window, ACT.Copy)
+                nc.scalar.activation(low_listed[b][:, first:last], v_low_bf[:].indirect(picks), ACT.Copy)
             else:
-                nc.vector.tensor_copy(low_listed[b][:, first:last], window)
+                nc.vector.tensor_copy(low_listed[b][:, first:last], v_low[:].indirect(picks))
 
         def turn_vs(b, number, copy):
             turned = bank(number, "vs_turned%d" % b, [P, P + PACK])
@@ -261,6 +264,7 @@ def tile_attend_relu2_kernel(tc, qT, k_words, k_scales, vT, vs, offs, out):
         quantize_queries(0)
         gather_keys(0)
         gather_keys(1)
+        cast_low(0, 0, LOW_CUTS[1])
         weave_queries(1, nc.scalar.copy)
         quantize_queries(1)
         gather_vs(1, 0, N)
@@ -272,37 +276,33 @@ def tile_attend_relu2_kernel(tc, qT, k_words, k_scales, vT, vs, offs, out):
         turn_squares(0, 2)
         relu(1)
         square(1)
+        cast_low(1, 0, 320)
+        cast_low(1, 320, T - LOW_CUTS[1])
         turn_vs(1, 1, nc.scalar.copy)
-        gather_low_whole(0)
-        gather_low_whole(1)
-        turn_values("low", 0, 4)
         turn_squares(1, 3)
-        copy_values("low", 0, nc.scalar.copy)
+        gather_low(1, 0, N, False)
+        gather_low(0, 0, 512, True)
         add_one()
-        turn_values("low", 1, 5)
-        copy_values("low", 1, nc.scalar.copy)
         weigh(0)
         gather_high(0)
         gather_high(1)
         weigh(1)
-        quantize_weights(0)
-        quantize_values("low", 0)
-        quantize_values("low", 1)
-        invert()
-        quantize_weights(1)
+        turn_values("low", 1, 1)
+        copy_values("low", 1, nc.scalar.copy)
         turn_values("high", 0, 7)
         copy_values("high", 0, nc.scalar.copy)
-        turn_values("high", 1, 6)
+        turn_values("low", 0, 4)
+        turn_values("high", 1, 5)
         copy_values("high", 1, nc.scalar.copy)
-        sums0 = bank(0, "sums0", [P, DV])
-        multiply(0, "low", sums0[:, 0:P])
-        sums1 = bank(1, "sums1", [P, P])
-        multiply(1, "low", sums1[:])
+        copy_values("low", 0, nc.scalar.copy)
+        quantize_weights(0)
+        invert()
+        quantize_weights(1)
+        quantize_values("low", 1)
         quantize_values("high", 0)
-        multiply(0, "high", sums0[:, P:DV])
         quantize_values("high", 1)
-        sums2 = bank(2, "sums2", [P, P])
-        multiply(1, "high", sums2[:])
-        finish(1, slice(0, P), sums1[:], True, nc.sync)
-        finish(0, slice(0, DV), sums0[:], True, nc.sync)
-        finish(1, slice(P, DV), sums2[:], False, nc.sync)
+        quantize_values("low", 0)
+        for b, half, number, on_scalar, queue in ((1, "low", 6, True, nc.sync), (0, "high", 0, True, nc.sync), (1, "high", 3, True, nc.scalar), (0, "low", 2, False, nc.sync)):
+            sums = bank(number, "sums%d" % number, [P, P])
+            multiply(b, half, sums[:])
+            finish(b, slice(0, P) if half == "low" else slice(P, DV), sums[:], on_scalar, queue)

@@ -277,8 +277,10 @@ def tile_attend_relu2_kernel(tc, qT, k_words, k_scales, vT, vs, offs, out):
         relu(1)
         square(1)
         cast_low(1, 0, 320)
-        cast_low(1, 320, T - LOW_CUTS[1])
-        turn_vs(1, 1, nc.scalar.copy)
+        for first in range(320, 704, 192):
+            cast_low(1, first, first + 192)
+        cast_low(1, 704, T - LOW_CUTS[1])
+        turn_vs(1, 6, nc.scalar.copy)
         turn_squares(1, 3)
         gather_low(1, 0, N, False)
         gather_low(0, 0, 512, True)
@@ -287,22 +289,22 @@ def tile_attend_relu2_kernel(tc, qT, k_words, k_scales, vT, vs, offs, out):
         gather_high(0)
         gather_high(1)
         weigh(1)
-        turn_values("low", 1, 1)
+        turn_values("low", 1, 6)
         copy_values("low", 1, nc.scalar.copy)
         turn_values("high", 0, 7)
         copy_values("high", 0, nc.scalar.copy)
         turn_values("low", 0, 4)
+        copy_values("low", 0, nc.scalar.copy)
         turn_values("high", 1, 5)
         copy_values("high", 1, nc.scalar.copy)
-        copy_values("low", 0, nc.scalar.copy)
         quantize_weights(0)
         invert()
         quantize_weights(1)
         quantize_values("low", 1)
         quantize_values("high", 0)
-        quantize_values("high", 1)
         quantize_values("low", 0)
-        for b, half, number, on_scalar, queue in ((1, "low", 6, True, nc.sync), (0, "high", 0, True, nc.sync), (1, "high", 3, True, nc.scalar), (0, "low", 2, False, nc.sync)):
+        quantize_values("high", 1)
+        for b, half, number, on_scalar, queue in ((1, "low", 6, True, nc.sync), (0, "high", 0, True, nc.sync), (0, "low", 2, True, nc.scalar), (1, "high", 3, False, nc.sync)):
             sums = bank(number, "sums%d" % number, [P, P])
             multiply(b, half, sums[:])
             finish(b, slice(0, P) if half == "low" else slice(P, DV), sums[:], on_scalar, queue)

@@ -9,9 +9,9 @@ FLOPS = 2 * B * NQ * N * (D + DV)
 P = 128
 PACK = 4
 VS_ROW = P - 1
-LOW_CUTS = (0, 768, T)
-PAD = {"q_raw1":1024,"square0":1024}
-OVER = {"positive0":["q_raw1",-1024],"vs_listed1":["q_raw1",1024],"low_listed1":["q_bf1",0],"vs_slot0":["positive0",0],"vs_slot1":["v_low",0],"low_bf1":["positive1",0],"high_listed0":["square0",0],"high_listed1":["square0",1024],"w_bf1":["high_listed0",-960],"w0_scale":["high_listed0",64],"inverse":["high_listed0",448]}
+ARENA = 16384
+PAD = {"scale_pool": ARENA, "q_raw1": 1024}
+OVER = {"w_bf1": ["scale_pool", 64 - ARENA], "high_listed0": ["scale_pool", 1024 - ARENA], "w0_scale": ["scale_pool", 1088 - ARENA], "inverse": ["scale_pool", 1472 - ARENA], "w_bf0": ["scale_pool", 1984 - ARENA], "positive0": ["q_raw1", -1024], "vs_listed1": ["q_raw1", 1024], "low_listed1": ["q_bf1", 0], "vs_slot0": ["positive0", 0], "vs_slot1": ["v_low", 0], "low_bf1": ["positive1", 0]}
 
 F32 = mybir.dt.float32
 BF16 = mybir.dt.bfloat16
@@ -55,100 +55,120 @@ def tile_attend_relu2_kernel(tc, qT, k_words, k_scales, vT, vs, offs, out):
 
         offsets = held.tile([P, B * N // 16], U16, name="offsets")
 
-        def listed(b):
-            return offsets[:, b * N // 16 : (b + 1) * N // 16]
+        def picks(b, first, last):
+            return offsets[:, (b * N + first) // 16 : (b * N + last) // 16]
 
         scale_pool = sbuf("scale_pool", [P, T], U8)
         vs_pool = sbuf("vs_pool", [P, T], F32)
         nc.gpsimd.memset(scale_pool[:].bitcast(I32), 0)
         nc.vector.memset(vs_pool[0:VS_ROW, 0 : 3 * T // 4], 0.0)
         nc.gpsimd.memset(vs_pool[0:VS_ROW, 3 * T // 4 : T], 0.0)
-        pieces = [slice(LOW_CUTS[c], LOW_CUTS[c + 1]) for c in range(len(LOW_CUTS) - 1)]
-        v_low = sbuf("v_low", [P, T], F32)
+        pool = {"low": sbuf("v_low", [P, T], F32), "high": sbuf("v_high", [P, T], F32)}
+        rows = {"low": slice(0, P), "high": slice(P, DV)}
         q_raw = [sbuf("q_raw%d" % b, [P, PACK, NQ], F32) for b in range(B)]
         word_pool = sbuf("word_pool", [P, T], U32)
-        v_high = sbuf("v_high", [P, T], F32)
+        got = {}
 
-        def load_scales(queue, quad):
-            queue.dma_start(
-                scale_pool[32 * quad : 32 * quad + 4, :].bitcast(I32),
-                k_scales[0, 4 * quad : 4 * quad + 4, :].bitcast(I32),
-            )
+        def load_scales(queue):
+            for quad in range(4):
+                queue.dma_start(
+                    scale_pool[32 * quad : 32 * quad + 4, :].bitcast(I32),
+                    k_scales[0, 4 * quad : 4 * quad + 4, :].bitcast(I32),
+                )
 
         def load_queries(b):
             nc.sync.dma_start(q_raw[b][:], qT[b].rearrange("(p j) n -> p j n", j=PACK))
 
-        def load_words(queue, first, last):
+        def load_words(first, last):
             words = k_words[0].rearrange("p t r -> p (t r)").bitcast(I32)
-            queue.dma_start(word_pool[:, first:last].bitcast(I32), words[:, first:last])
+            nc.sync.dma_start(word_pool[:, first:last].bitcast(I32), words[:, first:last])
 
-        def load_low(c):
-            nc.sync.dma_start(v_low[:, pieces[c]], vT[0:P, pieces[c]])
-
-        def load_high():
-            nc.sync.dma_start(v_high[:], vT[P:DV, :])
+        def load_values(half, first, last):
+            nc.sync.dma_start(pool[half][:, first:last], vT[rows[half], first:last])
 
         nc.sync.dma_start(offsets[:], offs)
         nc.scalar.dma_start(vs_pool[VS_ROW:P, :], vs[0:1, :])
         load_queries(0)
-        for quad in range(4):
-            load_scales(nc.sync, quad)
-        load_words(nc.sync, 0, T)
-        load_low(0)
+        load_scales(nc.sync)
+        load_words(0, T)
+        load_values("low", 0, 768)
         load_queries(1)
-        load_low(1)
-        load_high()
+        load_values("low", 768, T)
+        load_values("high", 0, T)
 
         ident = sbuf("ident", [P, P], F32)
         make_identity(nc, ident[:])
         total = sbuf("total", [P, B], F32)
-        got = {}
 
-        def gather_vs(b, first, last):
+        def probe(name, source, dtype=F32):
+            mark = sbuf("probe_" + name, [P, 1], dtype)
+            nc.gpsimd.tensor_copy(mark[:], source)
+
+        def gather_vs(first, last):
             if first == 0:
-                got["vs_listed", b] = sbuf("vs_listed%d" % b, [P, N], F32)
-            window = vs_pool[:].indirect(offsets[:, (b * N + first) // 16 : (b * N + last) // 16])
-            nc.vector.tensor_copy(got["vs_listed", b][:, first:last], window)
+                got["vs_listed"] = sbuf("vs_listed", [P, B * N], F32)
+            nc.vector.tensor_copy(got["vs_listed"][:, first:last], vs_pool[:].indirect(picks(0, first, last)))
+
+        def gather_vs_of(b):
+            got["vs_listed", b] = sbuf("vs_listed%d" % b, [P, N], F32)
+            nc.vector.tensor_copy(got["vs_listed", b][:], vs_pool[:].indirect(picks(b, 0, N)))
 
         def gather_scales():
             got["k_scale"] = sbuf("k_scale", [P, B * N], U8)
             nc.vector.tensor_copy(got["k_scale"][:], scale_pool[:].indirect(offsets[:]))
 
-        v_low_bf = sbuf("v_low_bf", [P, T], BF16)
+        def act_copy(to, source):
+            nc.scalar.activation(to, source, ACT.Copy)
 
-        def cast_low(c, first, last):
-            start = pieces[c].start
-            nc.scalar.activation(v_low_bf[:, start + first : start + last], v_low[:, start + first : start + last], ACT.Copy)
+        def cast(half, first, last, copy):
+            if (half, "bf") not in got:
+                got[half, "bf"] = sbuf("v_%s_bf" % half, [P, T], BF16)
+            copy(got[half, "bf"][:, first:last], pool[half][:, first:last])
 
-        low_listed = {}
-
-        def gather_low(b, first, last, on_scalar):
-            if b not in low_listed:
-                low_listed[b] = sbuf("low_listed%d" % b, [P, N], BF16)
-                got["low_listed", b] = low_listed[b]
-            picks = offsets[:, (b * N + first) // 16 : (b * N + last) // 16]
-            if on_scalar:
-                nc.scalar.activation(low_listed[b][:, first:last], v_low_bf[:].indirect(picks), ACT.Copy)
+        def gather_values(half, b, first, last, road):
+            if (half + "_listed", b) not in got:
+                got[half + "_listed", b] = sbuf("%s_listed%d" % (half, b), [P, N], BF16)
+            to = got[half + "_listed", b][:, first:last]
+            if road == "scalar":
+                nc.scalar.activation(to, got[half, "bf"][:].indirect(picks(b, first, last)), ACT.Copy)
+            elif road == "vector_bf":
+                nc.vector.tensor_copy(to, got[half, "bf"][:].indirect(picks(b, first, last)))
             else:
-                nc.vector.tensor_copy(low_listed[b][:, first:last], v_low[:].indirect(picks))
+                nc.vector.tensor_copy(to, pool[half][:].indirect(picks(b, first, last)))
 
-        def turn_vs(b, number, copy):
-            turned = bank(number, "vs_turned%d" % b, [P, P + PACK])
+        def listed_vs(b):
+            if ("vs_listed", b) in got:
+                return got["vs_listed", b][:]
+            return got["vs_listed"][:, b * N : (b + 1) * N]
+
+        def turn_vs(b, number):
+            got["vs_turned", b] = bank(number, "vs_turned%d" % b, [P, P + PACK])
             for t in reversed(range(PACK)):
-                nc.tensor.transpose(turned[:, t : t + P], got["vs_listed", b][:, t:N:PACK], ident[:])
-            got["vs_slot", b] = sbuf("vs_slot%d" % b, [P, 1, PACK], F32)
-            copy(got["vs_slot", b][:, 0, :], turned[:, VS_ROW : VS_ROW + PACK])
+                nc.tensor.transpose(got["vs_turned", b][:, t : t + P], listed_vs(b)[:, t:N:PACK], ident[:])
 
-        def spread_vs(b):
+        def copy_vs(b, copy):
             got["vs_slot", b] = sbuf("vs_slot%d" % b, [P, 1, PACK], F32)
-            nc.sync.dma_start(got["vs_slot", b][:, 0, :], got["vs_listed", b][VS_ROW:P, :])
+            copy(got["vs_slot", b][:, 0, :], got["vs_turned", b][:, VS_ROW : VS_ROW + PACK])
+
+        def turn_both_vs(number):
+            got["vs_turned"] = bank(number, "vs_turned", [P, B, P + PACK])
+            for b in range(B):
+                for t in reversed(range(PACK)):
+                    nc.tensor.transpose(got["vs_turned"][:, b, t : t + P], listed_vs(b)[:, t:N:PACK], ident[:])
+
+        def copy_both_vs(copy):
+            slots = sbuf("vs_slots", [P, B, PACK], F32)
+            copy(slots[:], got["vs_turned"][:, :, VS_ROW : VS_ROW + PACK])
+            for b in range(B):
+                got["vs_slot", b] = slots[:, b : b + 1, :]
+
+        def spread_vs(b, queue):
+            got["vs_slot", b] = sbuf("vs_slot%d" % b, [P, 1, PACK], F32)
+            queue.dma_start(got["vs_slot", b][:, 0, :], listed_vs(b)[VS_ROW:P, :])
 
         def gather_keys(b):
             got["k", b] = sbuf("k_listed%d" % b, [P, N], U32)
-            nc.vector.tensor_copy(got["k", b][:], word_pool[:].indirect(listed(b)))
-
-        def act_copy(to, source):
-            nc.scalar.activation(to, source, ACT.Copy)
+            nc.vector.tensor_copy(got["k", b][:], word_pool[:].indirect(picks(b, 0, N)))
 
         def weave_queries(b, copy):
             got["q_bf", b] = sbuf("q_bf%d" % b, [P, NQ * PACK], BF16)
@@ -194,13 +214,6 @@ def tile_attend_relu2_kernel(tc, qT, k_words, k_scales, vT, vs, offs, out):
             for t in range(PACK):
                 nc.tensor.transpose(got["p_turned", b][:, t, :], got["p", b][:, t // 2, t % 2, 0:P], ident[:])
 
-        def gather_high(b):
-            got["high_listed", b] = sbuf("high_listed%d" % b, [P, N], BF16)
-            nc.vector.tensor_copy(got["high_listed", b][:], v_high[:].indirect(listed(b)))
-
-        def gather_low_whole(b):
-            nc.vector.tensor_copy(low_listed[b][:], v_low[0][:].indirect(listed(b)))
-
         def turn_values(half, b, number):
             got[half + "_turned", b] = bank(number, "%s_turned%d" % (half, b), [P, 2, P])
             for u in range(2):
@@ -234,14 +247,19 @@ def tile_attend_relu2_kernel(tc, qT, k_words, k_scales, vT, vs, offs, out):
             got["plus_one"] = sbuf("plus_one", [P, B], F32)
             nc.scalar.activation(got["plus_one"][:], total[:], ACT.Identity, bias=1.0)
 
+        def add_one_gpsimd():
+            got["plus_one"] = sbuf("plus_one", [P, B], F32)
+            nc.gpsimd.tensor_scalar_add(got["plus_one"][:], total[:], 1.0)
+
         def invert():
             got["inverse"] = sbuf("inverse", [P, B], F32)
             nc.vector.reciprocal(got["inverse"][:], got["plus_one"][:])
 
-        def multiply(b, half, sums):
+        def finish(b, half, number, on_scalar, queue):
+            sums = bank(number, "sums_%s%d" % (half, b), [P, P])
             codes, scale = got[half, b]
             nc.tensor.matmul_mx(
-                out=sums,
+                out=sums[:],
                 lhsT=got["w", b][0][:].bitcast(FP8X4),
                 lhsT_scale=got["w", b][1][:],
                 rhs=codes[:].bitcast(FP8X4),
@@ -249,45 +267,45 @@ def tile_attend_relu2_kernel(tc, qT, k_words, k_scales, vT, vs, offs, out):
                 start=True,
                 stop=True,
             )
-
-        def finish(b, cols, sums, on_scalar, queue):
-            result = sbuf("result%d_%d" % (b, cols.start), [P, cols.stop - cols.start], F32)
+            result = sbuf("result_%s%d" % (half, b), [P, P], F32)
             if on_scalar:
-                nc.scalar.activation(result[:], sums, ACT.Copy, scale=got["inverse"][:, b : b + 1])
+                nc.scalar.activation(result[:], sums[:], ACT.Copy, scale=got["inverse"][:, b : b + 1])
             else:
-                nc.vector.tensor_scalar_mul(result[:], sums, got["inverse"][:, b : b + 1])
-            queue.dma_start(out[b, :, cols], result[:])
+                nc.vector.tensor_scalar_mul(result[:], sums[:], got["inverse"][:, b : b + 1])
+            queue.dma_start(out[b, :, rows[half]], result[:])
 
-        gather_vs(0, 0, N)
+        gather_vs_of(0)
         weave_queries(0, act_copy)
         gather_scales()
         quantize_queries(0)
         gather_keys(0)
         gather_keys(1)
-        cast_low(0, 0, LOW_CUTS[1])
+        cast("low", 0, 768, act_copy)
         weave_queries(1, nc.scalar.copy)
         quantize_queries(1)
-        gather_vs(1, 0, N)
+        gather_vs_of(1)
         score(0, 0)
         score(1, 1)
         relu(0)
         square(0)
-        turn_vs(0, 6, nc.scalar.copy)
+        turn_vs(0, 6)
+        copy_vs(0, nc.scalar.copy)
         turn_squares(0, 2)
         relu(1)
         square(1)
-        cast_low(1, 0, 320)
-        for first in range(320, 704, 192):
-            cast_low(1, first, first + 192)
-        cast_low(1, 704, T - LOW_CUTS[1])
-        turn_vs(1, 6, nc.scalar.copy)
+        cast("low", 768, 1088, act_copy)
+        cast("low", 1088, 1280, act_copy)
+        cast("low", 1280, 1472, act_copy)
+        cast("low", 1472, T, act_copy)
+        turn_vs(1, 6)
+        copy_vs(1, nc.scalar.copy)
         turn_squares(1, 3)
-        gather_low(1, 0, N, False)
-        gather_low(0, 0, 512, True)
+        gather_values("low", 1, 0, N, "vector")
+        gather_values("low", 0, 0, N, "scalar")
         add_one()
+        gather_values("high", 0, 0, N, "vector")
+        gather_values("high", 1, 0, N, "vector")
         weigh(0)
-        gather_high(0)
-        gather_high(1)
         weigh(1)
         turn_values("low", 1, 6)
         copy_values("low", 1, nc.scalar.copy)
@@ -304,7 +322,7 @@ def tile_attend_relu2_kernel(tc, qT, k_words, k_scales, vT, vs, offs, out):
         quantize_values("high", 0)
         quantize_values("low", 0)
         quantize_values("high", 1)
-        for b, half, number, on_scalar, queue in ((1, "low", 6, True, nc.sync), (0, "high", 0, True, nc.sync), (0, "low", 2, True, nc.scalar), (1, "high", 3, False, nc.sync)):
-            sums = bank(number, "sums%d" % number, [P, P])
-            multiply(b, half, sums[:])
-            finish(b, slice(0, P) if half == "low" else slice(P, DV), sums[:], on_scalar, queue)
+        finish(1, "low", 6, True, nc.sync)
+        finish(0, "high", 0, True, nc.sync)
+        finish(0, "low", 2, True, nc.scalar)
+        finish(1, "high", 3, False, nc.sync)

@@ -11,7 +11,7 @@ PACK = 4
 VS_ROW = P - 1
 ARENA = 16384
 PAD = {"scale_pool": ARENA, "q_raw1": 1024}
-OVER = {"w_bf1": ["scale_pool", 64 - ARENA], "high_listed0": ["scale_pool", 1024 - ARENA], "w0_scale": ["scale_pool", 1088 - ARENA], "inverse": ["scale_pool", 1472 - ARENA], "w_bf0": ["scale_pool", 1984 - ARENA], "positive0": ["q_raw1", -1024], "vs_listed1": ["q_raw1", 1024], "low_listed1": ["q_bf1", 0], "vs_slot0": ["positive0", 0], "vs_slot1": ["v_low", 0], "low_bf1": ["positive1", 0]}
+OVER = {"high_listed0": ["scale_pool", 1024 - ARENA], "w0_scale": ["scale_pool", 1088 - ARENA], "inverse": ["scale_pool", 1472 - ARENA], "w_bf0": ["v_high", 0], "w_bf1": ["v_high", 1024], "positive0": ["q_raw1", -1024], "vs_listed1": ["q_raw1", 1024], "low_listed1": ["q_bf1", 0], "vs_slot0": ["positive0", 0], "vs_slot1": ["v_low", 0], "low_bf1": ["positive1", 0]}
 
 F32 = mybir.dt.float32
 BF16 = mybir.dt.bfloat16

@@ -11,7 +11,7 @@ PACK = 4
 VS_ROW = P - 1
 ARENA = 16384
 PAD = {"scale_pool": ARENA, "q_raw1": 1024}
-OVER = {"high_listed0": ["scale_pool", 1024 - ARENA], "w0_scale": ["scale_pool", 1088 - ARENA], "inverse": ["scale_pool", 1472 - ARENA], "w_bf0": ["v_high", 0], "w_bf1": ["v_high", 1024], "positive0": ["q_raw1", -1024], "vs_listed1": ["q_raw1", 1024], "low_listed1": ["q_bf1", 0], "vs_slot0": ["positive0", 0], "vs_slot1": ["v_low", 0], "low_bf1": ["positive1", 0]}
+OVER = {"high_listed0": ["scale_pool", 1024 - ARENA], "w0_scale": ["scale_pool", 1088 - ARENA], "inverse": ["scale_pool", 1472 - ARENA], "positive0": ["q_raw1", -1024], "vs_listed1": ["q_raw1", 1024], "low_listed1": ["q_bf1", 0], "vs_slot0": ["positive0", 0], "vs_slot1": ["v_low", 0], "low_bf1": ["positive1", 0], "w_bf0": ["positive1", 1024]}
 
 F32 = mybir.dt.float32
 BF16 = mybir.dt.bfloat16

@@ -10,8 +10,6 @@ P = 128
 PACK = 4
 VS_ROW = P - 1
 ARENA = 16384
-PAD = {"scale_pool": ARENA, "q_raw1": 1024}
-OVER = {"high_listed0": ["scale_pool", 1024 - ARENA], "w0_scale": ["scale_pool", 1088 - ARENA], "inverse": ["scale_pool", 1472 - ARENA], "positive0": ["q_raw1", -1024], "vs_listed1": ["q_raw1", 1024], "low_listed1": ["q_bf1", 0], "vs_slot0": ["positive0", 0], "vs_slot1": ["v_low", 0], "low_bf1": ["positive1", 0], "w_bf0": ["positive1", 1024]}
 
 F32 = mybir.dt.float32
 BF16 = mybir.dt.bfloat16
@@ -23,6 +21,7 @@ FP8X4 = mybir.dt.float8_e4m3fn_x4
 ACT = mybir.ActivationFunctionType
 ALU = mybir.AluOpType
 WIDTH = {F32: 4, BF16: 2, U32: 4, U8: 1}
+OVER = {"low_bf0":["v_high",0],"low_bf1":["v_high",1024],"plus_one":["v_high",4096]}
 
 
 def tile_attend_relu2_kernel(tc, qT, k_words, k_scales, vT, vs, offs, out):
@@ -40,7 +39,7 @@ def tile_attend_relu2_kernel(tc, qT, k_words, k_scales, vT, vs, offs, out):
             if name in OVER:
                 places[name] = places[OVER[name][0]] + OVER[name][1]
             else:
-                places[name] = places["end"] + PAD.get(name, 0)
+                places[name] = places["end"]
                 places["end"] = places[name] + (size + 63) // 64 * 64
             return work.tile(shape, dtype, name=name, align_bytes=64, offset=places[name])
 
@@ -60,14 +59,24 @@ def tile_attend_relu2_kernel(tc, qT, k_words, k_scales, vT, vs, offs, out):
 
         scale_pool = sbuf("scale_pool", [P, T], U8)
         vs_pool = sbuf("vs_pool", [P, T], F32)
-        nc.gpsimd.memset(scale_pool[:].bitcast(I32), 0)
-        nc.vector.memset(vs_pool[0:VS_ROW, 0 : 3 * T // 4], 0.0)
-        nc.gpsimd.memset(vs_pool[0:VS_ROW, 3 * T // 4 : T], 0.0)
         pool = {"low": sbuf("v_low", [P, T], F32), "high": sbuf("v_high", [P, T], F32)}
         rows = {"low": slice(0, P), "high": slice(P, DV)}
-        q_raw = [sbuf("q_raw%d" % b, [P, PACK, NQ], F32) for b in range(B)]
+        q_raw = [sbuf("q_raw0", [P, PACK, NQ], F32)]
+        places["end"] = places["end"] + 1024
+        q_raw.append(sbuf("q_raw1", [P, PACK, NQ], F32))
         word_pool = sbuf("word_pool", [P, T], U32)
+        ident = sbuf("ident", [P, P], F32)
+        total = sbuf("total", [P, B], F32)
         got = {}
+
+        def zero_scales(engine):
+            engine.memset(scale_pool[:].bitcast(I32), 0)
+
+        def zero_vs(engine, first, last):
+            engine.memset(vs_pool[0:VS_ROW, first:last], 0.0)
+
+        def load_vs(queue):
+            queue.dma_start(vs_pool[VS_ROW:P, :], vs[0:1, :])
 
         def load_scales(queue):
             for quad in range(4):
@@ -76,8 +85,8 @@ def tile_attend_relu2_kernel(tc, qT, k_words, k_scales, vT, vs, offs, out):
                     k_scales[0, 4 * quad : 4 * quad + 4, :].bitcast(I32),
                 )
 
-        def load_queries(b):
-            nc.sync.dma_start(q_raw[b][:], qT[b].rearrange("(p j) n -> p j n", j=PACK))
+        def load_queries(b, queue=nc.sync):
+            queue.dma_start(q_raw[b][:], qT[b].rearrange("(p j) n -> p j n", j=PACK))
 
         def load_words(first, last):
             words = k_words[0].rearrange("p t r -> p (t r)").bitcast(I32)
@@ -86,85 +95,39 @@ def tile_attend_relu2_kernel(tc, qT, k_words, k_scales, vT, vs, offs, out):
         def load_values(half, first, last):
             nc.sync.dma_start(pool[half][:, first:last], vT[rows[half], first:last])
 
-        nc.sync.dma_start(offsets[:], offs)
-        nc.scalar.dma_start(vs_pool[VS_ROW:P, :], vs[0:1, :])
-        load_queries(0)
-        load_scales(nc.sync)
-        load_words(0, T)
-        load_values("low", 0, 768)
-        load_queries(1)
-        load_values("low", 768, T)
-        load_values("high", 0, T)
-
-        ident = sbuf("ident", [P, P], F32)
-        make_identity(nc, ident[:])
-        total = sbuf("total", [P, B], F32)
-
         def probe(name, source, dtype=F32):
             mark = sbuf("probe_" + name, [P, 1], dtype)
             nc.gpsimd.tensor_copy(mark[:], source)
 
-        def gather_vs(first, last):
-            if first == 0:
-                got["vs_listed"] = sbuf("vs_listed", [P, B * N], F32)
-            nc.vector.tensor_copy(got["vs_listed"][:, first:last], vs_pool[:].indirect(picks(0, first, last)))
-
-        def gather_vs_of(b):
-            got["vs_listed", b] = sbuf("vs_listed%d" % b, [P, N], F32)
-            nc.vector.tensor_copy(got["vs_listed", b][:], vs_pool[:].indirect(picks(b, 0, N)))
-
-        def gather_scales():
-            got["k_scale"] = sbuf("k_scale", [P, B * N], U8)
-            nc.vector.tensor_copy(got["k_scale"][:], scale_pool[:].indirect(offsets[:]))
-
         def act_copy(to, source):
             nc.scalar.activation(to, source, ACT.Copy)
 
-        def cast(half, first, last, copy):
-            if (half, "bf") not in got:
-                got[half, "bf"] = sbuf("v_%s_bf" % half, [P, T], BF16)
-            copy(got[half, "bf"][:, first:last], pool[half][:, first:last])
+        def gather_vs(b, copy):
+            got["vs_listed", b] = sbuf("vs_listed%d" % b, [P, N], F32)
+            copy(got["vs_listed", b][:], vs_pool[:].indirect(picks(b, 0, N)))
 
-        def gather_values(half, b, first, last, road):
+        def gather_scales(b, first=0, last=N):
+            if ("k_scale", b) not in got:
+                got["k_scale", b] = sbuf("k_scale%d" % b, [P, N], U8)
+            nc.vector.tensor_copy(got["k_scale", b][:, first:last], scale_pool[:].indirect(picks(b, first, last)))
+
+        def gather_values(half, b, first, last, copy):
             if (half + "_listed", b) not in got:
                 got[half + "_listed", b] = sbuf("%s_listed%d" % (half, b), [P, N], BF16)
-            to = got[half + "_listed", b][:, first:last]
-            if road == "scalar":
-                nc.scalar.activation(to, got[half, "bf"][:].indirect(picks(b, first, last)), ACT.Copy)
-            elif road == "vector_bf":
-                nc.vector.tensor_copy(to, got[half, "bf"][:].indirect(picks(b, first, last)))
-            else:
-                nc.vector.tensor_copy(to, pool[half][:].indirect(picks(b, first, last)))
-
-        def listed_vs(b):
-            if ("vs_listed", b) in got:
-                return got["vs_listed", b][:]
-            return got["vs_listed"][:, b * N : (b + 1) * N]
+            copy(got[half + "_listed", b][:, first:last], pool[half][:].indirect(picks(b, first, last)))
 
         def turn_vs(b, number):
             got["vs_turned", b] = bank(number, "vs_turned%d" % b, [P, P + PACK])
             for t in reversed(range(PACK)):
-                nc.tensor.transpose(got["vs_turned", b][:, t : t + P], listed_vs(b)[:, t:N:PACK], ident[:])
+                nc.tensor.transpose(got["vs_turned", b][:, t : t + P], got["vs_listed", b][:, t:N:PACK], ident[:])
 
         def copy_vs(b, copy):
             got["vs_slot", b] = sbuf("vs_slot%d" % b, [P, 1, PACK], F32)
             copy(got["vs_slot", b][:, 0, :], got["vs_turned", b][:, VS_ROW : VS_ROW + PACK])
 
-        def turn_both_vs(number):
-            got["vs_turned"] = bank(number, "vs_turned", [P, B, P + PACK])
-            for b in range(B):
-                for t in reversed(range(PACK)):
-                    nc.tensor.transpose(got["vs_turned"][:, b, t : t + P], listed_vs(b)[:, t:N:PACK], ident[:])
-
-        def copy_both_vs(copy):
-            slots = sbuf("vs_slots", [P, B, PACK], F32)
-            copy(slots[:], got["vs_turned"][:, :, VS_ROW : VS_ROW + PACK])
-            for b in range(B):
-                got["vs_slot", b] = slots[:, b : b + 1, :]
-
         def spread_vs(b, queue):
             got["vs_slot", b] = sbuf("vs_slot%d" % b, [P, 1, PACK], F32)
-            queue.dma_start(got["vs_slot", b][:, 0, :], listed_vs(b)[VS_ROW:P, :])
+            queue.dma_start(got["vs_slot", b][:, 0, :], got["vs_listed", b][VS_ROW:P, :])
 
         def gather_keys(b):
             got["k", b] = sbuf("k_listed%d" % b, [P, N], U32)
@@ -187,7 +150,7 @@ def tile_attend_relu2_kernel(tc, qT, k_words, k_scales, vT, vs, offs, out):
                 lhsT=got["q", b][0][:].bitcast(FP8X4),
                 lhsT_scale=got["q", b][1][:],
                 rhs=got["k", b][:].bitcast(FP8X4),
-                rhs_scale=got["k_scale"][:, b * N : (b + 1) * N],
+                rhs_scale=got["k_scale", b][:],
                 start=True,
                 stop=True,
             )
@@ -243,13 +206,9 @@ def tile_attend_relu2_kernel(tc, qT, k_words, k_scales, vT, vs, offs, out):
         def quantize_weights(b):
             got["w", b] = quantize("w%d" % b, got["w_bf", b][:].rearrange("p q t -> p (q t)"), NQ)
 
-        def add_one():
+        def add_one(engine):
             got["plus_one"] = sbuf("plus_one", [P, B], F32)
-            nc.scalar.activation(got["plus_one"][:], total[:], ACT.Identity, bias=1.0)
-
-        def add_one_gpsimd():
-            got["plus_one"] = sbuf("plus_one", [P, B], F32)
-            nc.gpsimd.tensor_scalar_add(got["plus_one"][:], total[:], 1.0)
+            engine.tensor_scalar_add(got["plus_one"][:], total[:], 1.0)
 
         def invert():
             got["inverse"] = sbuf("inverse", [P, B], F32)
@@ -274,55 +233,65 @@ def tile_attend_relu2_kernel(tc, qT, k_words, k_scales, vT, vs, offs, out):
                 nc.vector.tensor_scalar_mul(result[:], sums[:], got["inverse"][:, b : b + 1])
             queue.dma_start(out[b, :, rows[half]], result[:])
 
-        gather_vs_of(0)
+        vcopy = nc.vector.tensor_copy
+        scopy = nc.scalar.copy
+        zero_scales(nc.gpsimd)
+        zero_vs(nc.vector, 0, 3 * T // 4)
+        zero_vs(nc.gpsimd, 3 * T // 4, T)
+        nc.sync.dma_start(offsets[:], offs)
+        load_vs(nc.scalar)
+        load_queries(0)
+        load_scales(nc.sync)
+        load_words(0, T)
+        load_queries(1)
+        load_values("low", 0, T)
+        load_values("high", 0, T)
+        make_identity(nc, ident[:])
+
         weave_queries(0, act_copy)
-        gather_scales()
+        gather_scales(0)
+        gather_vs(0, act_copy)
         quantize_queries(0)
+        gather_scales(1)
+        gather_vs(1, act_copy)
+        spread_vs(0, nc.sync)
+        spread_vs(1, nc.sync)
         gather_keys(0)
+        weave_queries(1, act_copy)
         gather_keys(1)
-        cast("low", 0, 768, act_copy)
-        weave_queries(1, nc.scalar.copy)
         quantize_queries(1)
-        gather_vs_of(1)
         score(0, 0)
         score(1, 1)
         relu(0)
         square(0)
-        turn_vs(0, 6)
-        copy_vs(0, nc.scalar.copy)
-        turn_squares(0, 2)
         relu(1)
+        gather_values("low", 1, 384, N, act_copy)
         square(1)
-        cast("low", 768, 1088, act_copy)
-        cast("low", 1088, 1280, act_copy)
-        cast("low", 1280, 1472, act_copy)
-        cast("low", 1472, T, act_copy)
-        turn_vs(1, 6)
-        copy_vs(1, nc.scalar.copy)
+        gather_values("low", 0, 0, N, vcopy)
+        gather_values("low", 1, 0, 384, vcopy)
+        turn_squares(0, 2)
+        turn_values("low", 0, 4)
+        turn_values("low", 1, 5)
         turn_squares(1, 3)
-        gather_values("low", 1, 0, N, "vector")
-        gather_values("low", 0, 0, N, "scalar")
-        add_one()
-        gather_values("high", 0, 0, N, "vector")
-        gather_values("high", 1, 0, N, "vector")
+        gather_values("high", 1, 0, N, act_copy)
+        gather_values("high", 0, 0, N, vcopy)
         weigh(0)
         weigh(1)
-        turn_values("low", 1, 6)
-        copy_values("low", 1, nc.scalar.copy)
-        turn_values("high", 0, 7)
-        copy_values("high", 0, nc.scalar.copy)
-        turn_values("low", 0, 4)
-        copy_values("low", 0, nc.scalar.copy)
-        turn_values("high", 1, 5)
-        copy_values("high", 1, nc.scalar.copy)
+        add_one(nc.vector)
+        copy_values("low", 0, scopy)
+        copy_values("low", 1, scopy)
+        turn_values("high", 0, 6)
+        turn_values("high", 1, 7)
         quantize_weights(0)
         invert()
         quantize_weights(1)
+        copy_values("high", 0, scopy)
+        copy_values("high", 1, scopy)
+        quantize_values("low", 0)
         quantize_values("low", 1)
         quantize_values("high", 0)
-        quantize_values("low", 0)
         quantize_values("high", 1)
-        finish(1, "low", 6, True, nc.sync)
-        finish(0, "high", 0, True, nc.sync)
-        finish(0, "low", 2, True, nc.scalar)
+        finish(0, "low", 0, True, nc.sync)
+        finish(1, "low", 1, True, nc.sync)
+        finish(0, "high", 2, True, nc.scalar)
         finish(1, "high", 3, False, nc.sync)

@@ -1,7 +1,6 @@
 from contextlib import ExitStack
 
 import concourse.mybir as mybir
-from concourse.masks import make_identity
 
 B, N, T, D, DV, NQ = 2, 512, 2048, 512, 256, 128
 FLOPS = 2 * B * NQ * N * (D + DV)
@@ -21,7 +20,7 @@ FP8X4 = mybir.dt.float8_e4m3fn_x4
 ACT = mybir.ActivationFunctionType
 ALU = mybir.AluOpType
 WIDTH = {F32: 4, BF16: 2, U32: 4, U8: 1}
-OVER = {"low_bf0":["v_high",0],"low_bf1":["v_high",1024],"plus_one":["v_high",4096]}
+OVER = {"low_bf0":["v_high",0],"low_bf1":["v_high",1024],"w_bf1":["v_high",2048],"w0_codes":["v_high",3072],"inverse":["v_high",4096],"plus_one":["v_high",4160]}
 
 
 def tile_attend_relu2_kernel(tc, qT, k_words, k_scales, vT, vs, offs, out):
@@ -65,9 +64,42 @@ def tile_attend_relu2_kernel(tc, qT, k_words, k_scales, vT, vs, offs, out):
         places["end"] = places["end"] + 1024
         q_raw.append(sbuf("q_raw1", [P, PACK, NQ], F32))
         word_pool = sbuf("word_pool", [P, T], U32)
-        ident = sbuf("ident", [P, P], F32)
         total = sbuf("total", [P, B], F32)
         got = {}
+
+        def count_columns():
+            got["ones"] = sbuf("ones", [P, P], F32)
+            got["first"] = sbuf("first", [P, 1], F32)
+            got["column"] = sbuf("column", [P, P], F32)
+            nc.vector.memset(got["ones"][:], 1.0)
+            for quad in range(4):
+                nc.gpsimd.memset(got["first"][32 * quad : 32 * quad + 32, :], 32.0 * quad)
+            nc.vector.tensor_tensor_scan(got["column"][:], got["ones"][:], got["ones"][:], -1.0, ALU.mult, ALU.add)
+
+        def count_rows():
+            shifted = sbuf("shifted", [P, 32], F32)
+            got["row"] = sbuf("row", [P, 32], F32)
+            nc.vector.tensor_scalar_add(shifted[:], got["column"][:, 0:32], got["first"][:])
+            return shifted
+
+        def turn_rows(shifted):
+            nc.vector.transpose(got["row"][:], shifted[:])
+
+        def compare():
+            got["ident"] = sbuf("ident", [P, P], F32)
+            nc.vector.tensor_single_scalar(got["ident"][:], got["column"][:], got["row"][:, 0:1], ALU.is_equal)
+
+        def turn_both_vs(number):
+            got["vs_turned"] = bank(number, "vs_turned", [P, B, P + PACK])
+            for b in range(B):
+                for t in reversed(range(PACK)):
+                    nc.tensor.transpose(got["vs_turned"][:, b, t : t + P], got["vs_listed", b][:, t:N:PACK], got["ident"][:])
+
+        def copy_both_vs(copy):
+            slots = sbuf("vs_slots", [P, B, PACK], F32)
+            copy(slots[:], got["vs_turned"][:, :, VS_ROW : VS_ROW + PACK])
+            for b in range(B):
+                got["vs_slot", b] = slots[:, b : b + 1, :]
 
         def zero_scales(engine):
             engine.memset(scale_pool[:].bitcast(I32), 0)
@@ -119,7 +151,7 @@ def tile_attend_relu2_kernel(tc, qT, k_words, k_scales, vT, vs, offs, out):
         def turn_vs(b, number):
             got["vs_turned", b] = bank(number, "vs_turned%d" % b, [P, P + PACK])
             for t in reversed(range(PACK)):
-                nc.tensor.transpose(got["vs_turned", b][:, t : t + P], got["vs_listed", b][:, t:N:PACK], ident[:])
+                nc.tensor.transpose(got["vs_turned", b][:, t : t + P], got["vs_listed", b][:, t:N:PACK], got["ident"][:])
 
         def copy_vs(b, copy):
             got["vs_slot", b] = sbuf("vs_slot%d" % b, [P, 1, PACK], F32)
@@ -175,13 +207,13 @@ def tile_attend_relu2_kernel(tc, qT, k_words, k_scales, vT, vs, offs, out):
         def turn_squares(b, number):
             got["p_turned", b] = bank(number, "p_turned%d" % b, [P, PACK, NQ])
             for t in range(PACK):
-                nc.tensor.transpose(got["p_turned", b][:, t, :], got["p", b][:, t // 2, t % 2, 0:P], ident[:])
+                nc.tensor.transpose(got["p_turned", b][:, t, :], got["p", b][:, t // 2, t % 2, 0:P], got["ident"][:])
 
         def turn_values(half, b, number):
             got[half + "_turned", b] = bank(number, "%s_turned%d" % (half, b), [P, 2, P])
             for u in range(2):
                 nc.tensor.transpose(
-                    got[half + "_turned", b][:, u, :], got[half + "_listed", b][:].bitcast(F32)[:, u : N // 2 : 2], ident[:]
+                    got[half + "_turned", b][:, u, :], got[half + "_listed", b][:].bitcast(F32)[:, u : N // 2 : 2], got["ident"][:]
                 )
 
         def copy_values(half, b, copy):
@@ -199,7 +231,7 @@ def tile_attend_relu2_kernel(tc, qT, k_words, k_scales, vT, vs, offs, out):
             nc.vector.tensor_tensor(
                 got["w_bf", b][:].rearrange("p (c i) t -> p c t i", i=2),
                 got["p_turned", b][:].rearrange("p t (c i) -> p c t i", i=2),
-                got["vs_slot", b][:].unsqueeze(3).to_broadcast([P, NQ // 2, PACK, 2]),
+                got["vs_slot", b][:, :, :].unsqueeze(3).to_broadcast([P, NQ // 2, PACK, 2]),
                 ALU.mult,
             )
 
@@ -236,8 +268,14 @@ def tile_attend_relu2_kernel(tc, qT, k_words, k_scales, vT, vs, offs, out):
         vcopy = nc.vector.tensor_copy
         scopy = nc.scalar.copy
         zero_scales(nc.gpsimd)
-        zero_vs(nc.vector, 0, 3 * T // 4)
-        zero_vs(nc.gpsimd, 3 * T // 4, T)
+        count_columns()
+        zero_vs(nc.vector, 0, 512)
+        shifted = count_rows()
+        zero_vs(nc.vector, 512, 1024)
+        turn_rows(shifted)
+        zero_vs(nc.vector, 1024, 1536)
+        compare()
+        zero_vs(nc.gpsimd, 1536, T)
         nc.sync.dma_start(offsets[:], offs)
         load_vs(nc.scalar)
         load_queries(0)
@@ -246,16 +284,14 @@ def tile_attend_relu2_kernel(tc, qT, k_words, k_scales, vT, vs, offs, out):
         load_queries(1)
         load_values("low", 0, T)
         load_values("high", 0, T)
-        make_identity(nc, ident[:])
-
+        gather_vs(0, act_copy)
         weave_queries(0, act_copy)
         gather_scales(0)
-        gather_vs(0, act_copy)
         quantize_queries(0)
         gather_scales(1)
         gather_vs(1, act_copy)
-        spread_vs(0, nc.sync)
-        spread_vs(1, nc.sync)
+        turn_both_vs(7)
+        copy_both_vs(scopy)
         gather_keys(0)
         weave_queries(1, act_copy)
         gather_keys(1)
@@ -273,25 +309,25 @@ def tile_attend_relu2_kernel(tc, qT, k_words, k_scales, vT, vs, offs, out):
         turn_values("low", 0, 4)
         turn_values("low", 1, 5)
         turn_squares(1, 3)
+        weigh(0)
         gather_values("high", 1, 0, N, act_copy)
         gather_values("high", 0, 0, N, vcopy)
-        weigh(0)
         weigh(1)
         add_one(nc.vector)
         copy_values("low", 0, scopy)
         copy_values("low", 1, scopy)
-        turn_values("high", 0, 6)
         turn_values("high", 1, 7)
+        turn_values("high", 0, 6)
         quantize_weights(0)
         invert()
         quantize_weights(1)
-        copy_values("high", 0, scopy)
         copy_values("high", 1, scopy)
+        copy_values("high", 0, scopy)
         quantize_values("low", 0)
         quantize_values("low", 1)
-        quantize_values("high", 0)
         quantize_values("high", 1)
+        quantize_values("high", 0)
         finish(0, "low", 0, True, nc.sync)
         finish(1, "low", 1, True, nc.sync)
-        finish(0, "high", 2, True, nc.scalar)
-        finish(1, "high", 3, False, nc.sync)
+        finish(1, "high", 2, True, nc.scalar)
+        finish(0, "high", 3, False, nc.sync)

@@ -20,7 +20,8 @@ FP8X4 = mybir.dt.float8_e4m3fn_x4
 ACT = mybir.ActivationFunctionType
 ALU = mybir.AluOpType
 WIDTH = {F32: 4, BF16: 2, U32: 4, U8: 1}
-OVER = {"low_bf0":["v_high",0],"low_bf1":["v_high",1024],"w_bf1":["v_high",2048],"w0_codes":["v_high",3072],"inverse":["v_high",4096],"plus_one":["v_high",4160]}
+OVER = {"low_bf":["v_high",0],"w_bf1":["v_high",2048],"w0_codes":["v_high",3072],"inverse":["v_high",4096],"vs_slots":["q_raw1",1024],"k_scale1_1":["q_raw1",0]}
+ROOM = {}
 
 
 def tile_attend_relu2_kernel(tc, qT, k_words, k_scales, vT, vs, offs, out):
@@ -39,7 +40,7 @@ def tile_attend_relu2_kernel(tc, qT, k_words, k_scales, vT, vs, offs, out):
                 places[name] = places[OVER[name][0]] + OVER[name][1]
             else:
                 places[name] = places["end"]
-                places["end"] = places[name] + (size + 63) // 64 * 64
+                places["end"] = places[name] + (size + 63) // 64 * 64 + ROOM.get(name, 0)
             return work.tile(shape, dtype, name=name, align_bytes=64, offset=places[name])
 
         def bank(number, name, shape, dtype=F32):
@@ -143,6 +144,26 @@ def tile_attend_relu2_kernel(tc, qT, k_words, k_scales, vT, vs, offs, out):
                 got["k_scale", b] = sbuf("k_scale%d" % b, [P, N], U8)
             nc.vector.tensor_copy(got["k_scale", b][:, first:last], scale_pool[:].indirect(picks(b, first, last)))
 
+        def gather_scale_half(b, part):
+            got["k_scale", b, part] = sbuf("k_scale%d_%d" % (b, part), [P, N // 2], U8)
+            nc.vector.tensor_copy(
+                got["k_scale", b, part][:], scale_pool[:].indirect(picks(b, part * N // 2, (part + 1) * N // 2))
+            )
+
+        def score_halves(b, number):
+            got["scores", b] = bank(number, "scores%d" % b, [P, N])
+            for part in range(2):
+                cols = slice(part * N // 2, (part + 1) * N // 2)
+                nc.tensor.matmul_mx(
+                    out=got["scores", b][:, cols],
+                    lhsT=got["q", b][0][:].bitcast(FP8X4),
+                    lhsT_scale=got["q", b][1][:],
+                    rhs=got["k", b][:, cols].bitcast(FP8X4),
+                    rhs_scale=got["k_scale", b, part][:],
+                    start=True,
+                    stop=True,
+                )
+
         def gather_values(half, b, first, last, copy):
             if (half + "_listed", b) not in got:
                 got[half + "_listed", b] = sbuf("%s_listed%d" % (half, b), [P, N], BF16)
@@ -187,19 +208,22 @@ def tile_attend_relu2_kernel(tc, qT, k_words, k_scales, vT, vs, offs, out):
                 stop=True,
             )
 
+        def halves(b):
+            got["positive", b] = sbuf("positive%d" % b, [P, 2, P + 2, 2], F32)
+            nc.gpsimd.memset(got["positive", b][:, :, P : P + 1, :], 0.5)
+
         def relu(b):
-            got["positive", b] = sbuf("positive%d" % b, [P, 2, P, 2], F32)
             nc.scalar.activation(
-                got["positive", b][:].rearrange("p u s e -> p s u e"),
+                got["positive", b][:, :, 0:P, :].rearrange("p u s e -> p s u e"),
                 got["scores", b][:].rearrange("p (s u e) -> p s u e", u=2, e=2),
                 ACT.Relu,
             )
 
         def square(b):
-            got["p", b] = sbuf("square%d" % b, [P, 2, 2, P], F32)
+            got["p", b] = sbuf("square%d" % b, [P, 2, 2, P + 4], F32)
             nc.scalar.activation(
-                got["p", b][:],
-                got["positive", b][:].rearrange("p u s e -> p u e s"),
+                got["p", b][:, :, :, 0 : P + 1],
+                got["positive", b][:, :, 0 : P + 1, :].rearrange("p u s e -> p u e s"),
                 ACT.Square,
                 accum_out=total[:, b : b + 1],
             )
@@ -223,6 +247,19 @@ def tile_attend_relu2_kernel(tc, qT, k_words, k_scales, vT, vs, offs, out):
                 got[half + "_turned", b][:].rearrange("p u (c i) -> p c u i", i=2),
             )
 
+        def copy_low(b, copy):
+            if "low_bf" not in got:
+                got["low_bf"] = sbuf("low_bf", [P, B * N], BF16)
+            copy(
+                got["low_bf"][:, b * N : (b + 1) * N].bitcast(F32).rearrange("p (c i u) -> p c u i", i=2, u=2),
+                got["low_turned", b][:].rearrange("p u (c i) -> p c u i", i=2),
+            )
+
+        def quantize_low():
+            codes, scale = quantize("low", got["low_bf"][:], B * P)
+            for b in range(B):
+                got["low", b] = (codes[:, b * P : (b + 1) * P], scale[:, b * P : (b + 1) * P])
+
         def quantize_values(half, b):
             got[half, b] = quantize("%s%d" % (half, b), got[half + "_bf", b][:], P)
 
@@ -244,7 +281,7 @@ def tile_attend_relu2_kernel(tc, qT, k_words, k_scales, vT, vs, offs, out):
 
         def invert():
             got["inverse"] = sbuf("inverse", [P, B], F32)
-            nc.vector.reciprocal(got["inverse"][:], got["plus_one"][:])
+            nc.vector.reciprocal(got["inverse"][:], total[:])
 
         def finish(b, half, number, on_scalar, queue):
             sums = bank(number, "sums_%s%d" % (half, b), [P, P])
@@ -253,8 +290,8 @@ def tile_attend_relu2_kernel(tc, qT, k_words, k_scales, vT, vs, offs, out):
                 out=sums[:],
                 lhsT=got["w", b][0][:].bitcast(FP8X4),
                 lhsT_scale=got["w", b][1][:],
-                rhs=codes[:].bitcast(FP8X4),
-                rhs_scale=scale[:],
+                rhs=codes[:, :].bitcast(FP8X4),
+                rhs_scale=scale[:, :],
                 start=True,
                 stop=True,
             )
@@ -267,15 +304,17 @@ def tile_attend_relu2_kernel(tc, qT, k_words, k_scales, vT, vs, offs, out):
 
         vcopy = nc.vector.tensor_copy
         scopy = nc.scalar.copy
-        zero_scales(nc.gpsimd)
+        zero_scales(nc.vector)
         count_columns()
         zero_vs(nc.vector, 0, 512)
         shifted = count_rows()
-        zero_vs(nc.vector, 512, 1024)
+        zero_vs(nc.vector, 512, 768)
         turn_rows(shifted)
-        zero_vs(nc.vector, 1024, 1536)
+        zero_vs(nc.vector, 768, 1024)
         compare()
-        zero_vs(nc.gpsimd, 1536, T)
+        zero_vs(nc.gpsimd, 1024, T)
+        halves(0)
+        halves(1)
         nc.sync.dma_start(offsets[:], offs)
         load_vs(nc.scalar)
         load_queries(0)
@@ -288,23 +327,24 @@ def tile_attend_relu2_kernel(tc, qT, k_words, k_scales, vT, vs, offs, out):
         weave_queries(0, act_copy)
         gather_scales(0)
         quantize_queries(0)
-        gather_scales(1)
+        gather_scale_half(1, 0)
         gather_vs(1, act_copy)
         turn_both_vs(7)
-        copy_both_vs(scopy)
         gather_keys(0)
         weave_queries(1, act_copy)
+        copy_both_vs(scopy)
         gather_keys(1)
+        gather_scale_half(1, 1)
         quantize_queries(1)
         score(0, 0)
-        score(1, 1)
+        score_halves(1, 1)
         relu(0)
+        gather_values("low", 1, 256, N, act_copy)
         square(0)
         relu(1)
-        gather_values("low", 1, 384, N, act_copy)
         square(1)
         gather_values("low", 0, 0, N, vcopy)
-        gather_values("low", 1, 0, 384, vcopy)
+        gather_values("low", 1, 0, 256, vcopy)
         turn_squares(0, 2)
         turn_values("low", 0, 4)
         turn_values("low", 1, 5)
@@ -313,9 +353,8 @@ def tile_attend_relu2_kernel(tc, qT, k_words, k_scales, vT, vs, offs, out):
         gather_values("high", 1, 0, N, act_copy)
         gather_values("high", 0, 0, N, vcopy)
         weigh(1)
-        add_one(nc.vector)
-        copy_values("low", 0, scopy)
-        copy_values("low", 1, scopy)
+        copy_low(0, scopy)
+        copy_low(1, scopy)
         turn_values("high", 1, 7)
         turn_values("high", 0, 6)
         quantize_weights(0)
@@ -323,8 +362,7 @@ def tile_attend_relu2_kernel(tc, qT, k_words, k_scales, vT, vs, offs, out):
         quantize_weights(1)
         copy_values("high", 1, scopy)
         copy_values("high", 0, scopy)
-        quantize_values("low", 0)
-        quantize_values("low", 1)
+        quantize_low()
         quantize_values("high", 1)
         quantize_values("high", 0)
         finish(0, "low", 0, True, nc.sync)

@@ -20,8 +20,8 @@ FP8X4 = mybir.dt.float8_e4m3fn_x4
 ACT = mybir.ActivationFunctionType
 ALU = mybir.AluOpType
 WIDTH = {F32: 4, BF16: 2, U32: 4, U8: 1}
-OVER = {"low_bf":["v_high",0],"w_bf1":["v_high",2048],"w0_codes":["v_high",3072],"inverse":["v_high",4096],"vs_slots":["q_raw1",1024],"k_scale1_1":["q_raw1",0]}
-ROOM = {}
+OVER = {"vs_slots":["q_raw1",0],"unit":["q_raw1",1792],"high_bf0":["q_raw1",832],"low_bf":["q_raw1",1984],"w_bf":["total0",-1984],"high_bf1":["total0",192]}
+ROOM = {"q_raw1":2048,"total0":1024}
 
 
 def tile_attend_relu2_kernel(tc, qT, k_words, k_scales, vT, vs, offs, out):
@@ -65,7 +65,8 @@ def tile_attend_relu2_kernel(tc, qT, k_words, k_scales, vT, vs, offs, out):
         places["end"] = places["end"] + 1024
         q_raw.append(sbuf("q_raw1", [P, PACK, NQ], F32))
         word_pool = sbuf("word_pool", [P, T], U32)
-        total = sbuf("total", [P, B], F32)
+        places["end"] = places["end"] + 2048
+        total = [sbuf("total0", [P, 64], F32), sbuf("total1", [P, 1], F32)]
         got = {}
 
         def count_columns():
@@ -89,6 +90,19 @@ def tile_attend_relu2_kernel(tc, qT, k_words, k_scales, vT, vs, offs, out):
         def compare():
             got["ident"] = sbuf("ident", [P, P], F32)
             nc.vector.tensor_single_scalar(got["ident"][:], got["column"][:], got["row"][:, 0:1], ALU.is_equal)
+
+        def deal_vs(b):
+            got["vs_lanes", b] = sbuf("vs_lanes%d" % b, [P, PACK, P], F32)
+            act_copy(
+                got["vs_lanes", b][:].rearrange("p t s -> p s t"),
+                got["vs_listed", b][:].rearrange("p (s t) -> p s t", t=PACK),
+            )
+
+        def turn_lanes(number):
+            got["vs_turned"] = bank(number, "vs_turned", [P, B, P + PACK])
+            for b in range(B):
+                for t in reversed(range(PACK)):
+                    nc.tensor.transpose(got["vs_turned"][:, b, t : t + P], got["vs_lanes", b][:, t, :], got["ident"][:])
 
         def turn_both_vs(number):
             got["vs_turned"] = bank(number, "vs_turned", [P, B, P + PACK])
@@ -209,8 +223,7 @@ def tile_attend_relu2_kernel(tc, qT, k_words, k_scales, vT, vs, offs, out):
             )
 
         def halves(b):
-            got["positive", b] = sbuf("positive%d" % b, [P, 2, P + 2, 2], F32)
-            nc.gpsimd.memset(got["positive", b][:, :, P : P + 1, :], 0.5)
+            got["positive", b] = sbuf("positive%d" % b, [P, 2, P, 2], F32)
 
         def relu(b):
             nc.scalar.activation(
@@ -220,12 +233,12 @@ def tile_attend_relu2_kernel(tc, qT, k_words, k_scales, vT, vs, offs, out):
             )
 
         def square(b):
-            got["p", b] = sbuf("square%d" % b, [P, 2, 2, P + 4], F32)
+            got["p", b] = sbuf("square%d" % b, [P, 2, 2, P], F32)
             nc.scalar.activation(
-                got["p", b][:, :, :, 0 : P + 1],
-                got["positive", b][:, :, 0 : P + 1, :].rearrange("p u s e -> p u e s"),
+                got["p", b][:, :, :, 0:P],
+                got["positive", b][:, :, 0:P, :].rearrange("p u s e -> p u e s"),
                 ACT.Square,
-                accum_out=total[:, b : b + 1],
+                accum_out=total[b][:, 0:1],
             )
 
         def turn_squares(b, number):
@@ -264,24 +277,31 @@ def tile_attend_relu2_kernel(tc, qT, k_words, k_scales, vT, vs, offs, out):
             got[half, b] = quantize("%s%d" % (half, b), got[half + "_bf", b][:], P)
 
         def weigh(b):
-            got["w_bf", b] = sbuf("w_bf%d" % b, [P, NQ, PACK], BF16)
+            if "w_bf" not in got:
+                got["w_bf"] = sbuf("w_bf", [P, B * N], BF16)
+            got["w_bf", b] = got["w_bf"][:, b * N : (b + 1) * N]
             nc.vector.tensor_tensor(
-                got["w_bf", b][:].rearrange("p (c i) t -> p c t i", i=2),
+                got["w_bf", b].rearrange("p (c i t) -> p c t i", i=2, t=PACK),
                 got["p_turned", b][:].rearrange("p t (c i) -> p c t i", i=2),
                 got["vs_slot", b][:, :, :].unsqueeze(3).to_broadcast([P, NQ // 2, PACK, 2]),
                 ALU.mult,
             )
 
         def quantize_weights(b):
-            got["w", b] = quantize("w%d" % b, got["w_bf", b][:].rearrange("p q t -> p (q t)"), NQ)
+            got["w", b] = quantize("w%d" % b, got["w_bf", b], NQ)
 
-        def add_one(engine):
-            got["plus_one"] = sbuf("plus_one", [P, B], F32)
-            engine.tensor_scalar_add(got["plus_one"][:], total[:], 1.0)
+        def add_one(b):
+            if b == 0:
+                got["plus_one"] = sbuf("plus_one", [P, B], F32)
+            nc.gpsimd.tensor_tensor(got["plus_one"][:, b : b + 1], total[b][:, 0:1], got["unit"][:, 0:1], ALU.add)
+
+        def set_unit():
+            got["unit"] = sbuf("unit", [P, 64], F32)
+            nc.gpsimd.memset(got["unit"][:, 0:1], 1.0)
 
         def invert():
             got["inverse"] = sbuf("inverse", [P, B], F32)
-            nc.vector.reciprocal(got["inverse"][:], total[:])
+            nc.vector.reciprocal(got["inverse"][:], got["plus_one"][:])
 
         def finish(b, half, number, on_scalar, queue):
             sums = bank(number, "sums_%s%d" % (half, b), [P, P])
@@ -327,45 +347,47 @@ def tile_attend_relu2_kernel(tc, qT, k_words, k_scales, vT, vs, offs, out):
         weave_queries(0, act_copy)
         gather_scales(0)
         quantize_queries(0)
-        gather_scale_half(1, 0)
+        gather_scales(1)
         gather_vs(1, act_copy)
         turn_both_vs(7)
         gather_keys(0)
         weave_queries(1, act_copy)
         copy_both_vs(scopy)
+        set_unit()
         gather_keys(1)
-        gather_scale_half(1, 1)
         quantize_queries(1)
         score(0, 0)
-        score_halves(1, 1)
+        score(1, 1)
         relu(0)
         gather_values("low", 1, 256, N, act_copy)
         square(0)
+        add_one(0)
         relu(1)
         square(1)
+        add_one(1)
         gather_values("low", 0, 0, N, vcopy)
         gather_values("low", 1, 0, 256, vcopy)
         turn_squares(0, 2)
         turn_values("low", 0, 4)
         turn_values("low", 1, 5)
         turn_squares(1, 3)
-        weigh(0)
         gather_values("high", 1, 0, N, act_copy)
         gather_values("high", 0, 0, N, vcopy)
+        weigh(0)
         weigh(1)
         copy_low(0, scopy)
         copy_low(1, scopy)
-        turn_values("high", 1, 7)
         turn_values("high", 0, 6)
+        turn_values("high", 1, 7)
         quantize_weights(0)
         invert()
-        quantize_weights(1)
-        copy_values("high", 1, scopy)
-        copy_values("high", 0, scopy)
         quantize_low()
-        quantize_values("high", 1)
+        quantize_weights(1)
+        copy_values("high", 0, scopy)
+        copy_values("high", 1, scopy)
         quantize_values("high", 0)
+        quantize_values("high", 1)
         finish(0, "low", 0, True, nc.sync)
         finish(1, "low", 1, True, nc.sync)
-        finish(1, "high", 2, True, nc.scalar)
-        finish(0, "high", 3, False, nc.sync)
+        finish(0, "high", 2, True, nc.scalar)
+        finish(1, "high", 3, False, nc.sync)

from contextlib import ExitStack

import concourse.mybir as mybir

B, N, T, D, DV, NQ = 2, 512, 2048, 512, 256, 128
FLOPS = 2 * B * NQ * N * (D + DV)

P = 128
PACK = 4
VS_ROW = P - 1
ARENA = 16384

F32 = mybir.dt.float32
BF16 = mybir.dt.bfloat16
I32 = mybir.dt.int32
U32 = mybir.dt.uint32
U16 = mybir.dt.uint16
U8 = mybir.dt.uint8
FP8X4 = mybir.dt.float8_e4m3fn_x4
ACT = mybir.ActivationFunctionType
ALU = mybir.AluOpType
WIDTH = {F32: 4, BF16: 2, U32: 4, U8: 1}
OVER = {"vs_slots":["q_raw1",0],"unit":["q_raw1",1792],"high_bf0":["q_raw1",832],"low_bf":["q_raw1",1984],"w_bf":["total0",-1984],"high_bf1":["total0",192]}
ROOM = {"q_raw1":2048,"total0":1024}


def tile_attend_relu2_kernel(tc, qT, k_words, k_scales, vT, vs, offs, out):
    nc = tc.nc
    with ExitStack() as ctx:
        held = ctx.enter_context(tc.tile_pool(name="held", bufs=1))
        work = ctx.enter_context(tc.tile_pool(name="work", bufs=1))
        psum = ctx.enter_context(tc.psum_pool(name="psum", bufs=1))
        places = {"end": 0}

        def sbuf(name, shape, dtype):
            size = WIDTH[dtype]
            for extent in shape[1:]:
                size = size * extent
            if name in OVER:
                places[name] = places[OVER[name][0]] + OVER[name][1]
            else:
                places[name] = places["end"]
                places["end"] = places[name] + (size + 63) // 64 * 64 + ROOM.get(name, 0)
            return work.tile(shape, dtype, name=name, align_bytes=64, offset=places[name])

        def bank(number, name, shape, dtype=F32):
            return psum.tile(shape, dtype, name=name, tag="bank%d" % number)

        def quantize(name, values, words):
            codes = sbuf(name + "_codes", [P, words], U32)
            scale = sbuf(name + "_scale", [P, words], U8)
            nc.vector.quantize_mx(out=codes[:].bitcast(FP8X4), scales=scale[:], in_=values)
            return codes, scale

        offsets = held.tile([P, B * N // 16], U16, name="offsets")

        def picks(b, first, last):
            return offsets[:, (b * N + first) // 16 : (b * N + last) // 16]

        scale_pool = sbuf("scale_pool", [P, T], U8)
        vs_pool = sbuf("vs_pool", [P, T], F32)
        pool = {"low": sbuf("v_low", [P, T], F32), "high": sbuf("v_high", [P, T], F32)}
        rows = {"low": slice(0, P), "high": slice(P, DV)}
        q_raw = [sbuf("q_raw0", [P, PACK, NQ], F32)]
        places["end"] = places["end"] + 1024
        q_raw.append(sbuf("q_raw1", [P, PACK, NQ], F32))
        word_pool = sbuf("word_pool", [P, T], U32)
        places["end"] = places["end"] + 2048
        total = [sbuf("total0", [P, 64], F32), sbuf("total1", [P, 1], F32)]
        got = {}

        def count_columns():
            got["ones"] = sbuf("ones", [P, P], F32)
            got["first"] = sbuf("first", [P, 1], F32)
            got["column"] = sbuf("column", [P, P], F32)
            nc.vector.memset(got["ones"][:], 1.0)
            for quad in range(4):
                nc.gpsimd.memset(got["first"][32 * quad : 32 * quad + 32, :], 32.0 * quad)
            nc.vector.tensor_tensor_scan(got["column"][:], got["ones"][:], got["ones"][:], -1.0, ALU.mult, ALU.add)

        def count_rows():
            shifted = sbuf("shifted", [P, 32], F32)
            got["row"] = sbuf("row", [P, 32], F32)
            nc.vector.tensor_scalar_add(shifted[:], got["column"][:, 0:32], got["first"][:])
            return shifted

        def turn_rows(shifted):
            nc.vector.transpose(got["row"][:], shifted[:])

        def compare():
            got["ident"] = sbuf("ident", [P, P], F32)
            nc.vector.tensor_single_scalar(got["ident"][:], got["column"][:], got["row"][:, 0:1], ALU.is_equal)

        def deal_vs(b):
            got["vs_lanes", b] = sbuf("vs_lanes%d" % b, [P, PACK, P], F32)
            act_copy(
                got["vs_lanes", b][:].rearrange("p t s -> p s t"),
                got["vs_listed", b][:].rearrange("p (s t) -> p s t", t=PACK),
            )

        def turn_lanes(number):
            got["vs_turned"] = bank(number, "vs_turned", [P, B, P + PACK])
            for b in range(B):
                for t in reversed(range(PACK)):
                    nc.tensor.transpose(got["vs_turned"][:, b, t : t + P], got["vs_lanes", b][:, t, :], got["ident"][:])

        def turn_both_vs(number):
            got["vs_turned"] = bank(number, "vs_turned", [P, B, P + PACK])
            for b in range(B):
                for t in reversed(range(PACK)):
                    nc.tensor.transpose(got["vs_turned"][:, b, t : t + P], got["vs_listed", b][:, t:N:PACK], got["ident"][:])

        def copy_both_vs(copy):
            slots = sbuf("vs_slots", [P, B, PACK], F32)
            copy(slots[:], got["vs_turned"][:, :, VS_ROW : VS_ROW + PACK])
            for b in range(B):
                got["vs_slot", b] = slots[:, b : b + 1, :]

        def zero_scales(engine):
            engine.memset(scale_pool[:].bitcast(I32), 0)

        def zero_vs(engine, first, last):
            engine.memset(vs_pool[0:VS_ROW, first:last], 0.0)

        def load_vs(queue):
            queue.dma_start(vs_pool[VS_ROW:P, :], vs[0:1, :])

        def load_scales(queue):
            for quad in range(4):
                queue.dma_start(
                    scale_pool[32 * quad : 32 * quad + 4, :].bitcast(I32),
                    k_scales[0, 4 * quad : 4 * quad + 4, :].bitcast(I32),
                )

        def load_queries(b, queue=nc.sync):
            queue.dma_start(q_raw[b][:], qT[b].rearrange("(p j) n -> p j n", j=PACK))

        def load_words(first, last):
            words = k_words[0].rearrange("p t r -> p (t r)").bitcast(I32)
            nc.sync.dma_start(word_pool[:, first:last].bitcast(I32), words[:, first:last])

        def load_values(half, first, last):
            nc.sync.dma_start(pool[half][:, first:last], vT[rows[half], first:last])

        def probe(name, source, dtype=F32):
            mark = sbuf("probe_" + name, [P, 1], dtype)
            nc.gpsimd.tensor_copy(mark[:], source)

        def act_copy(to, source):
            nc.scalar.activation(to, source, ACT.Copy)

        def gather_vs(b, copy):
            got["vs_listed", b] = sbuf("vs_listed%d" % b, [P, N], F32)
            copy(got["vs_listed", b][:], vs_pool[:].indirect(picks(b, 0, N)))

        def gather_scales(b, first=0, last=N):
            if ("k_scale", b) not in got:
                got["k_scale", b] = sbuf("k_scale%d" % b, [P, N], U8)
            nc.vector.tensor_copy(got["k_scale", b][:, first:last], scale_pool[:].indirect(picks(b, first, last)))

        def gather_scale_half(b, part):
            got["k_scale", b, part] = sbuf("k_scale%d_%d" % (b, part), [P, N // 2], U8)
            nc.vector.tensor_copy(
                got["k_scale", b, part][:], scale_pool[:].indirect(picks(b, part * N // 2, (part + 1) * N // 2))
            )

        def score_halves(b, number):
            got["scores", b] = bank(number, "scores%d" % b, [P, N])
            for part in range(2):
                cols = slice(part * N // 2, (part + 1) * N // 2)
                nc.tensor.matmul_mx(
                    out=got["scores", b][:, cols],
                    lhsT=got["q", b][0][:].bitcast(FP8X4),
                    lhsT_scale=got["q", b][1][:],
                    rhs=got["k", b][:, cols].bitcast(FP8X4),
                    rhs_scale=got["k_scale", b, part][:],
                    start=True,
                    stop=True,
                )

        def gather_values(half, b, first, last, copy):
            if (half + "_listed", b) not in got:
                got[half + "_listed", b] = sbuf("%s_listed%d" % (half, b), [P, N], BF16)
            copy(got[half + "_listed", b][:, first:last], pool[half][:].indirect(picks(b, first, last)))

        def turn_vs(b, number):
            got["vs_turned", b] = bank(number, "vs_turned%d" % b, [P, P + PACK])
            for t in reversed(range(PACK)):
                nc.tensor.transpose(got["vs_turned", b][:, t : t + P], got["vs_listed", b][:, t:N:PACK], got["ident"][:])

        def copy_vs(b, copy):
            got["vs_slot", b] = sbuf("vs_slot%d" % b, [P, 1, PACK], F32)
            copy(got["vs_slot", b][:, 0, :], got["vs_turned", b][:, VS_ROW : VS_ROW + PACK])

        def spread_vs(b, queue):
            got["vs_slot", b] = sbuf("vs_slot%d" % b, [P, 1, PACK], F32)
            queue.dma_start(got["vs_slot", b][:, 0, :], got["vs_listed", b][VS_ROW:P, :])

        def gather_keys(b):
            got["k", b] = sbuf("k_listed%d" % b, [P, N], U32)
            nc.vector.tensor_copy(got["k", b][:], word_pool[:].indirect(picks(b, 0, N)))

        def weave_queries(b, copy):
            got["q_bf", b] = sbuf("q_bf%d" % b, [P, NQ * PACK], BF16)
            copy(
                got["q_bf", b][:].rearrange("p (c i j) -> p c j i", i=4, j=PACK),
                q_raw[b][:].rearrange("p j (c i) -> p c j i", i=4),
            )

        def quantize_queries(b):
            got["q", b] = quantize("q%d" % b, got["q_bf", b][:], NQ)

        def score(b, number):
            got["scores", b] = bank(number, "scores%d" % b, [P, N])
            nc.tensor.matmul_mx(
                out=got["scores", b][:],
                lhsT=got["q", b][0][:].bitcast(FP8X4),
                lhsT_scale=got["q", b][1][:],
                rhs=got["k", b][:].bitcast(FP8X4),
                rhs_scale=got["k_scale", b][:],
                start=True,
                stop=True,
            )

        def halves(b):
            got["positive", b] = sbuf("positive%d" % b, [P, 2, P, 2], F32)

        def relu(b):
            nc.scalar.activation(
                got["positive", b][:, :, 0:P, :].rearrange("p u s e -> p s u e"),
                got["scores", b][:].rearrange("p (s u e) -> p s u e", u=2, e=2),
                ACT.Relu,
            )

        def square(b):
            got["p", b] = sbuf("square%d" % b, [P, 2, 2, P], F32)
            nc.scalar.activation(
                got["p", b][:, :, :, 0:P],
                got["positive", b][:, :, 0:P, :].rearrange("p u s e -> p u e s"),
                ACT.Square,
                accum_out=total[b][:, 0:1],
            )

        def turn_squares(b, number):
            got["p_turned", b] = bank(number, "p_turned%d" % b, [P, PACK, NQ])
            for t in range(PACK):
                nc.tensor.transpose(got["p_turned", b][:, t, :], got["p", b][:, t // 2, t % 2, 0:P], got["ident"][:])

        def turn_values(half, b, number):
            got[half + "_turned", b] = bank(number, "%s_turned%d" % (half, b), [P, 2, P])
            for u in range(2):
                nc.tensor.transpose(
                    got[half + "_turned", b][:, u, :], got[half + "_listed", b][:].bitcast(F32)[:, u : N // 2 : 2], got["ident"][:]
                )

        def copy_values(half, b, copy):
            got[half + "_bf", b] = sbuf("%s_bf%d" % (half, b), [P, N], BF16)
            copy(
                got[half + "_bf", b][:].bitcast(F32).rearrange("p (c i u) -> p c u i", i=2, u=2),
                got[half + "_turned", b][:].rearrange("p u (c i) -> p c u i", i=2),
            )

        def copy_low(b, copy):
            if "low_bf" not in got:
                got["low_bf"] = sbuf("low_bf", [P, B * N], BF16)
            copy(
                got["low_bf"][:, b * N : (b + 1) * N].bitcast(F32).rearrange("p (c i u) -> p c u i", i=2, u=2),
                got["low_turned", b][:].rearrange("p u (c i) -> p c u i", i=2),
            )

        def quantize_low():
            codes, scale = quantize("low", got["low_bf"][:], B * P)
            for b in range(B):
                got["low", b] = (codes[:, b * P : (b + 1) * P], scale[:, b * P : (b + 1) * P])

        def quantize_values(half, b):
            got[half, b] = quantize("%s%d" % (half, b), got[half + "_bf", b][:], P)

        def weigh(b):
            if "w_bf" not in got:
                got["w_bf"] = sbuf("w_bf", [P, B * N], BF16)
            got["w_bf", b] = got["w_bf"][:, b * N : (b + 1) * N]
            nc.vector.tensor_tensor(
                got["w_bf", b].rearrange("p (c i t) -> p c t i", i=2, t=PACK),
                got["p_turned", b][:].rearrange("p t (c i) -> p c t i", i=2),
                got["vs_slot", b][:, :, :].unsqueeze(3).to_broadcast([P, NQ // 2, PACK, 2]),
                ALU.mult,
            )

        def quantize_weights(b):
            got["w", b] = quantize("w%d" % b, got["w_bf", b], NQ)

        def add_one(b):
            if b == 0:
                got["plus_one"] = sbuf("plus_one", [P, B], F32)
            nc.gpsimd.tensor_tensor(got["plus_one"][:, b : b + 1], total[b][:, 0:1], got["unit"][:, 0:1], ALU.add)

        def set_unit():
            got["unit"] = sbuf("unit", [P, 64], F32)
            nc.gpsimd.memset(got["unit"][:, 0:1], 1.0)

        def invert():
            got["inverse"] = sbuf("inverse", [P, B], F32)
            nc.vector.reciprocal(got["inverse"][:], got["plus_one"][:])

        def finish(b, half, number, on_scalar, queue):
            sums = bank(number, "sums_%s%d" % (half, b), [P, P])
            codes, scale = got[half, b]
            nc.tensor.matmul_mx(
                out=sums[:],
                lhsT=got["w", b][0][:].bitcast(FP8X4),
                lhsT_scale=got["w", b][1][:],
                rhs=codes[:, :].bitcast(FP8X4),
                rhs_scale=scale[:, :],
                start=True,
                stop=True,
            )
            result = sbuf("result_%s%d" % (half, b), [P, P], F32)
            if on_scalar:
                nc.scalar.activation(result[:], sums[:], ACT.Copy, scale=got["inverse"][:, b : b + 1])
            else:
                nc.vector.tensor_scalar_mul(result[:], sums[:], got["inverse"][:, b : b + 1])
            queue.dma_start(out[b, :, rows[half]], result[:])

        vcopy = nc.vector.tensor_copy
        scopy = nc.scalar.copy
        zero_scales(nc.vector)
        count_columns()
        zero_vs(nc.vector, 0, 512)
        shifted = count_rows()
        zero_vs(nc.vector, 512, 768)
        turn_rows(shifted)
        zero_vs(nc.vector, 768, 1024)
        compare()
        zero_vs(nc.gpsimd, 1024, T)
        halves(0)
        halves(1)
        nc.sync.dma_start(offsets[:], offs)
        load_vs(nc.scalar)
        load_queries(0)
        load_scales(nc.sync)
        load_words(0, T)
        load_queries(1)
        load_values("low", 0, T)
        load_values("high", 0, T)
        gather_vs(0, act_copy)
        weave_queries(0, act_copy)
        gather_scales(0)
        quantize_queries(0)
        gather_scales(1)
        gather_vs(1, act_copy)
        turn_both_vs(7)
        gather_keys(0)
        weave_queries(1, act_copy)
        copy_both_vs(scopy)
        set_unit()
        gather_keys(1)
        quantize_queries(1)
        score(0, 0)
        score(1, 1)
        relu(0)
        gather_values("low", 1, 256, N, act_copy)
        square(0)
        add_one(0)
        relu(1)
        square(1)
        add_one(1)
        gather_values("low", 0, 0, N, vcopy)
        gather_values("low", 1, 0, 256, vcopy)
        turn_squares(0, 2)
        turn_values("low", 0, 4)
        turn_values("low", 1, 5)
        turn_squares(1, 3)
        gather_values("high", 1, 0, N, act_copy)
        gather_values("high", 0, 0, N, vcopy)
        weigh(0)
        weigh(1)
        copy_low(0, scopy)
        copy_low(1, scopy)
        turn_values("high", 0, 6)
        turn_values("high", 1, 7)
        quantize_weights(0)
        invert()
        quantize_low()
        quantize_weights(1)
        copy_values("high", 0, scopy)
        copy_values("high", 1, scopy)
        quantize_values("high", 0)
        quantize_values("high", 1)
        finish(0, "low", 0, True, nc.sync)
        finish(1, "low", 1, True, nc.sync)
        finish(0, "high", 2, True, nc.scalar)
        finish(1, "high", 3, False, nc.sync)
